import numpy as np
import ml_dtypes


def mxq(x, axis, fmt="e4m3"):
    dtype, down = {"e4m3": (ml_dtypes.float8_e4m3fn, 7), "e5m2": (ml_dtypes.float8_e5m2, 14)}[fmt]
    v = np.moveaxis(np.asarray(x, np.float32).astype(ml_dtypes.bfloat16).astype(np.float64), axis, -1)
    blocks = v.reshape(v.shape[:-1] + (-1, 32))
    amax = np.abs(blocks).max(-1, keepdims=True)
    byte = np.maximum(np.where(amax > 0, np.frexp(amax)[1] - 1 + 127, 0) - down, 1)
    scale = np.exp2(byte - 127.0)
    codes = (blocks / scale).astype(np.float32).astype(dtype).astype(np.float64)
    return np.moveaxis((codes * scale).reshape(v.shape), -1, axis)


WIDE = False


def mx_kscale(k):
    if not WIDE:
        return np.ones(k)
    levels = np.array([10, -10, 5, -5, 0])
    if k % 512:
        return np.exp2(np.random.permutation(np.resize(levels, k // 32))).repeat(32)
    a = np.empty((k // 512, 16))
    for p in range(k // 512):
        a[p, :8] = np.random.permutation(np.resize(levels, 8))
        for g in range(8):
            far = levels[np.abs(levels - a[p, g]) >= 10]
            a[p, g + 8] = far[np.random.randint(len(far))]
    return np.exp2(a.ravel()).repeat(32)


def f64(x):
    return np.asarray(x).astype(np.float64)


def striped(idx):
    return np.tile(idx.reshape(-1, 16).T, (8, 1)).astype(np.uint16)


def unstriped(offs):
    return offs[:16].T.reshape(-1).astype(np.int64)


E2M1 = np.array([0.0, 0.5, 1.0, 1.5, 2.0, 3.0, 4.0, 6.0, -0.0, -0.5, -1.0, -1.5, -2.0, -3.0, -4.0, -6.0])


def pack_weight(w, fmt):
    k, n = w.shape
    w = f64(np.asarray(w, np.float32).astype(ml_dtypes.bfloat16)).reshape(k // 32, 32, n)
    amax = np.abs(w).max(1)
    if fmt == "e4m3":
        byte = np.frexp(amax)[1] - 1 + 127 - 7
    else:
        mant, ex = np.frexp(amax / 6.0)
        byte = np.where(mant > 0.5, ex, ex - 1) + 127
    byte = np.clip(np.where(amax > 0, byte, 1), 1, 254)
    scaled = (w * np.exp2(127.0 - byte)[:, None, :]).reshape(k, n).astype(np.float32)
    by_word = np.ascontiguousarray(scaled.reshape(k // 512, 128, 4, n).transpose(0, 1, 3, 2))
    if fmt == "e4m3":
        words = by_word.astype(ml_dtypes.float8_e4m3fn).view(np.uint8)
    else:
        c = by_word.astype(ml_dtypes.float4_e2m1fn).view(np.uint8) & 0xF
        words = (c[..., 0::2] | (c[..., 1::2] << 4)).reshape(k // 512, 128, 2 * n)
    return np.ascontiguousarray(words), np.ascontiguousarray(byte.astype(np.uint8).reshape(k // 512, 16, n))


def unpack_weight(words, scales, fmt):
    g, _, n = scales.shape
    words = np.ascontiguousarray(words).reshape(g, 128, n, -1)
    if fmt == "e4m3":
        vals = words.view(ml_dtypes.float8_e4m3fn).astype(np.float64)
    else:
        nib = np.empty((g, 128, n, 4), np.uint8)
        nib[..., 0::2] = words & 0xF
        nib[..., 1::2] = words >> 4
        vals = E2M1[nib]
    vals = vals * np.repeat(np.exp2(scales.astype(np.float64) - 127.0), 8, axis=1)[..., None]
    return vals.transpose(0, 1, 3, 2).reshape(g * 512, n)


def gelu(v):
    return 0.5 * v * (1.0 + np.tanh(np.sqrt(2.0 / np.pi) * (v + 0.044715 * v**3)))


K, T, S, T2, S2, N = 1024, 4096, 1536, 2048, 512, 512

def setup_inputs():
    n = np.random.standard_normal
    s = mx_kscale(K)[:, None]
    u = mx_kscale(S)[:, None]
    tab_words, tab_scales = pack_weight(n((K, T)) * s, "e4m3")
    tab2_words, tab2_scales = pack_weight(n((K, T2)) / np.sqrt(K) / s, "e4m3")
    wc_words, wc_scales = pack_weight(n((S, N)) / np.sqrt(S) / u, "e2m1")
    return {
        "tab_words": tab_words, "tab_scales": tab_scales,
        "offs": striped(np.random.permutation(T)[:S]),
        "tab2_words": tab2_words, "tab2_scales": tab2_scales,
        "offs2": striped(np.random.permutation(T2)[:S2]),
        "dens": (np.exp(0.3 * n(S)) * u[:, 0]).astype(np.float32),
        "wf": (n((S, N)) / np.sqrt(S) / u).astype(np.float32),
        "wc_words": wc_words, "wc_scales": wc_scales,
    }

def reference(tab_words, tab_scales, offs, tab2_words, tab2_scales, offs2, dens, wf, wc_words, wc_scales):
    v = unpack_weight(tab_words, tab_scales, "e4m3")[:, unstriped(offs)]
    v2 = unpack_weight(tab2_words, tab2_scales, "e4m3")[:, unstriped(offs2)]
    x = v.T @ v2
    h = f64(dens)[:, None] * (1.0 / (1.0 + x * x))
    hq = mxq(h, 0, "e4m3")
    wfq = mxq(f64(wf), 0, "e4m3")
    wc = unpack_weight(wc_words, wc_scales, "e2m1")
    f = wfq.T @ hq
    c = wc.T @ hq
    return np.maximum(f, c)

@@ -1,0 +1,213 @@
+from contextlib import ExitStack
+
+import concourse.mybir as mybir
+
+K, T, S, T2, S2, N = 1024, 4096, 1536, 2048, 512, 512
+FLOPS = 2 * K * S * S2 + 2 * 2 * S * N * S2
+
+F32 = mybir.dt.float32
+BF16 = mybir.dt.bfloat16
+I32 = mybir.dt.int32
+U32 = mybir.dt.uint32
+U16 = mybir.dt.uint16
+U8 = mybir.dt.uint8
+FP8X4 = mybir.dt.float8_e4m3fn_x4
+FP4X4 = mybir.dt.float4_e2m1fn_x4
+ACT = mybir.ActivationFunctionType
+ALU = mybir.AluOpType
+
+P = 128
+PACK = 4
+PASS = P * PACK
+K_PASSES = K // PASS
+I_PASSES = S // PASS
+N_TILES = N // P
+QUADS = 4
+ROWS = 4
+LIST_COLS = PASS // 16
+SCALAR_CAST = [0, 256, 512]
+
+
+def tile_list_cauchy_voxel_pooling_kernel(
+    tc, tab_words, tab_scales, offs, tab2_words, tab2_scales, offs2, dens, wf, wc_words, wc_scales, out
+):
+    nc = tc.nc
+    with ExitStack() as ctx:
+        keep = ctx.enter_context(tc.tile_pool(name="keep", bufs=1))
+        work = ctx.enter_context(tc.tile_pool(name="work", bufs=2))
+        psum = ctx.enter_context(tc.psum_pool(name="psum", bufs=1))
+
+        idx = keep.tile([P, S // 16], U16, name="idx")
+        idx2 = keep.tile([P, S2 // 16], U16, name="idx2")
+        v_win = [keep.tile([P, T], U32, name=f"v_win{a}") for a in range(K_PASSES)]
+        v2_win = [keep.tile([P, T2], U32, name=f"v2_win{a}") for a in range(K_PASSES)]
+        vs_win = keep.tile([P, T], U8, name="vs_win")
+        v2s_win = keep.tile([P, T2], U8, name="v2s_win")
+        wc_codes = keep.tile([P, I_PASSES, 2 * N], U8, name="wc_codes", align_bytes=64)
+        wc_sc = keep.tile([P, I_PASSES, N], U8, name="wc_sc", align_bytes=64)
+        d_sb = keep.tile([P, I_PASSES, PACK], F32, name="d_sb")
+        wf_raw = [keep.tile([P, PACK, N], F32, name=f"wf_raw{g}") for g in range(I_PASSES)]
+
+        nc.vector.memset(v2s_win[:].bitcast(I32), 0)
+        nc.vector.memset(vs_win[:].bitcast(I32), 0)
+        nc.vector.memset(wc_sc[:].rearrange("p g n -> p (g n)").bitcast(I32), 0)
+
+        warm_in = keep.tile([P, 1], F32, name="warm_in")
+        warm_out = keep.tile([P, 1], F32, name="warm_out")
+        nc.vector.memset(warm_in[:], 1.0)
+        nc.scalar.activation(warm_out[:], warm_in[:], ACT.Abs_reciprocal_sqrt)
+
+        nc.sync.dma_start(idx2[:], offs2)
+        nc.sync.dma_start(idx[:], offs)
+        for win, words in ((v2_win, tab2_words), (v_win, tab_words)):
+            for a in range(K_PASSES):
+                nc.sync.dma_start(win[a][:].bitcast(I32), words[a].rearrange("p t i -> p (t i)").bitcast(I32))
+        for win, scales in ((v2s_win, tab2_scales), (vs_win, tab_scales)):
+            for q in range(QUADS):
+                nc.gpsimd.dma_start(
+                    win[32 * q : 32 * q + ROWS * K_PASSES, :].bitcast(I32),
+                    scales[:, ROWS * q : ROWS * (q + 1), :].bitcast(I32),
+                )
+        for q in range(QUADS):
+            nc.gpsimd.dma_start(
+                wc_sc[32 * q : 32 * q + ROWS, :, :].bitcast(I32),
+                wc_scales[:, ROWS * q : ROWS * (q + 1), :].rearrange("g r n -> r g n").bitcast(I32),
+            )
+        nc.sync.dma_start(d_sb[:], dens.rearrange("(g p t) -> p g t", p=P, t=PACK))
+        nc.sync.dma_start(wf_raw[0][:], wf[0:PASS, :].rearrange("(p t) n -> p t n", t=PACK))
+        nc.sync.dma_start(wc_codes[:].bitcast(I32), wc_words.rearrange("g p b -> p g b").bitcast(I32))
+        for g in range(1, I_PASSES):
+            nc.sync.dma_start(wf_raw[g][:], wf[g * PASS : (g + 1) * PASS, :].rearrange("(p t) n -> p t n", t=PACK))
+
+        v2_codes = [keep.tile([P, S2], U32, name=f"v2_codes{a}", align_bytes=64) for a in range(K_PASSES)]
+        v2_sc = keep.tile([P, S2], U8, name="v2_sc", align_bytes=64)
+        v_codes = [
+            [keep.tile([P, PACK, P], U32, name=f"v_codes{a}_{g}", align_bytes=64) for g in range(I_PASSES)]
+            for a in range(K_PASSES)
+        ]
+        v_sc_list = [keep.tile([P, PASS], U8, name=f"v_sc_list{g}", align_bytes=64) for g in range(I_PASSES)]
+        v_sc = [keep.tile([P, PACK, P], U8, name=f"v_sc{g}", align_bytes=64) for g in range(I_PASSES)]
+
+        def entries(g):
+            return idx[:, g * LIST_COLS : (g + 1) * LIST_COLS]
+
+        def gather_v_words(a, g):
+            nc.vector.tensor_copy(v_codes[a][g][:].rearrange("p t m -> p m t"), v_win[a][:].indirect(entries(g)))
+
+        nc.vector.tensor_copy(v2_codes[0][:], v2_win[0][:].indirect(idx2[:]))
+        nc.vector.tensor_copy(v2_sc[:], v2s_win[:].indirect(idx2[:]))
+        nc.vector.tensor_copy(v2_codes[1][:], v2_win[1][:].indirect(idx2[:]))
+        for g in range(I_PASSES):
+            nc.vector.tensor_copy(v_sc_list[g][:], vs_win[:].indirect(entries(g)))
+        for g in range(I_PASSES):
+            nc.vector.tensor_copy(v_sc[g][:], v_sc_list[g][:].rearrange("p (m t) -> p t m", t=PACK))
+        for g in range(I_PASSES):
+            gather_v_words(0, g)
+        for g in range(I_PASSES):
+            gather_v_words(1, g)
+
+        h_codes = [keep.tile([P, S2], U32, name=f"h_codes{g}", align_bytes=64) for g in range(I_PASSES)]
+        h_sc = [keep.tile([P, S2], U8, name=f"h_sc{g}", align_bytes=64) for g in range(I_PASSES)]
+        wf_codes = [keep.tile([P, N], U32, name=f"wf_codes{g}", align_bytes=64) for g in range(I_PASSES)]
+        wf_sc = [keep.tile([P, N], U8, name=f"wf_sc{g}", align_bytes=64) for g in range(I_PASSES)]
+
+        def bank(half, b):
+            return psum.tile([P, 512], F32, name=f"bank{half}{b}", tag=f"bank{half}{b}")
+
+        def x_products(g):
+            banks = [bank(g % 2, t) for t in range(PACK)]
+            for a in range(K_PASSES):
+                for t in range(PACK):
+                    nc.tensor.matmul_mx(
+                        out=banks[t][:],
+                        lhsT=v_codes[a][g][:, t, :].bitcast(FP8X4),
+                        lhsT_scale=v_sc[g][ROWS * a :, t, :],
+                        rhs=v2_codes[a][:].bitcast(FP8X4),
+                        rhs_scale=v2_sc[ROWS * a :, :],
+                        start=(a == 0),
+                        stop=(a == K_PASSES - 1),
+                    )
+            return banks
+
+        def interleave(copy, dst, src, lo, hi):
+            copy(
+                dst[:, lo:hi, :].rearrange("p (c i) t -> p c t i", i=4),
+                src[:, :, lo:hi].rearrange("p t (c i) -> p c t i", i=4),
+            )
+
+        def round_wf(g):
+            wf_b = work.tile([P, N, PACK], BF16, name="wf_b", align_bytes=64)
+            cut = SCALAR_CAST[g]
+            if cut > 0:
+                interleave(nc.scalar.copy, wf_b, wf_raw[g], 0, cut)
+            if cut < N:
+                interleave(nc.vector.tensor_copy, wf_b, wf_raw[g], cut, N)
+            return wf_b
+
+        def quantize(codes, scales, src):
+            nc.vector.quantize_mx(out=codes[:].bitcast(FP8X4), scales=scales[:], in_=src[:].rearrange("p c t -> p (c t)"))
+
+        def make_h(g, banks):
+            sq = work.tile([P, PACK, S2], F32, name="sq")
+            rs = work.tile([P, PACK, S2], F32, name="rs")
+            hp = work.tile([P, PACK, S2], BF16, name="hp")
+            hb = work.tile([P, S2, PACK], BF16, name="hb", align_bytes=64)
+            for step in range(PACK + 1):
+                if step < PACK:
+                    nc.scalar.activation(sq[:, step, :], banks[step][:], ACT.Square)
+                if step > 0:
+                    t = step - 1
+                    nc.scalar.activation(rs[:, t, :], sq[:, t, :], ACT.Abs_reciprocal_sqrt, bias=1.0)
+                    nc.vector.scalar_tensor_tensor(
+                        hp[:, t, :], rs[:, t, :], d_sb[:, g, t : t + 1], rs[:, t, :], ALU.mult, ALU.mult
+                    )
+            wf_b = round_wf(g)
+            interleave(nc.vector.tensor_copy, hb, hp, 0, S2)
+            quantize(wf_codes[g], wf_sc[g], wf_b)
+            quantize(h_codes[g], h_sc[g], hb)
+
+        x0 = x_products(0)
+        x1 = x_products(1)
+        make_h(0, x0)
+        x2 = x_products(2)
+        make_h(1, x1)
+        c_banks = [bank(1, b) for b in range(N_TILES)]
+
+        def c_pass(g, b):
+            nc.tensor.matmul_mx(
+                out=c_banks[b][:],
+                lhsT=wc_codes[:, g, 2 * P * b : 2 * P * (b + 1)].bitcast(FP4X4),
+                lhsT_scale=wc_sc[:, g, P * b : P * (b + 1)],
+                rhs=h_codes[g][:].bitcast(FP8X4),
+                rhs_scale=h_sc[g][:],
+                start=(g == 0),
+                stop=(g == I_PASSES - 1),
+            )
+
+        def f_pass(g, b):
+            nc.tensor.matmul_mx(
+                out=f_banks[b][:],
+                lhsT=wf_codes[g][:, P * b : P * (b + 1)].bitcast(FP8X4),
+                lhsT_scale=wf_sc[g][:, P * b : P * (b + 1)],
+                rhs=h_codes[g][:].bitcast(FP8X4),
+                rhs_scale=h_sc[g][:],
+                start=(g == 0),
+                stop=(g == I_PASSES - 1),
+            )
+
+        for g in range(I_PASSES - 1):
+            for b in range(N_TILES):
+                c_pass(g, b)
+        make_h(2, x2)
+        f_banks = [bank(0, b) for b in range(N_TILES)]
+        for g in range(I_PASSES - 1):
+            for b in range(N_TILES):
+                f_pass(g, b)
+        for b in range(N_TILES):
+            c_pass(I_PASSES - 1, b)
+            f_pass(I_PASSES - 1, b)
+            c_sb = keep.tile([P, S2], F32, name=f"c_sb{b}")
+            res = keep.tile([P, S2], F32, name=f"res{b}")
+            nc.scalar.copy(c_sb[:], c_banks[b][:])
+            nc.vector.tensor_tensor(res[:], f_banks[b][:], c_sb[:], ALU.max)
+            nc.sync.dma_start(out[P * b : P * (b + 1), :], res[:])

@@ -25,7 +25,7 @@ N_TILES = N // P
 QUADS = 4
 ROWS = 4
 LIST_COLS = PASS // 16
-SCALAR_CAST = [0, 256, 512]
+SCALAR_CAST = [0, 512, 192]
 
 
 def tile_list_cauchy_voxel_pooling_kernel(
@@ -57,24 +57,31 @@ def tile_list_cauchy_voxel_pooling_kernel(
         nc.vector.memset(warm_in[:], 1.0)
         nc.scalar.activation(warm_out[:], warm_in[:], ACT.Abs_reciprocal_sqrt)
 
-        nc.sync.dma_start(idx2[:], offs2)
-        nc.sync.dma_start(idx[:], offs)
-        for win, words in ((v2_win, tab2_words), (v_win, tab_words)):
-            for a in range(K_PASSES):
-                nc.sync.dma_start(win[a][:].bitcast(I32), words[a].rearrange("p t i -> p (t i)").bitcast(I32))
-        for win, scales in ((v2s_win, tab2_scales), (vs_win, tab_scales)):
+        def load_words(win, words):
+            nc.sync.dma_start(win[:].bitcast(I32), words.rearrange("p t i -> p (t i)").bitcast(I32))
+
+        def load_scales(win, scales):
             for q in range(QUADS):
-                nc.gpsimd.dma_start(
+                nc.sync.dma_start(
                     win[32 * q : 32 * q + ROWS * K_PASSES, :].bitcast(I32),
                     scales[:, ROWS * q : ROWS * (q + 1), :].bitcast(I32),
                 )
+
+        nc.sync.dma_start(idx2[:], offs2)
+        load_words(v2_win[0], tab2_words[0])
+        load_scales(v2s_win, tab2_scales)
+        nc.sync.dma_start(idx[:], offs)
+        load_words(v2_win[1], tab2_words[1])
+        load_scales(vs_win, tab_scales)
+        load_words(v_win[0], tab_words[0])
+        load_words(v_win[1], tab_words[1])
+        nc.sync.dma_start(d_sb[:], dens.rearrange("(g p t) -> p g t", p=P, t=PACK))
+        nc.sync.dma_start(wf_raw[0][:], wf[0:PASS, :].rearrange("(p t) n -> p t n", t=PACK))
         for q in range(QUADS):
-            nc.gpsimd.dma_start(
+            nc.sync.dma_start(
                 wc_sc[32 * q : 32 * q + ROWS, :, :].bitcast(I32),
                 wc_scales[:, ROWS * q : ROWS * (q + 1), :].rearrange("g r n -> r g n").bitcast(I32),
             )
-        nc.sync.dma_start(d_sb[:], dens.rearrange("(g p t) -> p g t", p=P, t=PACK))
-        nc.sync.dma_start(wf_raw[0][:], wf[0:PASS, :].rearrange("(p t) n -> p t n", t=PACK))
         nc.sync.dma_start(wc_codes[:].bitcast(I32), wc_words.rearrange("g p b -> p g b").bitcast(I32))
         for g in range(1, I_PASSES):
             nc.sync.dma_start(wf_raw[g][:], wf[g * PASS : (g + 1) * PASS, :].rearrange("(p t) n -> p t n", t=PACK))

@@ -24,8 +24,8 @@ I_PASSES = S // PASS
 N_TILES = N // P
 QUADS = 4
 ROWS = 4
+SQ_BUFS = 3
 LIST_COLS = PASS // 16
-SCALAR_CAST = [0, 512, 192]
 
 
 def tile_list_cauchy_voxel_pooling_kernel(
@@ -48,8 +48,8 @@ def tile_list_cauchy_voxel_pooling_kernel(
         d_sb = keep.tile([P, I_PASSES, PACK], F32, name="d_sb")
         wf_raw = [keep.tile([P, PACK, N], F32, name=f"wf_raw{g}") for g in range(I_PASSES)]
 
-        nc.vector.memset(v2s_win[:].bitcast(I32), 0)
         nc.vector.memset(vs_win[:].bitcast(I32), 0)
+        nc.vector.memset(v2s_win[:].bitcast(I32), 0)
         nc.vector.memset(wc_sc[:].rearrange("p g n -> p (g n)").bitcast(I32), 0)
 
         warm_in = keep.tile([P, 1], F32, name="warm_in")
@@ -69,11 +69,11 @@ def tile_list_cauchy_voxel_pooling_kernel(
 
         nc.sync.dma_start(idx2[:], offs2)
         load_words(v2_win[0], tab2_words[0])
-        load_scales(v2s_win, tab2_scales)
         nc.sync.dma_start(idx[:], offs)
-        load_words(v2_win[1], tab2_words[1])
         load_scales(vs_win, tab_scales)
         load_words(v_win[0], tab_words[0])
+        load_scales(v2s_win, tab2_scales)
+        load_words(v2_win[1], tab2_words[1])
         load_words(v_win[1], tab_words[1])
         nc.sync.dma_start(d_sb[:], dens.rearrange("(g p t) -> p g t", p=P, t=PACK))
         nc.sync.dma_start(wf_raw[0][:], wf[0:PASS, :].rearrange("(p t) n -> p t n", t=PACK))
@@ -88,30 +88,27 @@ def tile_list_cauchy_voxel_pooling_kernel(
 
         v2_codes = [keep.tile([P, S2], U32, name=f"v2_codes{a}", align_bytes=64) for a in range(K_PASSES)]
         v2_sc = keep.tile([P, S2], U8, name="v2_sc", align_bytes=64)
-        v_codes = [
-            [keep.tile([P, PACK, P], U32, name=f"v_codes{a}_{g}", align_bytes=64) for g in range(I_PASSES)]
-            for a in range(K_PASSES)
-        ]
-        v_sc_list = [keep.tile([P, PASS], U8, name=f"v_sc_list{g}", align_bytes=64) for g in range(I_PASSES)]
-        v_sc = [keep.tile([P, PACK, P], U8, name=f"v_sc{g}", align_bytes=64) for g in range(I_PASSES)]
+        v_codes = [keep.tile([P, I_PASSES, PACK, P], U32, name=f"v_codes{a}", align_bytes=64) for a in range(K_PASSES)]
+        v_sc_list = keep.tile([P, S], U8, name="v_sc_list", align_bytes=64)
+        v_sc = keep.tile([P, I_PASSES, PACK, P], U8, name="v_sc", align_bytes=64)
 
-        def entries(g):
-            return idx[:, g * LIST_COLS : (g + 1) * LIST_COLS]
-
-        def gather_v_words(a, g):
-            nc.vector.tensor_copy(v_codes[a][g][:].rearrange("p t m -> p m t"), v_win[a][:].indirect(entries(g)))
+        def gather_v_words(a, lo, hi):
+            nc.vector.tensor_copy(
+                v_codes[a][:, lo:hi].rearrange("p g t m -> p g m t"),
+                v_win[a][:].indirect(idx[:, lo * LIST_COLS : hi * LIST_COLS]),
+            )
 
         nc.vector.tensor_copy(v2_codes[0][:], v2_win[0][:].indirect(idx2[:]))
+        nc.vector.tensor_copy(v_sc_list[:], vs_win[:].indirect(idx[:]))
+        gather_v_words(0, 0, I_PASSES)
+        nc.vector.tensor_copy(
+            v_sc[:].rearrange("p g t m -> p t g m"),
+            v_sc_list[:].rearrange("p (g m t) -> p t g m", g=I_PASSES, t=PACK),
+        )
         nc.vector.tensor_copy(v2_sc[:], v2s_win[:].indirect(idx2[:]))
         nc.vector.tensor_copy(v2_codes[1][:], v2_win[1][:].indirect(idx2[:]))
         for g in range(I_PASSES):
-            nc.vector.tensor_copy(v_sc_list[g][:], vs_win[:].indirect(entries(g)))
-        for g in range(I_PASSES):
-            nc.vector.tensor_copy(v_sc[g][:], v_sc_list[g][:].rearrange("p (m t) -> p t m", t=PACK))
-        for g in range(I_PASSES):
-            gather_v_words(0, g)
-        for g in range(I_PASSES):
-            gather_v_words(1, g)
+            gather_v_words(1, g, g + 1)
 
         h_codes = [keep.tile([P, S2], U32, name=f"h_codes{g}", align_bytes=64) for g in range(I_PASSES)]
         h_sc = [keep.tile([P, S2], U8, name=f"h_sc{g}", align_bytes=64) for g in range(I_PASSES)]
@@ -123,61 +120,72 @@ def tile_list_cauchy_voxel_pooling_kernel(
 
         def x_products(g):
             banks = [bank(g % 2, t) for t in range(PACK)]
-            for a in range(K_PASSES):
-                for t in range(PACK):
-                    nc.tensor.matmul_mx(
-                        out=banks[t][:],
-                        lhsT=v_codes[a][g][:, t, :].bitcast(FP8X4),
-                        lhsT_scale=v_sc[g][ROWS * a :, t, :],
-                        rhs=v2_codes[a][:].bitcast(FP8X4),
-                        rhs_scale=v2_sc[ROWS * a :, :],
-                        start=(a == 0),
-                        stop=(a == K_PASSES - 1),
-                    )
+            if g == 0:
+                order = [(a, t) for a in range(K_PASSES) for t in range(PACK)]
+            else:
+                order = [(a, t) for t in range(PACK) for a in reversed(range(K_PASSES))]
+            opened = set()
+            for a, t in order:
+                nc.tensor.matmul_mx(
+                    out=banks[t][:],
+                    lhsT=v_codes[a][:, g, t, :].bitcast(FP8X4),
+                    lhsT_scale=v_sc[ROWS * a :, g, t, :],
+                    rhs=v2_codes[a][:].bitcast(FP8X4),
+                    rhs_scale=v2_sc[ROWS * a :, :],
+                    start=(t not in opened),
+                    stop=(t in opened),
+                )
+                opened.add(t)
             return banks
 
-        def interleave(copy, dst, src, lo, hi):
-            copy(
-                dst[:, lo:hi, :].rearrange("p (c i) t -> p c t i", i=4),
-                src[:, :, lo:hi].rearrange("p t (c i) -> p c t i", i=4),
-            )
-
-        def round_wf(g):
-            wf_b = work.tile([P, N, PACK], BF16, name="wf_b", align_bytes=64)
-            cut = SCALAR_CAST[g]
-            if cut > 0:
-                interleave(nc.scalar.copy, wf_b, wf_raw[g], 0, cut)
-            if cut < N:
-                interleave(nc.vector.tensor_copy, wf_b, wf_raw[g], cut, N)
+        def round_wf(copy, g, lo, hi, tag, bufs):
+            wf_b = work.tile([P, hi - lo, PACK], BF16, name=f"wf_b{g}_{lo}", tag=tag, bufs=bufs, align_bytes=64)
+            copy(wf_b[:], wf_raw[g][:, :, lo:hi].rearrange("p t n -> p n t"))
             return wf_b
 
         def quantize(codes, scales, src):
-            nc.vector.quantize_mx(out=codes[:].bitcast(FP8X4), scales=scales[:], in_=src[:].rearrange("p c t -> p (c t)"))
+            nc.vector.quantize_mx(out=codes.bitcast(FP8X4), scales=scales, in_=src[:].rearrange("p c t -> p (c t)"))
 
-        def make_h(g, banks):
-            sq = work.tile([P, PACK, S2], F32, name="sq")
+        def quantize_wf(g, lo, hi, wf_b):
+            quantize(wf_codes[g][:, lo:hi], wf_sc[g][:, lo:hi], wf_b)
+
+        def weights(g, banks):
             rs = work.tile([P, PACK, S2], F32, name="rs")
             hp = work.tile([P, PACK, S2], BF16, name="hp")
-            hb = work.tile([P, S2, PACK], BF16, name="hb", align_bytes=64)
+            sq = []
             for step in range(PACK + 1):
                 if step < PACK:
-                    nc.scalar.activation(sq[:, step, :], banks[step][:], ACT.Square)
+                    sq.append(work.tile([P, S2], F32, name="sq", tag="sq", bufs=SQ_BUFS, align_bytes=64))
+                    nc.scalar.activation(sq[step][:], banks[step][:], ACT.Square)
                 if step > 0:
                     t = step - 1
-                    nc.scalar.activation(rs[:, t, :], sq[:, t, :], ACT.Abs_reciprocal_sqrt, bias=1.0)
+                    nc.scalar.activation(rs[:, t, :], sq[t][:], ACT.Abs_reciprocal_sqrt, bias=1.0)
                     nc.vector.scalar_tensor_tensor(
                         hp[:, t, :], rs[:, t, :], d_sb[:, g, t : t + 1], rs[:, t, :], ALU.mult, ALU.mult
                     )
-            wf_b = round_wf(g)
-            interleave(nc.vector.tensor_copy, hb, hp, 0, S2)
-            quantize(wf_codes[g], wf_sc[g], wf_b)
-            quantize(h_codes[g], h_sc[g], hb)
+            return hp
+
+        def interleave_h(hp):
+            hb = work.tile([P, S2, PACK], BF16, name="hb", align_bytes=64)
+            nc.vector.tensor_copy(hb[:], hp[:].rearrange("p t j -> p j t"))
+            return hb
+
+        def quantize_h(g, hb):
+            quantize(h_codes[g][:], h_sc[g][:], hb)
 
         x0 = x_products(0)
         x1 = x_products(1)
-        make_h(0, x0)
+        w0 = round_wf(nc.vector.tensor_copy, 0, 0, N, "wf_v", 2)
+        hp = weights(0, x0)
+        quantize_wf(0, 0, N, w0)
+        hb = interleave_h(hp)
+        w1 = round_wf(nc.vector.tensor_copy, 1, 0, N // 2, "wf_v", 2)
+        quantize_h(0, hb)
         x2 = x_products(2)
-        make_h(1, x1)
+        hp = weights(1, x1)
+        quantize_wf(1, 0, N // 2, w1)
+        hb = interleave_h(hp)
+        quantize_h(1, hb)
         c_banks = [bank(1, b) for b in range(N_TILES)]
 
         def c_pass(g, b):
@@ -205,7 +213,13 @@ def tile_list_cauchy_voxel_pooling_kernel(
         for g in range(I_PASSES - 1):
             for b in range(N_TILES):
                 c_pass(g, b)
-        make_h(2, x2)
+        hp = weights(2, x2)
+        w1 = round_wf(nc.scalar.copy, 1, N // 2, N, "sq", SQ_BUFS)
+        w2 = round_wf(nc.scalar.copy, 2, 0, N, "sq", SQ_BUFS)
+        hb = interleave_h(hp)
+        quantize_wf(1, N // 2, N, w1)
+        quantize_h(2, hb)
+        quantize_wf(2, 0, N, w2)
         f_banks = [bank(0, b) for b in range(N_TILES)]
         for g in range(I_PASSES - 1):
             for b in range(N_TILES):

@@ -22,9 +22,10 @@ PASS = P * PACK
 K_PASSES = K // PASS
 I_PASSES = S // PASS
 N_TILES = N // P
-QUADS = 4
 ROWS = 4
+QUADS = 4
 SQ_BUFS = 3
+HALF = S2 // 2
 LIST_COLS = PASS // 16
 
 
@@ -48,8 +49,8 @@ def tile_list_cauchy_voxel_pooling_kernel(
         d_sb = keep.tile([P, I_PASSES, PACK], F32, name="d_sb")
         wf_raw = [keep.tile([P, PACK, N], F32, name=f"wf_raw{g}") for g in range(I_PASSES)]
 
-        nc.vector.memset(vs_win[:].bitcast(I32), 0)
         nc.vector.memset(v2s_win[:].bitcast(I32), 0)
+        nc.vector.memset(vs_win[:].bitcast(I32), 0)
         nc.vector.memset(wc_sc[:].rearrange("p g n -> p (g n)").bitcast(I32), 0)
 
         warm_in = keep.tile([P, 1], F32, name="warm_in")
@@ -60,7 +61,15 @@ def tile_list_cauchy_voxel_pooling_kernel(
         def load_words(win, words):
             nc.sync.dma_start(win[:].bitcast(I32), words.rearrange("p t i -> p (t i)").bitcast(I32))
 
-        def load_scales(win, scales):
+        def load_scale_rows(win, scales):
+            for r in range(ROWS):
+                for a in range(K_PASSES):
+                    nc.sync.dma_start(
+                        win[ROWS * a + r : P : 32, :].bitcast(I32),
+                        scales[a].rearrange("(q r) t -> r q t", r=ROWS)[r].bitcast(I32),
+                    )
+
+        def load_scale_quadrants(win, scales):
             for q in range(QUADS):
                 nc.sync.dma_start(
                     win[32 * q : 32 * q + ROWS * K_PASSES, :].bitcast(I32),
@@ -70,21 +79,21 @@ def tile_list_cauchy_voxel_pooling_kernel(
         nc.sync.dma_start(idx2[:], offs2)
         load_words(v2_win[0], tab2_words[0])
         nc.sync.dma_start(idx[:], offs)
-        load_scales(vs_win, tab_scales)
+        load_scale_quadrants(v2s_win, tab2_scales)
+        load_scale_rows(vs_win, tab_scales)
         load_words(v_win[0], tab_words[0])
-        load_scales(v2s_win, tab2_scales)
-        load_words(v2_win[1], tab2_words[1])
         load_words(v_win[1], tab_words[1])
+        load_words(v2_win[1], tab2_words[1])
         nc.sync.dma_start(d_sb[:], dens.rearrange("(g p t) -> p g t", p=P, t=PACK))
-        nc.sync.dma_start(wf_raw[0][:], wf[0:PASS, :].rearrange("(p t) n -> p t n", t=PACK))
-        for q in range(QUADS):
-            nc.sync.dma_start(
-                wc_sc[32 * q : 32 * q + ROWS, :, :].bitcast(I32),
-                wc_scales[:, ROWS * q : ROWS * (q + 1), :].rearrange("g r n -> r g n").bitcast(I32),
-            )
-        nc.sync.dma_start(wc_codes[:].bitcast(I32), wc_words.rearrange("g p b -> p g b").bitcast(I32))
-        for g in range(1, I_PASSES):
+        for g in range(I_PASSES):
+            if g == I_PASSES - 1:
+                nc.sync.dma_start(wc_codes[:].bitcast(I32), wc_words.rearrange("g p b -> p g b").bitcast(I32))
             nc.sync.dma_start(wf_raw[g][:], wf[g * PASS : (g + 1) * PASS, :].rearrange("(p t) n -> p t n", t=PACK))
+        for r in range(ROWS):
+            nc.sync.dma_start(
+                wc_sc[r:P:32, :, :].bitcast(I32),
+                wc_scales.rearrange("g (q r) n -> r q g n", r=ROWS)[r].bitcast(I32),
+            )
 
         v2_codes = [keep.tile([P, S2], U32, name=f"v2_codes{a}", align_bytes=64) for a in range(K_PASSES)]
         v2_sc = keep.tile([P, S2], U8, name="v2_sc", align_bytes=64)
@@ -99,16 +108,16 @@ def tile_list_cauchy_voxel_pooling_kernel(
             )
 
         nc.vector.tensor_copy(v2_codes[0][:], v2_win[0][:].indirect(idx2[:]))
+        nc.vector.tensor_copy(v2_sc[:], v2s_win[:].indirect(idx2[:]))
         nc.vector.tensor_copy(v_sc_list[:], vs_win[:].indirect(idx[:]))
-        gather_v_words(0, 0, I_PASSES)
         nc.vector.tensor_copy(
             v_sc[:].rearrange("p g t m -> p t g m"),
             v_sc_list[:].rearrange("p (g m t) -> p t g m", g=I_PASSES, t=PACK),
         )
-        nc.vector.tensor_copy(v2_sc[:], v2s_win[:].indirect(idx2[:]))
+        gather_v_words(0, 0, I_PASSES)
+        gather_v_words(1, 0, I_PASSES - 1)
         nc.vector.tensor_copy(v2_codes[1][:], v2_win[1][:].indirect(idx2[:]))
-        for g in range(I_PASSES):
-            gather_v_words(1, g, g + 1)
+        gather_v_words(1, I_PASSES - 1, I_PASSES)
 
         h_codes = [keep.tile([P, S2], U32, name=f"h_codes{g}", align_bytes=64) for g in range(I_PASSES)]
         h_sc = [keep.tile([P, S2], U8, name=f"h_sc{g}", align_bytes=64) for g in range(I_PASSES)]
@@ -151,7 +160,7 @@ def tile_list_cauchy_voxel_pooling_kernel(
 
         def weights(g, banks):
             rs = work.tile([P, PACK, S2], F32, name="rs")
-            hp = work.tile([P, PACK, S2], BF16, name="hp")
+            hp = work.tile([P, 2, PACK, HALF], BF16, name="hp")
             sq = []
             for step in range(PACK + 1):
                 if step < PACK:
@@ -160,32 +169,35 @@ def tile_list_cauchy_voxel_pooling_kernel(
                 if step > 0:
                     t = step - 1
                     nc.scalar.activation(rs[:, t, :], sq[t][:], ACT.Abs_reciprocal_sqrt, bias=1.0)
-                    nc.vector.scalar_tensor_tensor(
-                        hp[:, t, :], rs[:, t, :], d_sb[:, g, t : t + 1], rs[:, t, :], ALU.mult, ALU.mult
-                    )
+                    d_col = d_sb[:, g, t : t + 1]
+                    if t < PACK - 1:
+                        r = rs[:, t, :].rearrange("p (u j) -> p u j", u=2)
+                        nc.vector.scalar_tensor_tensor(hp[:, :, t, :], r, d_col, r, ALU.mult, ALU.mult)
+                    else:
+                        for u in range(2):
+                            r = rs[:, t, u * HALF : (u + 1) * HALF]
+                            nc.vector.scalar_tensor_tensor(hp[:, u, t, :], r, d_col, r, ALU.mult, ALU.mult)
             return hp
 
-        def interleave_h(hp):
-            hb = work.tile([P, S2, PACK], BF16, name="hb", align_bytes=64)
-            nc.vector.tensor_copy(hb[:], hp[:].rearrange("p t j -> p j t"))
-            return hb
-
-        def quantize_h(g, hb):
-            quantize(h_codes[g][:], h_sc[g][:], hb)
+        def finish_h(g, hp):
+            hb = [work.tile([P, HALF, PACK], BF16, name=f"hb{u}", align_bytes=64) for u in range(2)]
+            for u in range(2):
+                nc.vector.tensor_copy(hb[u][:], hp[:, u].rearrange("p t j -> p j t"))
+            for u in range(2):
+                cols = slice(u * HALF, (u + 1) * HALF)
+                quantize(h_codes[g][:, cols], h_sc[g][:, cols], hb[u])
 
         x0 = x_products(0)
         x1 = x_products(1)
         w0 = round_wf(nc.vector.tensor_copy, 0, 0, N, "wf_v", 2)
         hp = weights(0, x0)
         quantize_wf(0, 0, N, w0)
-        hb = interleave_h(hp)
+        finish_h(0, hp)
         w1 = round_wf(nc.vector.tensor_copy, 1, 0, N // 2, "wf_v", 2)
-        quantize_h(0, hb)
         x2 = x_products(2)
         hp = weights(1, x1)
         quantize_wf(1, 0, N // 2, w1)
-        hb = interleave_h(hp)
-        quantize_h(1, hb)
+        finish_h(1, hp)
         c_banks = [bank(1, b) for b in range(N_TILES)]
 
         def c_pass(g, b):
@@ -216,9 +228,8 @@ def tile_list_cauchy_voxel_pooling_kernel(
         hp = weights(2, x2)
         w1 = round_wf(nc.scalar.copy, 1, N // 2, N, "sq", SQ_BUFS)
         w2 = round_wf(nc.scalar.copy, 2, 0, N, "sq", SQ_BUFS)
-        hb = interleave_h(hp)
         quantize_wf(1, N // 2, N, w1)
-        quantize_h(2, hb)
+        finish_h(2, hp)
         quantize_wf(2, 0, N, w2)
         f_banks = [bank(0, b) for b in range(N_TILES)]
         for g in range(I_PASSES - 1):
@@ -229,6 +240,10 @@ def tile_list_cauchy_voxel_pooling_kernel(
             f_pass(I_PASSES - 1, b)
             c_sb = keep.tile([P, S2], F32, name=f"c_sb{b}")
             res = keep.tile([P, S2], F32, name=f"res{b}")
-            nc.scalar.copy(c_sb[:], c_banks[b][:])
-            nc.vector.tensor_tensor(res[:], f_banks[b][:], c_sb[:], ALU.max)
-            nc.sync.dma_start(out[P * b : P * (b + 1), :], res[:])
+            pieces = 2 if b in (0, N_TILES - 1) else 1
+            width = S2 // pieces
+            for u in range(pieces):
+                cols = slice(u * width, (u + 1) * width)
+                nc.scalar.copy(c_sb[:, cols], c_banks[b][:, cols])
+                nc.vector.tensor_tensor(res[:, cols], f_banks[b][:, cols], c_sb[:, cols], ALU.max)
+                nc.sync.dma_start(out[P * b : P * (b + 1), cols], res[:, cols])

@@ -23,7 +23,7 @@ K_PASSES = K // PASS
 I_PASSES = S // PASS
 N_TILES = N // P
 ROWS = 4
-QUADS = 4
+SC_BASE = 96
 SQ_BUFS = 3
 HALF = S2 // 2
 LIST_COLS = PASS // 16
@@ -36,22 +36,22 @@ def tile_list_cauchy_voxel_pooling_kernel(
     with ExitStack() as ctx:
         keep = ctx.enter_context(tc.tile_pool(name="keep", bufs=1))
         work = ctx.enter_context(tc.tile_pool(name="work", bufs=2))
+        reuse = ctx.enter_context(tc.tile_pool(name="reuse", bufs=1))
         psum = ctx.enter_context(tc.psum_pool(name="psum", bufs=1))
 
         idx = keep.tile([P, S // 16], U16, name="idx")
         idx2 = keep.tile([P, S2 // 16], U16, name="idx2")
-        v_win = [keep.tile([P, T], U32, name=f"v_win{a}") for a in range(K_PASSES)]
-        v2_win = [keep.tile([P, T2], U32, name=f"v2_win{a}") for a in range(K_PASSES)]
+        v_win = [reuse.tile([P, T], U32, name="v_win0", offset=0)]
+        v_win.append(keep.tile([P, T], U32, name="v_win1"))
+        v2_win = [keep.tile([P, T2], U32, name=f"v2_win{a}", tag=f"v2_win{a}", align_bytes=64) for a in range(K_PASSES)]
         vs_win = keep.tile([P, T], U8, name="vs_win")
         v2s_win = keep.tile([P, T2], U8, name="v2s_win")
-        wc_codes = keep.tile([P, I_PASSES, 2 * N], U8, name="wc_codes", align_bytes=64)
-        wc_sc = keep.tile([P, I_PASSES, N], U8, name="wc_sc", align_bytes=64)
+        sc_mm = keep.tile([P, S + S2], U8, name="sc_mm", align_bytes=64)
         d_sb = keep.tile([P, I_PASSES, PACK], F32, name="d_sb")
-        wf_raw = [keep.tile([P, PACK, N], F32, name=f"wf_raw{g}") for g in range(I_PASSES)]
 
-        nc.vector.memset(v2s_win[:].bitcast(I32), 0)
-        nc.vector.memset(vs_win[:].bitcast(I32), 0)
-        nc.vector.memset(wc_sc[:].rearrange("p g n -> p (g n)").bitcast(I32), 0)
+        for win in (vs_win, v2s_win):
+            nc.vector.memset(win[0:SC_BASE, :].bitcast(I32), 0)
+        nc.gpsimd.memset(sc_mm[:].bitcast(I32), 0)
 
         warm_in = keep.tile([P, 1], F32, name="warm_in")
         warm_out = keep.tile([P, 1], F32, name="warm_out")
@@ -61,63 +61,69 @@ def tile_list_cauchy_voxel_pooling_kernel(
         def load_words(win, words):
             nc.sync.dma_start(win[:].bitcast(I32), words.rearrange("p t i -> p (t i)").bitcast(I32))
 
-        def load_scale_rows(win, scales):
-            for r in range(ROWS):
-                for a in range(K_PASSES):
-                    nc.sync.dma_start(
-                        win[ROWS * a + r : P : 32, :].bitcast(I32),
-                        scales[a].rearrange("(q r) t -> r q t", r=ROWS)[r].bitcast(I32),
-                    )
+        def load_scales(win, scales):
+            nc.sync.dma_start(win[SC_BASE:P, :].bitcast(I32), scales.rearrange("a q t -> (a q) t").bitcast(I32))
 
-        def load_scale_quadrants(win, scales):
-            for q in range(QUADS):
-                nc.sync.dma_start(
-                    win[32 * q : 32 * q + ROWS * K_PASSES, :].bitcast(I32),
-                    scales[:, ROWS * q : ROWS * (q + 1), :].bitcast(I32),
+        nc.sync.dma_start(idx[:], offs)
+        load_scales(vs_win, tab_scales)
+        nc.sync.dma_start(idx2[:], offs2)
+        load_scales(v2s_win, tab2_scales)
+        for a in range(K_PASSES):
+            load_words(v_win[a], tab_words[a])
+        for a in range(K_PASSES):
+            load_words(v2_win[a], tab2_words[a])
+        nc.gpsimd.dma_start(d_sb[:], dens.rearrange("(g p t) -> p g t", p=P, t=PACK))
+
+        v_sc_list = keep.tile([P, S], U8, name="v_sc_list", tag="v_first", align_bytes=64)
+        v2_sc_list = keep.tile([P, S2], U8, name="v2_sc_list", align_bytes=64)
+        sc_all = keep.tile([P, S + S2], U8, name="sc_all", align_bytes=64)
+        nc.vector.tensor_copy(v_sc_list[:], vs_win[:].indirect(idx[:]))
+        nc.vector.tensor_copy(v2_sc_list[:], v2s_win[:].indirect(idx2[:]))
+        nc.vector.tensor_copy(sc_all[:, S : S + S2].bitcast(I32), v2_sc_list[:].bitcast(I32))
+        nc.vector.tensor_copy(
+            sc_all[:, 0:S].rearrange("p (g t m) -> p t g m", g=I_PASSES, t=PACK),
+            v_sc_list[:].rearrange("p (g m t) -> p t g m", g=I_PASSES, t=PACK),
+        )
+        for r in range(ROWS):
+            for a in range(K_PASSES):
+                (nc.gpsimd if r == 0 else nc.scalar).dma_start(
+                    sc_mm[ROWS * a + r : P : 32, :].bitcast(I32),
+                    sc_all[SC_BASE + 16 * a + r : SC_BASE + 16 * (a + 1) : ROWS, :].bitcast(I32),
                 )
 
-        nc.sync.dma_start(idx2[:], offs2)
-        load_words(v2_win[0], tab2_words[0])
-        nc.sync.dma_start(idx[:], offs)
-        load_scale_quadrants(v2s_win, tab2_scales)
-        load_scale_rows(vs_win, tab_scales)
-        load_words(v_win[0], tab_words[0])
-        load_words(v_win[1], tab_words[1])
-        load_words(v2_win[1], tab2_words[1])
-        nc.sync.dma_start(d_sb[:], dens.rearrange("(g p t) -> p g t", p=P, t=PACK))
+        v_codes = {}
+
+        def gather_v_words(a, lo, hi, tag):
+            codes = keep.tile([P, hi - lo, PACK, P], U32, name=f"v_codes{a}{lo}", tag=tag, align_bytes=64)
+            for g in range(lo, hi):
+                v_codes[a, g] = codes[:, g - lo]
+            nc.vector.tensor_copy(
+                codes[:].rearrange("p g t m -> p g m t"),
+                v_win[a][:].indirect(idx[:, lo * LIST_COLS : hi * LIST_COLS]),
+            )
+
+        gather_v_words(0, 0, I_PASSES, "v_first")
+        wf_rows = reuse.tile([P, I_PASSES * PACK * N], F32, name="wf_rows", offset=I_PASSES * N)
+        wf_raw = [wf_rows[:, g * PACK * N : (g + 1) * PACK * N].rearrange("p (t n) -> p t n", t=PACK) for g in range(I_PASSES)]
         for g in range(I_PASSES):
-            if g == I_PASSES - 1:
-                nc.sync.dma_start(wc_codes[:].bitcast(I32), wc_words.rearrange("g p b -> p g b").bitcast(I32))
-            nc.sync.dma_start(wf_raw[g][:], wf[g * PASS : (g + 1) * PASS, :].rearrange("(p t) n -> p t n", t=PACK))
+            nc.sync.dma_start(
+                wf_rows[:, g * PACK * N : (g + 1) * PACK * N],
+                wf[g * PASS : (g + 1) * PASS, :].rearrange("(p t) n -> p (t n)", t=PACK),
+            )
+        wc_sc = reuse.tile([P, I_PASSES, N], U8, name="wc_sc", offset=0, align_bytes=64)
+        nc.vector.memset(wc_sc[:].rearrange("p g n -> p (g n)").bitcast(I32), 0)
         for r in range(ROWS):
             nc.sync.dma_start(
                 wc_sc[r:P:32, :, :].bitcast(I32),
                 wc_scales.rearrange("g (q r) n -> r q g n", r=ROWS)[r].bitcast(I32),
             )
-
+        gather_v_words(1, 0, I_PASSES - 1, "v_second")
         v2_codes = [keep.tile([P, S2], U32, name=f"v2_codes{a}", align_bytes=64) for a in range(K_PASSES)]
-        v2_sc = keep.tile([P, S2], U8, name="v2_sc", align_bytes=64)
-        v_codes = [keep.tile([P, I_PASSES, PACK, P], U32, name=f"v_codes{a}", align_bytes=64) for a in range(K_PASSES)]
-        v_sc_list = keep.tile([P, S], U8, name="v_sc_list", align_bytes=64)
-        v_sc = keep.tile([P, I_PASSES, PACK, P], U8, name="v_sc", align_bytes=64)
-
-        def gather_v_words(a, lo, hi):
-            nc.vector.tensor_copy(
-                v_codes[a][:, lo:hi].rearrange("p g t m -> p g m t"),
-                v_win[a][:].indirect(idx[:, lo * LIST_COLS : hi * LIST_COLS]),
-            )
-
-        nc.vector.tensor_copy(v2_codes[0][:], v2_win[0][:].indirect(idx2[:]))
-        nc.vector.tensor_copy(v2_sc[:], v2s_win[:].indirect(idx2[:]))
-        nc.vector.tensor_copy(v_sc_list[:], vs_win[:].indirect(idx[:]))
-        nc.vector.tensor_copy(
-            v_sc[:].rearrange("p g t m -> p t g m"),
-            v_sc_list[:].rearrange("p (g m t) -> p t g m", g=I_PASSES, t=PACK),
-        )
-        gather_v_words(0, 0, I_PASSES)
-        gather_v_words(1, 0, I_PASSES - 1)
-        nc.vector.tensor_copy(v2_codes[1][:], v2_win[1][:].indirect(idx2[:]))
-        gather_v_words(1, I_PASSES - 1, I_PASSES)
+        for a in range(K_PASSES):
+            nc.vector.tensor_copy(v2_codes[a][:], v2_win[a][:].indirect(idx2[:]))
+        wc_codes = keep.tile([P, I_PASSES, 2 * N], U8, name="wc_codes", tag="v2_win0", align_bytes=64)
+        nc.sync.dma_start(wc_codes[:].bitcast(I32), wc_words.rearrange("g p b -> p g b").bitcast(I32))
+        gather_v_words(1, I_PASSES - 1, I_PASSES, "v2_win1")
 
         h_codes = [keep.tile([P, S2], U32, name=f"h_codes{g}", align_bytes=64) for g in range(I_PASSES)]
         h_sc = [keep.tile([P, S2], U8, name=f"h_sc{g}", align_bytes=64) for g in range(I_PASSES)]
@@ -137,10 +143,10 @@ def tile_list_cauchy_voxel_pooling_kernel(
             for a, t in order:
                 nc.tensor.matmul_mx(
                     out=banks[t][:],
-                    lhsT=v_codes[a][:, g, t, :].bitcast(FP8X4),
-                    lhsT_scale=v_sc[ROWS * a :, g, t, :],
+                    lhsT=v_codes[a, g][:, t, :].bitcast(FP8X4),
+                    lhsT_scale=sc_mm[ROWS * a :, (g * PACK + t) * P : (g * PACK + t + 1) * P],
                     rhs=v2_codes[a][:].bitcast(FP8X4),
-                    rhs_scale=v2_sc[ROWS * a :, :],
+                    rhs_scale=sc_mm[ROWS * a :, S : S + S2],
                     start=(t not in opened),
                     stop=(t in opened),
                 )

@@ -41,17 +41,18 @@ def tile_list_cauchy_voxel_pooling_kernel(
 
         idx = keep.tile([P, S // 16], U16, name="idx")
         idx2 = keep.tile([P, S2 // 16], U16, name="idx2")
-        v_win = [reuse.tile([P, T], U32, name="v_win0", offset=0)]
-        v_win.append(keep.tile([P, T], U32, name="v_win1"))
+        v_win = [reuse.tile([P, T], U32, name="v_win0", offset=0), keep.tile([P, T], U32, name="v_win1")]
         v2_win = [keep.tile([P, T2], U32, name=f"v2_win{a}", tag=f"v2_win{a}", align_bytes=64) for a in range(K_PASSES)]
         vs_win = keep.tile([P, T], U8, name="vs_win")
         v2s_win = keep.tile([P, T2], U8, name="v2s_win")
-        sc_mm = keep.tile([P, S + S2], U8, name="sc_mm", align_bytes=64)
+        sc_mm = [keep.tile([P, S + S2], U8, name=f"sc_mm{a}", align_bytes=64) for a in range(K_PASSES)]
         d_sb = keep.tile([P, I_PASSES, PACK], F32, name="d_sb")
 
         for win in (vs_win, v2s_win):
             nc.vector.memset(win[0:SC_BASE, :].bitcast(I32), 0)
-        nc.gpsimd.memset(sc_mm[:].bitcast(I32), 0)
+        nc.gpsimd.dma_start(d_sb[:], dens.rearrange("(g p t) -> p g t", p=P, t=PACK))
+        for a in range(K_PASSES):
+            nc.gpsimd.memset(sc_mm[a][:].bitcast(I32), 0)
 
         warm_in = keep.tile([P, 1], F32, name="warm_in")
         warm_out = keep.tile([P, 1], F32, name="warm_out")
@@ -68,11 +69,10 @@ def tile_list_cauchy_voxel_pooling_kernel(
         load_scales(vs_win, tab_scales)
         nc.sync.dma_start(idx2[:], offs2)
         load_scales(v2s_win, tab2_scales)
-        for a in range(K_PASSES):
-            load_words(v_win[a], tab_words[a])
-        for a in range(K_PASSES):
-            load_words(v2_win[a], tab2_words[a])
-        nc.gpsimd.dma_start(d_sb[:], dens.rearrange("(g p t) -> p g t", p=P, t=PACK))
+        load_words(v_win[0], tab_words[0])
+        load_words(v_win[1], tab_words[1])
+        load_words(v2_win[0], tab2_words[0])
+        load_words(v2_win[1], tab2_words[1])
 
         v_sc_list = keep.tile([P, S], U8, name="v_sc_list", tag="v_first", align_bytes=64)
         v2_sc_list = keep.tile([P, S2], U8, name="v2_sc_list", align_bytes=64)
@@ -84,17 +84,16 @@ def tile_list_cauchy_voxel_pooling_kernel(
             sc_all[:, 0:S].rearrange("p (g t m) -> p t g m", g=I_PASSES, t=PACK),
             v_sc_list[:].rearrange("p (g m t) -> p t g m", g=I_PASSES, t=PACK),
         )
-        for r in range(ROWS):
-            for a in range(K_PASSES):
-                (nc.gpsimd if r == 0 else nc.scalar).dma_start(
-                    sc_mm[ROWS * a + r : P : 32, :].bitcast(I32),
+        for a in range(K_PASSES):
+            for r in range(ROWS):
+                (nc.gpsimd if a == 1 and r > 1 else nc.scalar).dma_start(
+                    sc_mm[a][r:P:32, :].bitcast(I32),
                     sc_all[SC_BASE + 16 * a + r : SC_BASE + 16 * (a + 1) : ROWS, :].bitcast(I32),
                 )
 
         v_codes = {}
 
-        def gather_v_words(a, lo, hi, tag):
-            codes = keep.tile([P, hi - lo, PACK, P], U32, name=f"v_codes{a}{lo}", tag=tag, align_bytes=64)
+        def gather_v_words(a, lo, hi, codes):
             for g in range(lo, hi):
                 v_codes[a, g] = codes[:, g - lo]
             nc.vector.tensor_copy(
@@ -102,28 +101,34 @@ def tile_list_cauchy_voxel_pooling_kernel(
                 v_win[a][:].indirect(idx[:, lo * LIST_COLS : hi * LIST_COLS]),
             )
 
-        gather_v_words(0, 0, I_PASSES, "v_first")
-        wf_rows = reuse.tile([P, I_PASSES * PACK * N], F32, name="wf_rows", offset=I_PASSES * N)
+        gather_v_words(0, 0, I_PASSES, keep.tile([P, I_PASSES, PACK, P], U32, name="v_codes0", tag="v_first", align_bytes=64))
+        v2_codes = [keep.tile([P, S2], U32, name=f"v2_codes{a}", align_bytes=64) for a in range(K_PASSES)]
+        wf_rows = reuse.tile([P, I_PASSES * PACK * N], F32, name="wf_rows", offset=I_PASSES * 3 * N)
         wf_raw = [wf_rows[:, g * PACK * N : (g + 1) * PACK * N].rearrange("p (t n) -> p t n", t=PACK) for g in range(I_PASSES)]
         for g in range(I_PASSES):
             nc.sync.dma_start(
                 wf_rows[:, g * PACK * N : (g + 1) * PACK * N],
                 wf[g * PASS : (g + 1) * PASS, :].rearrange("(p t) n -> p (t n)", t=PACK),
             )
-        wc_sc = reuse.tile([P, I_PASSES, N], U8, name="wc_sc", offset=0, align_bytes=64)
-        nc.vector.memset(wc_sc[:].rearrange("p g n -> p (g n)").bitcast(I32), 0)
+        wc_codes = reuse.tile([P, I_PASSES, 2 * N], U8, name="wc_codes", offset=0, align_bytes=64)
+        nc.sync.dma_start(wc_codes[:].bitcast(I32), wc_words.rearrange("g p b -> p g b").bitcast(I32))
+        wc_sc = reuse.tile([P, I_PASSES, N], U8, name="wc_sc", offset=I_PASSES * 2 * N, align_bytes=64)
+        nc.gpsimd.memset(wc_sc[:].rearrange("p g n -> p (g n)").bitcast(I32), 0)
         for r in range(ROWS):
             nc.sync.dma_start(
                 wc_sc[r:P:32, :, :].bitcast(I32),
                 wc_scales.rearrange("g (q r) n -> r q g n", r=ROWS)[r].bitcast(I32),
             )
-        gather_v_words(1, 0, I_PASSES - 1, "v_second")
-        v2_codes = [keep.tile([P, S2], U32, name=f"v2_codes{a}", align_bytes=64) for a in range(K_PASSES)]
+        gather_v_words(1, 0, I_PASSES - 1, keep.tile([P, I_PASSES - 1, PACK, P], U32, name="v_codes1", align_bytes=64))
         for a in range(K_PASSES):
-            nc.vector.tensor_copy(v2_codes[a][:], v2_win[a][:].indirect(idx2[:]))
-        wc_codes = keep.tile([P, I_PASSES, 2 * N], U8, name="wc_codes", tag="v2_win0", align_bytes=64)
-        nc.sync.dma_start(wc_codes[:].bitcast(I32), wc_words.rearrange("g p b -> p g b").bitcast(I32))
-        gather_v_words(1, I_PASSES - 1, I_PASSES, "v2_win1")
+            for u in range(2):
+                nc.vector.tensor_copy(
+                    v2_codes[a][:, u * HALF : (u + 1) * HALF],
+                    v2_win[a][:].indirect(idx2[:, u * HALF // 16 : (u + 1) * HALF // 16]),
+                )
+            if a == 0:
+                v_last = keep.tile([P, 1, PACK, P], U32, name="v_last", tag="v2_win0", align_bytes=64)
+                gather_v_words(1, I_PASSES - 1, I_PASSES, v_last)
 
         h_codes = [keep.tile([P, S2], U32, name=f"h_codes{g}", align_bytes=64) for g in range(I_PASSES)]
         h_sc = [keep.tile([P, S2], U8, name=f"h_sc{g}", align_bytes=64) for g in range(I_PASSES)]
@@ -133,29 +138,45 @@ def tile_list_cauchy_voxel_pooling_kernel(
         def bank(half, b):
             return psum.tile([P, 512], F32, name=f"bank{half}{b}", tag=f"bank{half}{b}")
 
+        def x_pass(out_ap, g, t, a, cols, start, stop):
+            nc.tensor.matmul_mx(
+                out=out_ap,
+                lhsT=v_codes[a, g][:, t, :].bitcast(FP8X4),
+                lhsT_scale=sc_mm[a][:, (g * PACK + t) * P : (g * PACK + t + 1) * P],
+                rhs=v2_codes[a][:, cols].bitcast(FP8X4),
+                rhs_scale=sc_mm[a][:, S + cols.start : S + cols.stop],
+                start=start,
+                stop=stop,
+            )
+
         def x_products(g):
             banks = [bank(g % 2, t) for t in range(PACK)]
-            if g == 0:
-                order = [(a, t) for a in range(K_PASSES) for t in range(PACK)]
-            else:
-                order = [(a, t) for t in range(PACK) for a in reversed(range(K_PASSES))]
-            opened = set()
-            for a, t in order:
-                nc.tensor.matmul_mx(
-                    out=banks[t][:],
-                    lhsT=v_codes[a, g][:, t, :].bitcast(FP8X4),
-                    lhsT_scale=sc_mm[ROWS * a :, (g * PACK + t) * P : (g * PACK + t + 1) * P],
-                    rhs=v2_codes[a][:].bitcast(FP8X4),
-                    rhs_scale=sc_mm[ROWS * a :, S : S + S2],
-                    start=(t not in opened),
-                    stop=(t in opened),
+            for t in range(PACK):
+                for a in reversed(range(K_PASSES)):
+                    x_pass(banks[t][:], g, t, a, slice(0, S2), a == 1, a == 0)
+            return banks
+
+        def x_first():
+            banks = [bank(0, n) for n in range(PACK)]
+            order = [(u, a, e, s) for a in range(K_PASSES) for u in range(2) for e in range(2) for s in range(2)]
+            for u, a, e, s in order:
+                x_pass(
+                    banks[2 * u + e][:, s * HALF : (s + 1) * HALF],
+                    0,
+                    2 * e + s,
+                    a,
+                    slice(u * HALF, (u + 1) * HALF),
+                    (a, s) == (0, 0),
+                    (a, s) == (1, 1),
                 )
-                opened.add(t)
             return banks
 
         def round_wf(copy, g, lo, hi, tag, bufs):
             wf_b = work.tile([P, hi - lo, PACK], BF16, name=f"wf_b{g}_{lo}", tag=tag, bufs=bufs, align_bytes=64)
-            copy(wf_b[:], wf_raw[g][:, :, lo:hi].rearrange("p t n -> p n t"))
+            copy(
+                wf_b[:].rearrange("p (c i) t -> p c t i", i=4),
+                wf_raw[g][:, :, lo:hi].rearrange("p t (c i) -> p c t i", i=4),
+            )
             return wf_b
 
         def quantize(codes, scales, src):
@@ -176,7 +197,15 @@ def tile_list_cauchy_voxel_pooling_kernel(
                     t = step - 1
                     nc.scalar.activation(rs[:, t, :], sq[t][:], ACT.Abs_reciprocal_sqrt, bias=1.0)
                     d_col = d_sb[:, g, t : t + 1]
-                    if t < PACK - 1:
+                    if g == 0:
+                        u, e = divmod(t, 2)
+                        for s in range(2):
+                            r = rs[:, t, s * HALF : (s + 1) * HALF]
+                            slot = 2 * e + s
+                            nc.vector.scalar_tensor_tensor(
+                                hp[:, u, slot, :], r, d_sb[:, g, slot : slot + 1], r, ALU.mult, ALU.mult
+                            )
+                    elif t < PACK - 1:
                         r = rs[:, t, :].rearrange("p (u j) -> p u j", u=2)
                         nc.vector.scalar_tensor_tensor(hp[:, :, t, :], r, d_col, r, ALU.mult, ALU.mult)
                     else:
@@ -188,12 +217,14 @@ def tile_list_cauchy_voxel_pooling_kernel(
         def finish_h(g, hp):
             hb = [work.tile([P, HALF, PACK], BF16, name=f"hb{u}", align_bytes=64) for u in range(2)]
             for u in range(2):
-                nc.vector.tensor_copy(hb[u][:], hp[:, u].rearrange("p t j -> p j t"))
+                nc.vector.tensor_copy(
+                    hb[u][:].rearrange("p (c i) t -> p c t i", i=4), hp[:, u].rearrange("p t (c i) -> p c t i", i=4)
+                )
             for u in range(2):
                 cols = slice(u * HALF, (u + 1) * HALF)
                 quantize(h_codes[g][:, cols], h_sc[g][:, cols], hb[u])
 
-        x0 = x_products(0)
+        x0 = x_first()
         x1 = x_products(1)
         w0 = round_wf(nc.vector.tensor_copy, 0, 0, N, "wf_v", 2)
         hp = weights(0, x0)

@@ -25,6 +25,7 @@ N_TILES = N // P
 ROWS = 4
 SC_BASE = 96
 SQ_BUFS = 3
+TINY = 2.0**-100
 HALF = S2 // 2
 LIST_COLS = PASS // 16
 
@@ -54,10 +55,6 @@ def tile_list_cauchy_voxel_pooling_kernel(
         for a in range(K_PASSES):
             nc.gpsimd.memset(sc_mm[a][:].bitcast(I32), 0)
 
-        warm_in = keep.tile([P, 1], F32, name="warm_in")
-        warm_out = keep.tile([P, 1], F32, name="warm_out")
-        nc.vector.memset(warm_in[:], 1.0)
-        nc.scalar.activation(warm_out[:], warm_in[:], ACT.Abs_reciprocal_sqrt)
 
         def load_words(win, words):
             nc.sync.dma_start(win[:].bitcast(I32), words.rearrange("p t i -> p (t i)").bitcast(I32))
@@ -73,6 +70,17 @@ def tile_list_cauchy_voxel_pooling_kernel(
         load_words(v_win[1], tab_words[1])
         load_words(v2_win[0], tab2_words[0])
         load_words(v2_win[1], tab2_words[1])
+
+        last = I_PASSES - 1
+        d_root = keep.tile([P, PACK], F32, name="d_root")
+        d_inv = keep.tile([P, PACK], F32, name="d_inv")
+        sign = keep.tile([P, PACK], BF16, name="sign")
+        d_sign = keep.tile([P, HALF, PACK], BF16, name="d_sign")
+        nc.scalar.activation(d_root[:], d_sb[:, last, :], ACT.Abs_reciprocal_sqrt, bias=TINY)
+        nc.scalar.activation(d_inv[:], d_root[:], ACT.Square)
+        for t in range(PACK):
+            nc.scalar.activation(sign[:, t : t + 1], d_sb[:, last, t : t + 1], ACT.Copy, scale=d_inv[:, t : t + 1])
+        nc.scalar.copy(d_sign[:], sign[:].unsqueeze(1).to_broadcast([P, HALF, PACK]))
 
         v_sc_list = keep.tile([P, S], U8, name="v_sc_list", tag="v_first", align_bytes=64)
         v2_sc_list = keep.tile([P, S2], U8, name="v2_sc_list", align_bytes=64)
@@ -126,8 +134,8 @@ def tile_list_cauchy_voxel_pooling_kernel(
                     v2_codes[a][:, u * HALF : (u + 1) * HALF],
                     v2_win[a][:].indirect(idx2[:, u * HALF // 16 : (u + 1) * HALF // 16]),
                 )
-            if a == 0:
-                v_last = keep.tile([P, 1, PACK, P], U32, name="v_last", tag="v2_win0", align_bytes=64)
+            if a == 1:
+                v_last = keep.tile([P, 1, PACK, P], U32, name="v_last", tag="v2_win1", align_bytes=64)
                 gather_v_words(1, I_PASSES - 1, I_PASSES, v_last)
 
         h_codes = [keep.tile([P, S2], U32, name=f"h_codes{g}", align_bytes=64) for g in range(I_PASSES)]
@@ -171,6 +179,20 @@ def tile_list_cauchy_voxel_pooling_kernel(
                 )
             return banks
 
+        def x_last():
+            banks = [bank(0, n) for n in range(PACK)]
+            for n in range(PACK):
+                u, e = divmod(n, 2)
+                for s in range(2):
+                    for a in range(K_PASSES):
+                        x_pass(
+                            banks[n][:, s * HALF : (s + 1) * HALF], last, 2 * e + s, a, half_cols(u), a == 0, a == 1
+                        )
+            return banks
+
+        def half_cols(u):
+            return slice(u * HALF, (u + 1) * HALF)
+
         def round_wf(copy, g, lo, hi, tag, bufs):
             wf_b = work.tile([P, hi - lo, PACK], BF16, name=f"wf_b{g}_{lo}", tag=tag, bufs=bufs, align_bytes=64)
             copy(
@@ -185,102 +207,145 @@ def tile_list_cauchy_voxel_pooling_kernel(
         def quantize_wf(g, lo, hi, wf_b):
             quantize(wf_codes[g][:, lo:hi], wf_sc[g][:, lo:hi], wf_b)
 
-        def weights(g, banks):
+        def roots(banks, root_of, after):
             rs = work.tile([P, PACK, S2], F32, name="rs")
-            hp = work.tile([P, 2, PACK, HALF], BF16, name="hp")
             sq = []
             for step in range(PACK + 1):
                 if step < PACK:
                     sq.append(work.tile([P, S2], F32, name="sq", tag="sq", bufs=SQ_BUFS, align_bytes=64))
                     nc.scalar.activation(sq[step][:], banks[step][:], ACT.Square)
                 if step > 0:
-                    t = step - 1
-                    nc.scalar.activation(rs[:, t, :], sq[t][:], ACT.Abs_reciprocal_sqrt, bias=1.0)
-                    d_col = d_sb[:, g, t : t + 1]
-                    if g == 0:
-                        u, e = divmod(t, 2)
-                        for s in range(2):
-                            r = rs[:, t, s * HALF : (s + 1) * HALF]
-                            slot = 2 * e + s
-                            nc.vector.scalar_tensor_tensor(
-                                hp[:, u, slot, :], r, d_sb[:, g, slot : slot + 1], r, ALU.mult, ALU.mult
-                            )
-                    elif t < PACK - 1:
-                        r = rs[:, t, :].rearrange("p (u j) -> p u j", u=2)
-                        nc.vector.scalar_tensor_tensor(hp[:, :, t, :], r, d_col, r, ALU.mult, ALU.mult)
-                    else:
-                        for u in range(2):
-                            r = rs[:, t, u * HALF : (u + 1) * HALF]
-                            nc.vector.scalar_tensor_tensor(hp[:, u, t, :], r, d_col, r, ALU.mult, ALU.mult)
-            return hp
+                    root_of(rs, sq[step - 1], step - 1)
+                    after(rs, step - 1)
+            return rs
+
+        def plain_root(rs, sq, n):
+            nc.scalar.activation(rs[:, n, :], sq[:], ACT.Abs_reciprocal_sqrt, bias=1.0)
+
+        def weigh(out_ap, r, g, t):
+            nc.vector.scalar_tensor_tensor(out_ap, r, d_sb[:, g, t : t + 1], r, ALU.mult, ALU.mult)
+
+        def weigh_pair(hp, rs, g, n):
+            u, e = divmod(n, 2)
+            for s in range(2):
+                weigh(hp[:, u, 2 * e + s, :], rs[:, n, half_cols(s)], g, 2 * e + s)
+
+        def interleave(hp, u):
+            hb = work.tile([P, HALF, PACK], BF16, name=f"hb{u}", align_bytes=64)
+            nc.vector.tensor_copy(
+                hb[:].rearrange("p (c i) t -> p c t i", i=4), hp[:, u].rearrange("p t (c i) -> p c t i", i=4)
+            )
+            return hb
+
+        def quantize_h(g, u, hb):
+            quantize(h_codes[g][:, half_cols(u)], h_sc[g][:, half_cols(u)], hb)
 
         def finish_h(g, hp):
-            hb = [work.tile([P, HALF, PACK], BF16, name=f"hb{u}", align_bytes=64) for u in range(2)]
+            hb = [interleave(hp, u) for u in range(2)]
             for u in range(2):
-                nc.vector.tensor_copy(
-                    hb[u][:].rearrange("p (c i) t -> p c t i", i=4), hp[:, u].rearrange("p t (c i) -> p c t i", i=4)
-                )
-            for u in range(2):
-                cols = slice(u * HALF, (u + 1) * HALF)
-                quantize(h_codes[g][:, cols], h_sc[g][:, cols], hb[u])
+                quantize_h(g, u, hb[u])
 
         x0 = x_first()
         x1 = x_products(1)
         w0 = round_wf(nc.vector.tensor_copy, 0, 0, N, "wf_v", 2)
-        hp = weights(0, x0)
+        hp0 = work.tile([P, 2, PACK, HALF], BF16, name="hp")
+        roots(x0, plain_root, lambda rs, n: weigh_pair(hp0, rs, 0, n))
         quantize_wf(0, 0, N, w0)
-        finish_h(0, hp)
-        w1 = round_wf(nc.vector.tensor_copy, 1, 0, N // 2, "wf_v", 2)
-        x2 = x_products(2)
-        hp = weights(1, x1)
-        quantize_wf(1, 0, N // 2, w1)
-        finish_h(1, hp)
-        c_banks = [bank(1, b) for b in range(N_TILES)]
+        finish_h(0, hp0)
+        w1 = round_wf(nc.vector.tensor_copy, 1, 0, N, "wf_v", 2)
+        x2 = x_last()
+        hp1 = work.tile([P, 2, PACK, HALF], BF16, name="hp")
+        roots(
+            x1,
+            plain_root,
+            lambda rs, t: weigh(hp1[:, :, t, :], rs[:, t, :].rearrange("p (u j) -> p u j", u=2), 1, t),
+        )
+        quantize_wf(1, 0, N, w1)
+        w2 = round_wf(nc.vector.tensor_copy, last, 0, N, "wf_v", 2)
+        finish_h(1, hp1)
+        quantize_wf(last, 0, N, w2)
 
-        def c_pass(g, b):
-            nc.tensor.matmul_mx(
-                out=c_banks[b][:],
-                lhsT=wc_codes[:, g, 2 * P * b : 2 * P * (b + 1)].bitcast(FP4X4),
-                lhsT_scale=wc_sc[:, g, P * b : P * (b + 1)],
-                rhs=h_codes[g][:].bitcast(FP8X4),
-                rhs_scale=h_sc[g][:],
-                start=(g == 0),
-                stop=(g == I_PASSES - 1),
-            )
+        c_banks, f_banks = {}, {}
 
-        def f_pass(g, b):
-            nc.tensor.matmul_mx(
-                out=f_banks[b][:],
-                lhsT=wf_codes[g][:, P * b : P * (b + 1)].bitcast(FP8X4),
-                lhsT_scale=wf_sc[g][:, P * b : P * (b + 1)],
-                rhs=h_codes[g][:].bitcast(FP8X4),
-                rhs_scale=h_sc[g][:],
-                start=(g == 0),
-                stop=(g == I_PASSES - 1),
-            )
+        def c_passes(g, u, k):
+            for e in range(2):
+                b = 2 * k + e
+                for s in range(2):
+                    lo = u * HALF + s * P
+                    nc.tensor.matmul_mx(
+                        out=c_banks[u, k][:, e * HALF + s * P : e * HALF + (s + 1) * P],
+                        lhsT=wc_codes[:, g, 2 * P * b : 2 * P * (b + 1)].bitcast(FP4X4),
+                        lhsT_scale=wc_sc[:, g, P * b : P * (b + 1)],
+                        rhs=h_codes[g][:, lo : lo + P].bitcast(FP8X4),
+                        rhs_scale=h_sc[g][:, lo : lo + P],
+                        start=(g == 0 and e == 0 and s == 0),
+                        stop=(g == I_PASSES - 1 and e == 1 and s == 1),
+                    )
 
-        for g in range(I_PASSES - 1):
-            for b in range(N_TILES):
-                c_pass(g, b)
-        hp = weights(2, x2)
-        w1 = round_wf(nc.scalar.copy, 1, N // 2, N, "sq", SQ_BUFS)
-        w2 = round_wf(nc.scalar.copy, 2, 0, N, "sq", SQ_BUFS)
-        quantize_wf(1, N // 2, N, w1)
-        finish_h(2, hp)
-        quantize_wf(2, 0, N, w2)
-        f_banks = [bank(0, b) for b in range(N_TILES)]
-        for g in range(I_PASSES - 1):
-            for b in range(N_TILES):
-                f_pass(g, b)
-        for b in range(N_TILES):
-            c_pass(I_PASSES - 1, b)
-            f_pass(I_PASSES - 1, b)
-            c_sb = keep.tile([P, S2], F32, name=f"c_sb{b}")
-            res = keep.tile([P, S2], F32, name=f"res{b}")
-            pieces = 2 if b in (0, N_TILES - 1) else 1
-            width = S2 // pieces
-            for u in range(pieces):
-                cols = slice(u * width, (u + 1) * width)
-                nc.scalar.copy(c_sb[:, cols], c_banks[b][:, cols])
-                nc.vector.tensor_tensor(res[:, cols], f_banks[b][:, cols], c_sb[:, cols], ALU.max)
-                nc.sync.dma_start(out[P * b : P * (b + 1), cols], res[:, cols])
+        def f_passes(g, u, k):
+            for e in range(2):
+                b = 2 * k + e
+                nc.tensor.matmul_mx(
+                    out=f_banks[u, k][:, e * HALF : (e + 1) * HALF],
+                    lhsT=wf_codes[g][:, P * b : P * (b + 1)].bitcast(FP8X4),
+                    lhsT_scale=wf_sc[g][:, P * b : P * (b + 1)],
+                    rhs=h_codes[g][:, half_cols(u)].bitcast(FP8X4),
+                    rhs_scale=h_sc[g][:, half_cols(u)],
+                    start=(g == 0 and e == 0),
+                    stop=(g == I_PASSES - 1 and e == 1),
+                )
+
+        def early_passes(passes, banks, u, first_bank):
+            for k in range(2):
+                banks[u, k] = bank(1 - u, first_bank + k)
+                for g in range(I_PASSES - 1):
+                    passes(g, u, k)
+
+        def last_passes(u):
+            for k in range(2):
+                c_passes(I_PASSES - 1, u, k)
+                f_passes(I_PASSES - 1, u, k)
+
+        def finish(u):
+            for k in range(2):
+                c_sb = keep.tile([P, 2, HALF], F32, name=f"c_sb{u}{k}")
+                res = keep.tile([P, 2, HALF], F32, name=f"res{u}{k}")
+                pieces = [slice(0, 1), slice(1, 2)] if u == 1 else [slice(0, 2)]
+                for e in pieces:
+                    nc.scalar.copy(c_sb[:, e, :], c_banks[u, k][:].rearrange("p (e j) -> p e j", e=2)[:, e, :])
+                    nc.vector.tensor_tensor(
+                        res[:, e, :], f_banks[u, k][:].rearrange("p (e j) -> p e j", e=2)[:, e, :], c_sb[:, e, :], ALU.max
+                    )
+                    rows = out[2 * P * k : 2 * P * (k + 1), half_cols(u)].rearrange("(e p) j -> p e j", p=P)
+                    nc.sync.dma_start(rows[:, e, :], res[:, e, :])
+
+        early_passes(c_passes, c_banks, 0, 0)
+        early_passes(f_passes, f_banks, 0, 2)
+
+        def scaled_root(rs, sq, n):
+            for s in range(2):
+                t = 2 * (n % 2) + s
+                inv = d_inv[:, t : t + 1]
+                nc.scalar.activation(
+                    rs[:, n, half_cols(s)], sq[:, half_cols(s)], ACT.Abs_reciprocal_sqrt, bias=inv, scale=inv
+                )
+
+        def last_after(rs, n):
+            u, e = divmod(n, 2)
+            if e == 0:
+                early_passes((c_passes, f_passes)[u], (c_banks, f_banks)[u], 1, n)
+            else:
+                size = work.tile([P, HALF, PACK], BF16, name="size")
+                nc.scalar.activation(
+                    size[:].rearrange("p (c i) t -> p c t i", i=4),
+                    rs[:, 2 * u : 2 * u + 2, :].rearrange("p e (s c i) -> p c (e s) i", s=2, i=4),
+                    ACT.Square,
+                )
+                hb = work.tile([P, HALF, PACK], BF16, name=f"hb{u}", align_bytes=64)
+                nc.vector.tensor_tensor(hb[:], size[:], d_sign[:], ALU.mult)
+                quantize_h(last, u, hb)
+
+        roots(x2, scaled_root, last_after)
+        for u in range(2):
+            last_passes(u)
+            finish(u)

@@ -112,11 +112,13 @@ def tile_list_cauchy_voxel_pooling_kernel(
         gather_v_words(0, 0, I_PASSES, keep.tile([P, I_PASSES, PACK, P], U32, name="v_codes0", tag="v_first", align_bytes=64))
         v2_codes = [keep.tile([P, S2], U32, name=f"v2_codes{a}", align_bytes=64) for a in range(K_PASSES)]
         wf_rows = reuse.tile([P, I_PASSES * PACK * N], F32, name="wf_rows", offset=I_PASSES * 3 * N)
-        wf_raw = [wf_rows[:, g * PACK * N : (g + 1) * PACK * N].rearrange("p (t n) -> p t n", t=PACK) for g in range(I_PASSES)]
-        for g in range(I_PASSES):
+        wf_pieces = [(0, 0, N // 2), (0, N // 2, N), (1, 0, N), (2, 0, N)]
+        wf_raw = {}
+        for g, lo, hi in wf_pieces:
+            first = PACK * (g * N + lo)
+            wf_raw[g, lo] = wf_rows[:, first : first + PACK * (hi - lo)].rearrange("p (t n) -> p t n", t=PACK)
             nc.sync.dma_start(
-                wf_rows[:, g * PACK * N : (g + 1) * PACK * N],
-                wf[g * PASS : (g + 1) * PASS, :].rearrange("(p t) n -> p (t n)", t=PACK),
+                wf_raw[g, lo], wf[g * PASS : (g + 1) * PASS, lo:hi].rearrange("(p t) n -> p t n", t=PACK)
             )
         wc_codes = reuse.tile([P, I_PASSES, 2 * N], U8, name="wc_codes", offset=0, align_bytes=64)
         nc.sync.dma_start(wc_codes[:].bitcast(I32), wc_words.rearrange("g p b -> p g b").bitcast(I32))
@@ -134,8 +136,8 @@ def tile_list_cauchy_voxel_pooling_kernel(
                     v2_codes[a][:, u * HALF : (u + 1) * HALF],
                     v2_win[a][:].indirect(idx2[:, u * HALF // 16 : (u + 1) * HALF // 16]),
                 )
-            if a == 1:
-                v_last = keep.tile([P, 1, PACK, P], U32, name="v_last", tag="v2_win1", align_bytes=64)
+            if a == 0:
+                v_last = keep.tile([P, 1, PACK, P], U32, name="v_last", tag="v2_win0", align_bytes=64)
                 gather_v_words(1, I_PASSES - 1, I_PASSES, v_last)
 
         h_codes = [keep.tile([P, S2], U32, name=f"h_codes{g}", align_bytes=64) for g in range(I_PASSES)]
@@ -197,7 +199,7 @@ def tile_list_cauchy_voxel_pooling_kernel(
             wf_b = work.tile([P, hi - lo, PACK], BF16, name=f"wf_b{g}_{lo}", tag=tag, bufs=bufs, align_bytes=64)
             copy(
                 wf_b[:].rearrange("p (c i) t -> p c t i", i=4),
-                wf_raw[g][:, :, lo:hi].rearrange("p t (c i) -> p c t i", i=4),
+                wf_raw[g, lo].rearrange("p t (c i) -> p c t i", i=4),
             )
             return wf_b
 
@@ -247,10 +249,11 @@ def tile_list_cauchy_voxel_pooling_kernel(
 
         x0 = x_first()
         x1 = x_products(1)
-        w0 = round_wf(nc.vector.tensor_copy, 0, 0, N, "wf_v", 2)
+        w0 = [round_wf(nc.vector.tensor_copy, 0, lo, lo + N // 2, "wf_v", 2) for lo in (0, N // 2)]
         hp0 = work.tile([P, 2, PACK, HALF], BF16, name="hp")
         roots(x0, plain_root, lambda rs, n: weigh_pair(hp0, rs, 0, n))
-        quantize_wf(0, 0, N, w0)
+        for u in range(2):
+            quantize_wf(0, u * N // 2, (u + 1) * N // 2, w0[u])
         finish_h(0, hp0)
         w1 = round_wf(nc.vector.tensor_copy, 1, 0, N, "wf_v", 2)
         x2 = x_last()

@@ -43,17 +43,16 @@ def tile_list_cauchy_voxel_pooling_kernel(
         idx = keep.tile([P, S // 16], U16, name="idx")
         idx2 = keep.tile([P, S2 // 16], U16, name="idx2")
         v_win = [reuse.tile([P, T], U32, name="v_win0", offset=0), keep.tile([P, T], U32, name="v_win1")]
-        v2_win = [keep.tile([P, T2], U32, name=f"v2_win{a}", tag=f"v2_win{a}", align_bytes=64) for a in range(K_PASSES)]
+        v2_win = [keep.tile([P, T2], U32, name=f"v2_win{a}", tag="v2_win", align_bytes=64) for a in range(1)]
         vs_win = keep.tile([P, T], U8, name="vs_win")
         v2s_win = keep.tile([P, T2], U8, name="v2s_win")
-        sc_mm = [keep.tile([P, S + S2], U8, name=f"sc_mm{a}", align_bytes=64) for a in range(K_PASSES)]
+        sc_mm = keep.tile([P, S + S2], U8, name="sc_mm", align_bytes=64)
         d_sb = keep.tile([P, I_PASSES, PACK], F32, name="d_sb")
 
         for win in (vs_win, v2s_win):
             nc.vector.memset(win[0:SC_BASE, :].bitcast(I32), 0)
-        nc.gpsimd.dma_start(d_sb[:], dens.rearrange("(g p t) -> p g t", p=P, t=PACK))
-        for a in range(K_PASSES):
-            nc.gpsimd.memset(sc_mm[a][:].bitcast(I32), 0)
+        nc.scalar.dma_start(d_sb[:], dens.rearrange("(g p t) -> p g t", p=P, t=PACK))
+        nc.gpsimd.memset(sc_mm[:].bitcast(I32), 0)
 
 
         def load_words(win, words):
@@ -66,21 +65,19 @@ def tile_list_cauchy_voxel_pooling_kernel(
         load_scales(vs_win, tab_scales)
         nc.sync.dma_start(idx2[:], offs2)
         load_scales(v2s_win, tab2_scales)
+        load_words(v2_win[0], tab2_words[0])
         load_words(v_win[0], tab_words[0])
         load_words(v_win[1], tab_words[1])
-        load_words(v2_win[0], tab2_words[0])
-        load_words(v2_win[1], tab2_words[1])
 
         last = I_PASSES - 1
-        d_root = keep.tile([P, PACK], F32, name="d_root")
-        d_inv = keep.tile([P, PACK], F32, name="d_inv")
-        sign = keep.tile([P, PACK], BF16, name="sign")
-        d_sign = keep.tile([P, HALF, PACK], BF16, name="d_sign")
-        nc.scalar.activation(d_root[:], d_sb[:, last, :], ACT.Abs_reciprocal_sqrt, bias=TINY)
-        nc.scalar.activation(d_inv[:], d_root[:], ACT.Square)
-        for t in range(PACK):
-            nc.scalar.activation(sign[:, t : t + 1], d_sb[:, last, t : t + 1], ACT.Copy, scale=d_inv[:, t : t + 1])
-        nc.scalar.copy(d_sign[:], sign[:].unsqueeze(1).to_broadcast([P, HALF, PACK]))
+        d_root = keep.tile([P, I_PASSES, PACK], F32, name="d_root")
+        d_inv = keep.tile([P, I_PASSES, PACK], F32, name="d_inv")
+        sign = keep.tile([P, I_PASSES, PACK], F32, name="sign")
+        nc.scalar.activation(d_root[:, 1:, :], d_sb[:, 1:, :], ACT.Abs_reciprocal_sqrt, bias=TINY)
+        nc.gpsimd.tensor_tensor(d_inv[:, 1:, :], d_root[:, 1:, :], d_root[:, 1:, :], ALU.mult)
+        nc.gpsimd.tensor_tensor(sign[:, 1:, :], d_sb[:, 1:, :], d_inv[:, 1:, :], ALU.mult)
+        sign_b = keep.tile([P, I_PASSES, PACK], BF16, name="sign_b")
+        nc.gpsimd.tensor_tensor(sign_b[:, 1:, :], d_sb[:, 1:, :], d_inv[:, 1:, :], ALU.mult)
 
         v_sc_list = keep.tile([P, S], U8, name="v_sc_list", tag="v_first", align_bytes=64)
         v2_sc_list = keep.tile([P, S2], U8, name="v2_sc_list", align_bytes=64)
@@ -92,10 +89,11 @@ def tile_list_cauchy_voxel_pooling_kernel(
             sc_all[:, 0:S].rearrange("p (g t m) -> p t g m", g=I_PASSES, t=PACK),
             v_sc_list[:].rearrange("p (g m t) -> p t g m", g=I_PASSES, t=PACK),
         )
+        planes = [sc_mm[ROWS * (a + 1) :, :] for a in range(K_PASSES)]
         for a in range(K_PASSES):
             for r in range(ROWS):
                 (nc.gpsimd if a == 1 and r > 1 else nc.scalar).dma_start(
-                    sc_mm[a][r:P:32, :].bitcast(I32),
+                    sc_mm[ROWS * (a + 1) + r : P : 32, :].bitcast(I32),
                     sc_all[SC_BASE + 16 * a + r : SC_BASE + 16 * (a + 1) : ROWS, :].bitcast(I32),
                 )
 
@@ -109,8 +107,14 @@ def tile_list_cauchy_voxel_pooling_kernel(
                 v_win[a][:].indirect(idx[:, lo * LIST_COLS : hi * LIST_COLS]),
             )
 
-        gather_v_words(0, 0, I_PASSES, keep.tile([P, I_PASSES, PACK, P], U32, name="v_codes0", tag="v_first", align_bytes=64))
-        v2_codes = [keep.tile([P, S2], U32, name=f"v2_codes{a}", align_bytes=64) for a in range(K_PASSES)]
+        v2_codes = [
+            keep.tile([P, S2], U32, name="v2_codes0", tag="v_first", align_bytes=64),
+            keep.tile([P, S2], U32, name="v2_codes1", align_bytes=64),
+        ]
+        nc.vector.tensor_copy(v2_codes[0][:], v2_win[0][:].indirect(idx2[:]))
+        v2_win.append(keep.tile([P, T2], U32, name="v2_win1", tag="v2_win", align_bytes=64))
+        load_words(v2_win[1], tab2_words[1])
+        gather_v_words(0, 0, I_PASSES, keep.tile([P, I_PASSES, PACK, P], U32, name="v_codes0", align_bytes=64))
         wf_rows = reuse.tile([P, I_PASSES * PACK * N], F32, name="wf_rows", offset=I_PASSES * 3 * N)
         wf_pieces = [(0, 0, N // 2), (0, N // 2, N), (1, 0, N), (2, 0, N)]
         wf_raw = {}
@@ -122,23 +126,14 @@ def tile_list_cauchy_voxel_pooling_kernel(
             )
         wc_codes = reuse.tile([P, I_PASSES, 2 * N], U8, name="wc_codes", offset=0, align_bytes=64)
         nc.sync.dma_start(wc_codes[:].bitcast(I32), wc_words.rearrange("g p b -> p g b").bitcast(I32))
-        wc_sc = reuse.tile([P, I_PASSES, N], U8, name="wc_sc", offset=I_PASSES * 2 * N, align_bytes=64)
-        nc.gpsimd.memset(wc_sc[:].rearrange("p g n -> p (g n)").bitcast(I32), 0)
-        for r in range(ROWS):
-            nc.sync.dma_start(
-                wc_sc[r:P:32, :, :].bitcast(I32),
-                wc_scales.rearrange("g (q r) n -> r q g n", r=ROWS)[r].bitcast(I32),
-            )
         gather_v_words(1, 0, I_PASSES - 1, keep.tile([P, I_PASSES - 1, PACK, P], U32, name="v_codes1", align_bytes=64))
-        for a in range(K_PASSES):
-            for u in range(2):
-                nc.vector.tensor_copy(
-                    v2_codes[a][:, u * HALF : (u + 1) * HALF],
-                    v2_win[a][:].indirect(idx2[:, u * HALF // 16 : (u + 1) * HALF // 16]),
-                )
-            if a == 0:
-                v_last = keep.tile([P, 1, PACK, P], U32, name="v_last", tag="v2_win0", align_bytes=64)
-                gather_v_words(1, I_PASSES - 1, I_PASSES, v_last)
+        for u in range(2):
+            nc.vector.tensor_copy(
+                v2_codes[1][:, u * HALF : (u + 1) * HALF],
+                v2_win[1][:].indirect(idx2[:, u * HALF // 16 : (u + 1) * HALF // 16]),
+            )
+        v_last = keep.tile([P, 1, PACK, P], U32, name="v_last", tag="v2_win", align_bytes=64)
+        gather_v_words(1, I_PASSES - 1, I_PASSES, v_last)
 
         h_codes = [keep.tile([P, S2], U32, name=f"h_codes{g}", align_bytes=64) for g in range(I_PASSES)]
         h_sc = [keep.tile([P, S2], U8, name=f"h_sc{g}", align_bytes=64) for g in range(I_PASSES)]
@@ -152,9 +147,9 @@ def tile_list_cauchy_voxel_pooling_kernel(
             nc.tensor.matmul_mx(
                 out=out_ap,
                 lhsT=v_codes[a, g][:, t, :].bitcast(FP8X4),
-                lhsT_scale=sc_mm[a][:, (g * PACK + t) * P : (g * PACK + t + 1) * P],
+                lhsT_scale=planes[a][:, (g * PACK + t) * P : (g * PACK + t + 1) * P],
                 rhs=v2_codes[a][:, cols].bitcast(FP8X4),
-                rhs_scale=sc_mm[a][:, S + cols.start : S + cols.stop],
+                rhs_scale=planes[a][:, S + cols.start : S + cols.stop],
                 start=start,
                 stop=stop,
             )
@@ -257,15 +252,35 @@ def tile_list_cauchy_voxel_pooling_kernel(
         finish_h(0, hp0)
         w1 = round_wf(nc.vector.tensor_copy, 1, 0, N, "wf_v", 2)
         x2 = x_last()
+        wc_sc = sc_mm[:, 0 : I_PASSES * N].rearrange("p (g n) -> p g n", g=I_PASSES)
+        for r in range(ROWS):
+            nc.sync.dma_start(
+                wc_sc[r:P:32, :, :].bitcast(I32),
+                wc_scales.rearrange("g (q r) n -> r q g n", r=ROWS)[r].bitcast(I32),
+            )
         hp1 = work.tile([P, 2, PACK, HALF], BF16, name="hp")
-        roots(
-            x1,
-            plain_root,
-            lambda rs, t: weigh(hp1[:, :, t, :], rs[:, t, :].rearrange("p (u j) -> p u j", u=2), 1, t),
-        )
+
+        def slot_root(rs, sq, t):
+            inv = d_inv[:, 1, t : t + 1]
+            nc.scalar.activation(rs[:, t, :], sq[:], ACT.Abs_reciprocal_sqrt, bias=inv, scale=inv)
+
+        def weigh_signed(rs, t):
+            r = rs[:, t, half_cols(0)]
+            nc.vector.scalar_tensor_tensor(hp1[:, 0, t, :], r, sign[:, 1, t : t + 1], r, ALU.mult, ALU.mult)
+
+        def square_and_sign(g, u, r_by_slot):
+            size = work.tile([P, HALF, PACK], BF16, name="size")
+            nc.scalar.activation(size[:].rearrange("p (c i) t -> p c t i", i=4), r_by_slot, ACT.Square)
+            hb = work.tile([P, HALF, PACK], BF16, name=f"hb{u}", align_bytes=64)
+            nc.vector.tensor_tensor(hb[:], size[:], sign_b[:, g, :].unsqueeze(1).to_broadcast([P, HALF, PACK]), ALU.mult)
+            quantize_h(g, u, hb)
+
+        rs1 = roots(x1, slot_root, weigh_signed)
         quantize_wf(1, 0, N, w1)
+        hb10 = interleave(hp1, 0)
         w2 = round_wf(nc.vector.tensor_copy, last, 0, N, "wf_v", 2)
-        finish_h(1, hp1)
+        quantize_h(1, 0, hb10)
+        square_and_sign(1, 1, rs1[:, :, half_cols(1)].rearrange("p t (c i) -> p c t i", i=4))
         quantize_wf(last, 0, N, w2)
 
         c_banks, f_banks = {}, {}
@@ -328,7 +343,7 @@ def tile_list_cauchy_voxel_pooling_kernel(
         def scaled_root(rs, sq, n):
             for s in range(2):
                 t = 2 * (n % 2) + s
-                inv = d_inv[:, t : t + 1]
+                inv = d_inv[:, last, t : t + 1]
                 nc.scalar.activation(
                     rs[:, n, half_cols(s)], sq[:, half_cols(s)], ACT.Abs_reciprocal_sqrt, bias=inv, scale=inv
                 )
@@ -338,15 +353,9 @@ def tile_list_cauchy_voxel_pooling_kernel(
             if e == 0:
                 early_passes((c_passes, f_passes)[u], (c_banks, f_banks)[u], 1, n)
             else:
-                size = work.tile([P, HALF, PACK], BF16, name="size")
-                nc.scalar.activation(
-                    size[:].rearrange("p (c i) t -> p c t i", i=4),
-                    rs[:, 2 * u : 2 * u + 2, :].rearrange("p e (s c i) -> p c (e s) i", s=2, i=4),
-                    ACT.Square,
+                square_and_sign(
+                    last, u, rs[:, 2 * u : 2 * u + 2, :].rearrange("p e (s c i) -> p c (e s) i", s=2, i=4)
                 )
-                hb = work.tile([P, HALF, PACK], BF16, name=f"hb{u}", align_bytes=64)
-                nc.vector.tensor_tensor(hb[:], size[:], d_sign[:], ALU.mult)
-                quantize_h(last, u, hb)
 
         roots(x2, scaled_root, last_after)
         for u in range(2):

@@ -24,6 +24,8 @@ I_PASSES = S // PASS
 N_TILES = N // P
 ROWS = 4
 SC_BASE = 96
+PLANE = (12, 4)
+EARLY_CARRIES = 6
 SQ_BUFS = 3
 TINY = 2.0**-100
 HALF = S2 // 2
@@ -74,10 +76,14 @@ def tile_list_cauchy_voxel_pooling_kernel(
         d_inv = keep.tile([P, I_PASSES, PACK], F32, name="d_inv")
         sign = keep.tile([P, I_PASSES, PACK], F32, name="sign")
         nc.scalar.activation(d_root[:, 1:, :], d_sb[:, 1:, :], ACT.Abs_reciprocal_sqrt, bias=TINY)
-        nc.gpsimd.tensor_tensor(d_inv[:, 1:, :], d_root[:, 1:, :], d_root[:, 1:, :], ALU.mult)
-        nc.gpsimd.tensor_tensor(sign[:, 1:, :], d_sb[:, 1:, :], d_inv[:, 1:, :], ALU.mult)
+        nc.scalar.activation(d_inv[:, 1:, :], d_root[:, 1:, :], ACT.Square)
+        for g in range(1, I_PASSES):
+            for t in range(PACK):
+                nc.scalar.activation(
+                    sign[:, g, t : t + 1], d_sb[:, g, t : t + 1], ACT.Copy, scale=d_inv[:, g, t : t + 1]
+                )
         sign_b = keep.tile([P, I_PASSES, PACK], BF16, name="sign_b")
-        nc.gpsimd.tensor_tensor(sign_b[:, 1:, :], d_sb[:, 1:, :], d_inv[:, 1:, :], ALU.mult)
+        nc.scalar.copy(sign_b[:, 1:, :], sign[:, 1:, :])
 
         v_sc_list = keep.tile([P, S], U8, name="v_sc_list", tag="v_first", align_bytes=64)
         v2_sc_list = keep.tile([P, S2], U8, name="v2_sc_list", align_bytes=64)
@@ -89,13 +95,19 @@ def tile_list_cauchy_voxel_pooling_kernel(
             sc_all[:, 0:S].rearrange("p (g t m) -> p t g m", g=I_PASSES, t=PACK),
             v_sc_list[:].rearrange("p (g m t) -> p t g m", g=I_PASSES, t=PACK),
         )
-        planes = [sc_mm[ROWS * (a + 1) :, :] for a in range(K_PASSES)]
-        for a in range(K_PASSES):
-            for r in range(ROWS):
-                (nc.gpsimd if a == 1 and r > 1 else nc.scalar).dma_start(
-                    sc_mm[ROWS * (a + 1) + r : P : 32, :].bitcast(I32),
-                    sc_all[SC_BASE + 16 * a + r : SC_BASE + 16 * (a + 1) : ROWS, :].bitcast(I32),
-                )
+        plane_tiles = (sc_all, sc_mm)
+        planes = [plane_tiles[a][PLANE[a] :, :] for a in range(K_PASSES)]
+
+        def carry(queue, a, q):
+            src = SC_BASE + 16 * a + ROWS * q
+            dst = 32 * q + PLANE[a]
+            queue.dma_start(
+                plane_tiles[a][dst : dst + ROWS, :].bitcast(I32), sc_all[src : src + ROWS, :].bitcast(I32)
+            )
+
+        rows = [(a, q) for a in range(K_PASSES) for q in range(4) if (a, q) != (0, 3)]
+        for a, r in rows[:EARLY_CARRIES]:
+            carry(nc.scalar, a, r)
 
         v_codes = {}
 
@@ -114,6 +126,8 @@ def tile_list_cauchy_voxel_pooling_kernel(
         nc.vector.tensor_copy(v2_codes[0][:], v2_win[0][:].indirect(idx2[:]))
         v2_win.append(keep.tile([P, T2], U32, name="v2_win1", tag="v2_win", align_bytes=64))
         load_words(v2_win[1], tab2_words[1])
+        for a, r in rows[EARLY_CARRIES:]:
+            carry(nc.sync, a, r)
         gather_v_words(0, 0, I_PASSES, keep.tile([P, I_PASSES, PACK, P], U32, name="v_codes0", align_bytes=64))
         wf_rows = reuse.tile([P, I_PASSES * PACK * N], F32, name="wf_rows", offset=I_PASSES * 3 * N)
         wf_pieces = [(0, 0, N // 2), (0, N // 2, N), (1, 0, N), (2, 0, N)]
@@ -334,8 +348,8 @@ def tile_list_cauchy_voxel_pooling_kernel(
                     nc.vector.tensor_tensor(
                         res[:, e, :], f_banks[u, k][:].rearrange("p (e j) -> p e j", e=2)[:, e, :], c_sb[:, e, :], ALU.max
                     )
-                    rows = out[2 * P * k : 2 * P * (k + 1), half_cols(u)].rearrange("(e p) j -> p e j", p=P)
-                    nc.sync.dma_start(rows[:, e, :], res[:, e, :])
+                    dst = out[2 * P * k : 2 * P * (k + 1), half_cols(u)].rearrange("(e p) j -> p e j", p=P)
+                    nc.sync.dma_start(dst[:, e, :], res[:, e, :])
 
         early_passes(c_passes, c_banks, 0, 0)
         early_passes(f_passes, f_banks, 0, 2)

@@ -24,7 +24,7 @@ I_PASSES = S // PASS
 N_TILES = N // P
 ROWS = 4
 SC_BASE = 96
-PLANE = (12, 4)
+PLANE = (8, 4)
 EARLY_CARRIES = 6
 SQ_BUFS = 3
 TINY = 2.0**-100
@@ -48,13 +48,14 @@ def tile_list_cauchy_voxel_pooling_kernel(
         v2_win = [keep.tile([P, T2], U32, name=f"v2_win{a}", tag="v2_win", align_bytes=64) for a in range(1)]
         vs_win = keep.tile([P, T], U8, name="vs_win")
         v2s_win = keep.tile([P, T2], U8, name="v2s_win")
-        sc_mm = keep.tile([P, S + S2], U8, name="sc_mm", align_bytes=64)
+        sc_mm = [keep.tile([P, S + S2], U8, name=f"sc_mm{a}", align_bytes=64) for a in range(K_PASSES)]
         d_sb = keep.tile([P, I_PASSES, PACK], F32, name="d_sb")
 
         for win in (vs_win, v2s_win):
             nc.vector.memset(win[0:SC_BASE, :].bitcast(I32), 0)
-        nc.scalar.dma_start(d_sb[:], dens.rearrange("(g p t) -> p g t", p=P, t=PACK))
-        nc.gpsimd.memset(sc_mm[:].bitcast(I32), 0)
+        nc.gpsimd.dma_start(d_sb[:], dens.rearrange("(g p t) -> p g t", p=P, t=PACK))
+        for a in range(K_PASSES):
+            nc.gpsimd.memset(sc_mm[a][:].bitcast(I32), 0)
 
 
         def load_words(win, words):
@@ -72,42 +73,37 @@ def tile_list_cauchy_voxel_pooling_kernel(
         load_words(v_win[1], tab_words[1])
 
         last = I_PASSES - 1
-        d_root = keep.tile([P, I_PASSES, PACK], F32, name="d_root")
-        d_inv = keep.tile([P, I_PASSES, PACK], F32, name="d_inv")
-        sign = keep.tile([P, I_PASSES, PACK], F32, name="sign")
-        nc.scalar.activation(d_root[:, 1:, :], d_sb[:, 1:, :], ACT.Abs_reciprocal_sqrt, bias=TINY)
-        nc.scalar.activation(d_inv[:, 1:, :], d_root[:, 1:, :], ACT.Square)
-        for g in range(1, I_PASSES):
-            for t in range(PACK):
-                nc.scalar.activation(
-                    sign[:, g, t : t + 1], d_sb[:, g, t : t + 1], ACT.Copy, scale=d_inv[:, g, t : t + 1]
-                )
-        sign_b = keep.tile([P, I_PASSES, PACK], BF16, name="sign_b")
-        nc.scalar.copy(sign_b[:, 1:, :], sign[:, 1:, :])
-
         v_sc_list = keep.tile([P, S], U8, name="v_sc_list", tag="v_first", align_bytes=64)
-        v2_sc_list = keep.tile([P, S2], U8, name="v2_sc_list", align_bytes=64)
+        v2_sc_list = keep.tile([P, S2], U8, name="v2_sc_list", tag="v2_first", align_bytes=64)
         sc_all = keep.tile([P, S + S2], U8, name="sc_all", align_bytes=64)
         nc.vector.tensor_copy(v_sc_list[:], vs_win[:].indirect(idx[:]))
         nc.vector.tensor_copy(v2_sc_list[:], v2s_win[:].indirect(idx2[:]))
-        nc.vector.tensor_copy(sc_all[:, S : S + S2].bitcast(I32), v2_sc_list[:].bitcast(I32))
         nc.vector.tensor_copy(
             sc_all[:, 0:S].rearrange("p (g t m) -> p t g m", g=I_PASSES, t=PACK),
             v_sc_list[:].rearrange("p (g m t) -> p t g m", g=I_PASSES, t=PACK),
         )
-        plane_tiles = (sc_all, sc_mm)
-        planes = [plane_tiles[a][PLANE[a] :, :] for a in range(K_PASSES)]
+        nc.vector.tensor_copy(sc_all[:, S : S + S2].bitcast(I32), v2_sc_list[:].bitcast(I32))
+        planes = [sc_mm[a][PLANE[a] :, :] for a in range(K_PASSES)]
 
-        def carry(queue, a, q):
-            src = SC_BASE + 16 * a + ROWS * q
-            dst = 32 * q + PLANE[a]
+        def carry(queue, a, r):
             queue.dma_start(
-                plane_tiles[a][dst : dst + ROWS, :].bitcast(I32), sc_all[src : src + ROWS, :].bitcast(I32)
+                sc_mm[a][PLANE[a] + r : P : 32, :].bitcast(I32),
+                sc_all[SC_BASE + 16 * a + r : SC_BASE + 16 * (a + 1) : ROWS, :].bitcast(I32),
             )
 
-        rows = [(a, q) for a in range(K_PASSES) for q in range(4) if (a, q) != (0, 3)]
+        rows = [(a, r) for a in range(K_PASSES) for r in range(ROWS)]
         for a, r in rows[:EARLY_CARRIES]:
             carry(nc.scalar, a, r)
+
+        d_root = keep.tile([P, PACK], F32, name="d_root", tag="v2_first", align_bytes=64)
+        d_inv = keep.tile([P, PACK], F32, name="d_inv")
+        sign = keep.tile([P, PACK], BF16, name="sign")
+        d_sign = keep.tile([P, HALF, PACK], BF16, name="d_sign")
+        nc.scalar.activation(d_root[:], d_sb[:, last, :], ACT.Abs_reciprocal_sqrt, bias=TINY)
+        nc.scalar.activation(d_inv[:], d_root[:], ACT.Square)
+        for t in range(PACK):
+            nc.scalar.activation(sign[:, t : t + 1], d_sb[:, last, t : t + 1], ACT.Copy, scale=d_inv[:, t : t + 1])
+        nc.scalar.copy(d_sign[:], sign[:].unsqueeze(1).to_broadcast([P, HALF, PACK]))
 
         v_codes = {}
 
@@ -140,14 +136,12 @@ def tile_list_cauchy_voxel_pooling_kernel(
             )
         wc_codes = reuse.tile([P, I_PASSES, 2 * N], U8, name="wc_codes", offset=0, align_bytes=64)
         nc.sync.dma_start(wc_codes[:].bitcast(I32), wc_words.rearrange("g p b -> p g b").bitcast(I32))
-        gather_v_words(1, 0, I_PASSES - 1, keep.tile([P, I_PASSES - 1, PACK, P], U32, name="v_codes1", align_bytes=64))
+        gather_v_words(1, 0, I_PASSES, keep.tile([P, I_PASSES, PACK, P], U32, name="v_codes1", align_bytes=64))
         for u in range(2):
             nc.vector.tensor_copy(
                 v2_codes[1][:, u * HALF : (u + 1) * HALF],
                 v2_win[1][:].indirect(idx2[:, u * HALF // 16 : (u + 1) * HALF // 16]),
             )
-        v_last = keep.tile([P, 1, PACK, P], U32, name="v_last", tag="v2_win", align_bytes=64)
-        gather_v_words(1, I_PASSES - 1, I_PASSES, v_last)
 
         h_codes = [keep.tile([P, S2], U32, name=f"h_codes{g}", align_bytes=64) for g in range(I_PASSES)]
         h_sc = [keep.tile([P, S2], U8, name=f"h_sc{g}", align_bytes=64) for g in range(I_PASSES)]
@@ -266,7 +260,7 @@ def tile_list_cauchy_voxel_pooling_kernel(
         finish_h(0, hp0)
         w1 = round_wf(nc.vector.tensor_copy, 1, 0, N, "wf_v", 2)
         x2 = x_last()
-        wc_sc = sc_mm[:, 0 : I_PASSES * N].rearrange("p (g n) -> p g n", g=I_PASSES)
+        wc_sc = sc_mm[1][:, 0 : I_PASSES * N].rearrange("p (g n) -> p g n", g=I_PASSES)
         for r in range(ROWS):
             nc.sync.dma_start(
                 wc_sc[r:P:32, :, :].bitcast(I32),
@@ -274,27 +268,21 @@ def tile_list_cauchy_voxel_pooling_kernel(
             )
         hp1 = work.tile([P, 2, PACK, HALF], BF16, name="hp")
 
-        def slot_root(rs, sq, t):
-            inv = d_inv[:, 1, t : t + 1]
-            nc.scalar.activation(rs[:, t, :], sq[:], ACT.Abs_reciprocal_sqrt, bias=inv, scale=inv)
-
-        def weigh_signed(rs, t):
-            r = rs[:, t, half_cols(0)]
-            nc.vector.scalar_tensor_tensor(hp1[:, 0, t, :], r, sign[:, 1, t : t + 1], r, ALU.mult, ALU.mult)
-
         def square_and_sign(g, u, r_by_slot):
             size = work.tile([P, HALF, PACK], BF16, name="size")
             nc.scalar.activation(size[:].rearrange("p (c i) t -> p c t i", i=4), r_by_slot, ACT.Square)
             hb = work.tile([P, HALF, PACK], BF16, name=f"hb{u}", align_bytes=64)
-            nc.vector.tensor_tensor(hb[:], size[:], sign_b[:, g, :].unsqueeze(1).to_broadcast([P, HALF, PACK]), ALU.mult)
+            nc.vector.tensor_tensor(hb[:], size[:], d_sign[:], ALU.mult)
             quantize_h(g, u, hb)
 
-        rs1 = roots(x1, slot_root, weigh_signed)
+        roots(
+            x1,
+            plain_root,
+            lambda rs, t: weigh(hp1[:, :, t, :], rs[:, t, :].rearrange("p (u j) -> p u j", u=2), 1, t),
+        )
         quantize_wf(1, 0, N, w1)
-        hb10 = interleave(hp1, 0)
         w2 = round_wf(nc.vector.tensor_copy, last, 0, N, "wf_v", 2)
-        quantize_h(1, 0, hb10)
-        square_and_sign(1, 1, rs1[:, :, half_cols(1)].rearrange("p t (c i) -> p c t i", i=4))
+        finish_h(1, hp1)
         quantize_wf(last, 0, N, w2)
 
         c_banks, f_banks = {}, {}
@@ -357,7 +345,7 @@ def tile_list_cauchy_voxel_pooling_kernel(
         def scaled_root(rs, sq, n):
             for s in range(2):
                 t = 2 * (n % 2) + s
-                inv = d_inv[:, last, t : t + 1]
+                inv = d_inv[:, t : t + 1]
                 nc.scalar.activation(
                     rs[:, n, half_cols(s)], sq[:, half_cols(s)], ACT.Abs_reciprocal_sqrt, bias=inv, scale=inv
                 )

@@ -25,7 +25,7 @@ N_TILES = N // P
 ROWS = 4
 SC_BASE = 96
 PLANE = (8, 4)
-EARLY_CARRIES = 6
+EARLY_CARRIES = 4
 SQ_BUFS = 3
 TINY = 2.0**-100
 HALF = S2 // 2
@@ -136,12 +136,14 @@ def tile_list_cauchy_voxel_pooling_kernel(
             )
         wc_codes = reuse.tile([P, I_PASSES, 2 * N], U8, name="wc_codes", offset=0, align_bytes=64)
         nc.sync.dma_start(wc_codes[:].bitcast(I32), wc_words.rearrange("g p b -> p g b").bitcast(I32))
-        gather_v_words(1, 0, I_PASSES, keep.tile([P, I_PASSES, PACK, P], U32, name="v_codes1", align_bytes=64))
+        gather_v_words(1, 0, last, keep.tile([P, last, PACK, P], U32, name="v_codes1", align_bytes=64))
         for u in range(2):
             nc.vector.tensor_copy(
                 v2_codes[1][:, u * HALF : (u + 1) * HALF],
                 v2_win[1][:].indirect(idx2[:, u * HALF // 16 : (u + 1) * HALF // 16]),
             )
+
+        gather_v_words(1, last, I_PASSES, keep.tile([P, 1, PACK, P], U32, name="v_last", tag="v2_win", align_bytes=64))
 
         h_codes = [keep.tile([P, S2], U32, name=f"h_codes{g}", align_bytes=64) for g in range(I_PASSES)]
         h_sc = [keep.tile([P, S2], U8, name=f"h_sc{g}", align_bytes=64) for g in range(I_PASSES)]

@@ -26,6 +26,7 @@ ROWS = 4
 SC_BASE = 96
 PLANE = (8, 4)
 EARLY_CARRIES = 4
+WEIGH_COLS = 128
 SQ_BUFS = 3
 TINY = 2.0**-100
 HALF = S2 // 2
@@ -97,7 +98,7 @@ def tile_list_cauchy_voxel_pooling_kernel(
 
         d_root = keep.tile([P, PACK], F32, name="d_root", tag="v2_first", align_bytes=64)
         d_inv = keep.tile([P, PACK], F32, name="d_inv")
-        sign = keep.tile([P, PACK], BF16, name="sign")
+        sign = keep.tile([P, PACK], F32, name="sign")
         d_sign = keep.tile([P, HALF, PACK], BF16, name="d_sign")
         nc.scalar.activation(d_root[:], d_sb[:, last, :], ACT.Abs_reciprocal_sqrt, bias=TINY)
         nc.scalar.activation(d_inv[:], d_root[:], ACT.Square)
@@ -352,14 +353,33 @@ def tile_list_cauchy_voxel_pooling_kernel(
                     rs[:, n, half_cols(s)], sq[:, half_cols(s)], ACT.Abs_reciprocal_sqrt, bias=inv, scale=inv
                 )
 
+        hp2 = keep.tile([P, PACK, WEIGH_COLS], BF16, name="hp2")
+
         def last_after(rs, n):
             u, e = divmod(n, 2)
+            by_slot = rs[:, 2 * u : 2 * u + 2, :].rearrange("p e (s j) -> p (e s) j", s=2)
+            if u == 1:
+                for t in (2 * e, 2 * e + 1):
+                    r = by_slot[:, t, 0:WEIGH_COLS]
+                    nc.vector.scalar_tensor_tensor(hp2[:, t, :], r, sign[:, t : t + 1], r, ALU.mult, ALU.mult)
             if e == 0:
                 early_passes((c_passes, f_passes)[u], (c_banks, f_banks)[u], 1, n)
+            elif u == 0:
+                square_and_sign(last, u, by_slot.rearrange("p t (c i) -> p c t i", i=4))
             else:
-                square_and_sign(
-                    last, u, rs[:, 2 * u : 2 * u + 2, :].rearrange("p e (s c i) -> p c (e s) i", s=2, i=4)
+                size = work.tile([P, HALF - WEIGH_COLS, PACK], BF16, name="size")
+                nc.scalar.activation(
+                    size[:].rearrange("p (c i) t -> p c t i", i=4),
+                    by_slot[:, :, WEIGH_COLS:HALF].rearrange("p t (c i) -> p c t i", i=4),
+                    ACT.Square,
                 )
+                hb = work.tile([P, HALF, PACK], BF16, name="hb1", align_bytes=64)
+                nc.vector.tensor_copy(
+                    hb[:, 0:WEIGH_COLS, :].rearrange("p (c i) t -> p c t i", i=4),
+                    hp2[:].rearrange("p t (c i) -> p c t i", i=4),
+                )
+                nc.vector.tensor_tensor(hb[:, WEIGH_COLS:HALF, :], size[:], d_sign[:, WEIGH_COLS:HALF, :], ALU.mult)
+                quantize_h(last, u, hb)
 
         roots(x2, scaled_root, last_after)
         for u in range(2):

@@ -210,10 +210,10 @@ def tile_list_cauchy_voxel_pooling_kernel(
             return wf_b
 
         def quantize(codes, scales, src):
-            nc.vector.quantize_mx(out=codes.bitcast(FP8X4), scales=scales, in_=src[:].rearrange("p c t -> p (c t)"))
+            nc.vector.quantize_mx(out=codes.bitcast(FP8X4), scales=scales, in_=src.rearrange("p c t -> p (c t)"))
 
         def quantize_wf(g, lo, hi, wf_b):
-            quantize(wf_codes[g][:, lo:hi], wf_sc[g][:, lo:hi], wf_b)
+            quantize(wf_codes[g][:, lo:hi], wf_sc[g][:, lo:hi], wf_b[:])
 
         def roots(banks, root_of, after):
             rs = work.tile([P, PACK, S2], F32, name="rs")
@@ -246,7 +246,7 @@ def tile_list_cauchy_voxel_pooling_kernel(
             return hb
 
         def quantize_h(g, u, hb):
-            quantize(h_codes[g][:, half_cols(u)], h_sc[g][:, half_cols(u)], hb)
+            quantize(h_codes[g][:, half_cols(u)], h_sc[g][:, half_cols(u)], hb[:])
 
         def finish_h(g, hp):
             hb = [interleave(hp, u) for u in range(2)]
@@ -324,13 +324,36 @@ def tile_list_cauchy_voxel_pooling_kernel(
                 for g in range(I_PASSES - 1):
                     passes(g, u, k)
 
-        def last_passes(u):
+        def quarter_passes(s):
+            cols = slice(HALF + s * P, HALF + (s + 1) * P)
             for k in range(2):
-                c_passes(I_PASSES - 1, u, k)
-                f_passes(I_PASSES - 1, u, k)
+                for banks, codes, scales, step, fmt in (
+                    (c_banks, wc_codes[:, last, :], wc_sc[:, last, :], 2, FP4X4),
+                    (f_banks, wf_codes[last][:], wf_sc[last][:], 1, FP8X4),
+                ):
+                    for e in range(2):
+                        b = 2 * k + e
+                        nc.tensor.matmul_mx(
+                            out=banks[1, k][:, e * HALF + s * P : e * HALF + (s + 1) * P],
+                            lhsT=codes[:, step * P * b : step * P * (b + 1)].bitcast(fmt),
+                            lhsT_scale=scales[:, P * b : P * (b + 1)],
+                            rhs=h_codes[last][:, cols].bitcast(FP8X4),
+                            rhs_scale=h_sc[last][:, cols],
+                            start=False,
+                            stop=(s == 1 and e == 1),
+                        )
 
-        def finish(u):
-            for k in range(2):
+        def last_passes(u):
+            if u == 0:
+                for k in range(2):
+                    c_passes(last, u, k)
+                    f_passes(last, u, k)
+            else:
+                for s in range(2):
+                    quarter_passes(s)
+
+        def finish(u, pairs):
+            for k in pairs:
                 c_sb = keep.tile([P, 2, HALF], F32, name=f"c_sb{u}{k}")
                 res = keep.tile([P, 2, HALF], F32, name=f"res{u}{k}")
                 pieces = [slice(0, 1), slice(1, 2)] if u == 1 else [slice(0, 2)]
@@ -362,6 +385,9 @@ def tile_list_cauchy_voxel_pooling_kernel(
                 for t in (2 * e, 2 * e + 1):
                     r = by_slot[:, t, 0:WEIGH_COLS]
                     nc.vector.scalar_tensor_tensor(hp2[:, t, :], r, sign[:, t : t + 1], r, ALU.mult, ALU.mult)
+            if n == 2:
+                last_passes(0)
+                finish(0, [0])
             if e == 0:
                 early_passes((c_passes, f_passes)[u], (c_banks, f_banks)[u], 1, n)
             elif u == 0:
@@ -378,10 +404,11 @@ def tile_list_cauchy_voxel_pooling_kernel(
                     hb[:, 0:WEIGH_COLS, :].rearrange("p (c i) t -> p c t i", i=4),
                     hp2[:].rearrange("p t (c i) -> p c t i", i=4),
                 )
+                quantize(h_codes[last][:, HALF : HALF + P], h_sc[last][:, HALF : HALF + P], hb[:, 0:P, :])
                 nc.vector.tensor_tensor(hb[:, WEIGH_COLS:HALF, :], size[:], d_sign[:, WEIGH_COLS:HALF, :], ALU.mult)
-                quantize_h(last, u, hb)
+                quantize(h_codes[last][:, HALF + P : S2], h_sc[last][:, HALF + P : S2], hb[:, P:HALF, :])
 
         roots(x2, scaled_root, last_after)
-        for u in range(2):
-            last_passes(u)
-            finish(u)
+        finish(0, [1])
+        last_passes(1)
+        finish(1, [0, 1])

@@ -27,6 +27,7 @@ SC_BASE = 96
 PLANE = (8, 4)
 EARLY_CARRIES = 4
 WEIGH_COLS = 128
+MID_COLS = 128
 SQ_BUFS = 3
 TINY = 2.0**-100
 HALF = S2 // 2
@@ -96,15 +97,18 @@ def tile_list_cauchy_voxel_pooling_kernel(
         for a, r in rows[:EARLY_CARRIES]:
             carry(nc.scalar, a, r)
 
-        d_root = keep.tile([P, PACK], F32, name="d_root", tag="v2_first", align_bytes=64)
-        d_inv = keep.tile([P, PACK], F32, name="d_inv")
-        sign = keep.tile([P, PACK], F32, name="sign")
-        d_sign = keep.tile([P, HALF, PACK], BF16, name="d_sign")
-        nc.scalar.activation(d_root[:], d_sb[:, last, :], ACT.Abs_reciprocal_sqrt, bias=TINY)
+        d_root = keep.tile([P, I_PASSES, PACK], F32, name="d_root", tag="v2_first", align_bytes=64)
+        d_inv = keep.tile([P, I_PASSES, PACK], F32, name="d_inv")
+        sign = keep.tile([P, I_PASSES, PACK], F32, name="sign")
+        d_sign = {1: keep.tile([P, MID_COLS, PACK], BF16, name="d_sign1"), last: keep.tile([P, HALF, PACK], BF16, name="d_sign2")}
+        nc.scalar.activation(d_root[:], d_sb[:], ACT.Abs_reciprocal_sqrt, bias=TINY)
         nc.scalar.activation(d_inv[:], d_root[:], ACT.Square)
-        for t in range(PACK):
-            nc.scalar.activation(sign[:, t : t + 1], d_sb[:, last, t : t + 1], ACT.Copy, scale=d_inv[:, t : t + 1])
-        nc.scalar.copy(d_sign[:], sign[:].unsqueeze(1).to_broadcast([P, HALF, PACK]))
+        for g, cols in ((1, MID_COLS), (last, HALF)):
+            for t in range(PACK):
+                nc.scalar.activation(
+                    sign[:, g, t : t + 1], d_sb[:, g, t : t + 1], ACT.Copy, scale=d_inv[:, g, t : t + 1]
+                )
+            nc.scalar.copy(d_sign[g][:], sign[:, g, :].unsqueeze(1).to_broadcast([P, cols, PACK]))
 
         v_codes = {}
 
@@ -138,11 +142,8 @@ def tile_list_cauchy_voxel_pooling_kernel(
         wc_codes = reuse.tile([P, I_PASSES, 2 * N], U8, name="wc_codes", offset=0, align_bytes=64)
         nc.sync.dma_start(wc_codes[:].bitcast(I32), wc_words.rearrange("g p b -> p g b").bitcast(I32))
         gather_v_words(1, 0, last, keep.tile([P, last, PACK, P], U32, name="v_codes1", align_bytes=64))
-        for u in range(2):
-            nc.vector.tensor_copy(
-                v2_codes[1][:, u * HALF : (u + 1) * HALF],
-                v2_win[1][:].indirect(idx2[:, u * HALF // 16 : (u + 1) * HALF // 16]),
-            )
+        for lo, hi in ((0, P), (P, HALF), (HALF, S2)):
+            nc.vector.tensor_copy(v2_codes[1][:, lo:hi], v2_win[1][:].indirect(idx2[:, lo // 16 : hi // 16]))
 
         gather_v_words(1, last, I_PASSES, keep.tile([P, 1, PACK, P], U32, name="v_last", tag="v2_win", align_bytes=64))
 
@@ -174,17 +175,23 @@ def tile_list_cauchy_voxel_pooling_kernel(
 
         def x_first():
             banks = [bank(0, n) for n in range(PACK)]
-            order = [(u, a, e, s) for a in range(K_PASSES) for u in range(2) for e in range(2) for s in range(2)]
-            for u, a, e, s in order:
-                x_pass(
-                    banks[2 * u + e][:, s * HALF : (s + 1) * HALF],
-                    0,
-                    2 * e + s,
-                    a,
-                    slice(u * HALF, (u + 1) * HALF),
-                    (a, s) == (0, 0),
-                    (a, s) == (1, 1),
-                )
+            for a in range(K_PASSES):
+                for q in range(2):
+                    for t in range(PACK):
+                        x_pass(
+                            banks[q][:, t * P : (t + 1) * P],
+                            0,
+                            t,
+                            a,
+                            slice(q * P, (q + 1) * P),
+                            (a, t) == (0, 0),
+                            (a, t) == (1, PACK - 1),
+                        )
+                for e in range(2):
+                    for s in range(2):
+                        x_pass(
+                            banks[2 + e][:, half_cols(s)], 0, 2 * e + s, a, half_cols(1), (a, s) == (0, 0), (a, s) == (1, 1)
+                        )
             return banks
 
         def x_last():
@@ -201,11 +208,12 @@ def tile_list_cauchy_voxel_pooling_kernel(
         def half_cols(u):
             return slice(u * HALF, (u + 1) * HALF)
 
-        def round_wf(copy, g, lo, hi, tag, bufs):
-            wf_b = work.tile([P, hi - lo, PACK], BF16, name=f"wf_b{g}_{lo}", tag=tag, bufs=bufs, align_bytes=64)
-            copy(
+        def round_wf(g, lo, hi):
+            wf_b = work.tile([P, hi - lo, PACK], BF16, name=f"wf_b{g}_{lo}", tag="wf_v", bufs=4, align_bytes=64)
+            first = lo if g == 0 else 0
+            nc.vector.tensor_copy(
                 wf_b[:].rearrange("p (c i) t -> p c t i", i=4),
-                wf_raw[g, lo].rearrange("p t (c i) -> p c t i", i=4),
+                wf_raw[g, first][:, :, lo - first : hi - first].rearrange("p t (c i) -> p c t i", i=4),
             )
             return wf_b
 
@@ -246,22 +254,56 @@ def tile_list_cauchy_voxel_pooling_kernel(
             return hb
 
         def quantize_h(g, u, hb):
-            quantize(h_codes[g][:, half_cols(u)], h_sc[g][:, half_cols(u)], hb[:])
+            quantize(h_codes[g][:, half_cols(u)], h_sc[g][:, half_cols(u)], hb)
 
         def finish_h(g, hp):
             hb = [interleave(hp, u) for u in range(2)]
             for u in range(2):
-                quantize_h(g, u, hb[u])
+                quantize_h(g, u, hb[u][:])
 
         x0 = x_first()
         x1 = x_products(1)
-        w0 = [round_wf(nc.vector.tensor_copy, 0, lo, lo + N // 2, "wf_v", 2) for lo in (0, N // 2)]
+        w0 = [round_wf(0, lo, lo + N // 2) for lo in (0, N // 2)]
         hp0 = work.tile([P, 2, PACK, HALF], BF16, name="hp")
-        roots(x0, plain_root, lambda rs, n: weigh_pair(hp0, rs, 0, n))
+
+        def first_root(rs, sq, n):
+            if n < 2:
+                by_slot = rs[:, 0:2, :].rearrange("p e (s j) -> p (e s) j", s=2)
+                nc.scalar.activation(
+                    by_slot[:, :, n * P : (n + 1) * P],
+                    sq[:].rearrange("p (t j) -> p t j", t=PACK),
+                    ACT.Abs_reciprocal_sqrt,
+                    bias=1.0,
+                )
+            else:
+                plain_root(rs, sq, n)
+
+        def first_after(rs, n):
+            if n < 2:
+                by_slot = rs[:, 0:2, :].rearrange("p e (s j) -> p (e s) j", s=2)
+                for t in range(PACK):
+                    weigh(hp0[:, 0, t, n * P : (n + 1) * P], by_slot[:, t, n * P : (n + 1) * P], 0, t)
+            elif n == 2:
+                weigh_pair(hp0, rs, 0, n)
+            else:
+                for q in range(2):
+                    for s in range(2):
+                        weigh(hp0[:, 1, 2 + s, q * P : (q + 1) * P], rs[:, n, s * HALF + q * P : s * HALF + (q + 1) * P], 0, 2 + s)
+
+        roots(x0, first_root, first_after)
         for u in range(2):
             quantize_wf(0, u * N // 2, (u + 1) * N // 2, w0[u])
-        finish_h(0, hp0)
-        w1 = round_wf(nc.vector.tensor_copy, 1, 0, N, "wf_v", 2)
+        for u in range(2):
+            hb0 = work.tile([P, HALF, PACK], BF16, name=f"hb{u}", align_bytes=64)
+            for q in range(2):
+                nc.vector.tensor_copy(
+                    hb0[:, q * P : (q + 1) * P, :].rearrange("p (c i) t -> p c t i", i=4),
+                    hp0[:, u, :, q * P : (q + 1) * P].rearrange("p t (c i) -> p c t i", i=4),
+                )
+            for q in range(2):
+                cols = slice(u * HALF + q * P, u * HALF + (q + 1) * P)
+                quantize(h_codes[0][:, cols], h_sc[0][:, cols], hb0[:, q * P : (q + 1) * P, :])
+        w1 = [round_wf(1, lo, lo + N // 2) for lo in (0, N // 2)]
         x2 = x_last()
         wc_sc = sc_mm[1][:, 0 : I_PASSES * N].rearrange("p (g n) -> p g n", g=I_PASSES)
         for r in range(ROWS):
@@ -269,41 +311,71 @@ def tile_list_cauchy_voxel_pooling_kernel(
                 wc_sc[r:P:32, :, :].bitcast(I32),
                 wc_scales.rearrange("g (q r) n -> r q g n", r=ROWS)[r].bitcast(I32),
             )
-        hp1 = work.tile([P, 2, PACK, HALF], BF16, name="hp")
 
         def square_and_sign(g, u, r_by_slot):
             size = work.tile([P, HALF, PACK], BF16, name="size")
-            nc.scalar.activation(size[:].rearrange("p (c i) t -> p c t i", i=4), r_by_slot, ACT.Square)
+            for q in range(2):
+                nc.scalar.activation(
+                    size[:, q * P : (q + 1) * P, :].rearrange("p (c i) t -> p c t i", i=4),
+                    r_by_slot[:, q * P // 4 : (q + 1) * P // 4],
+                    ACT.Square,
+                )
             hb = work.tile([P, HALF, PACK], BF16, name=f"hb{u}", align_bytes=64)
-            nc.vector.tensor_tensor(hb[:], size[:], d_sign[:], ALU.mult)
-            quantize_h(g, u, hb)
+            for q in range(2):
+                part = slice(q * P, (q + 1) * P)
+                nc.vector.tensor_tensor(hb[:, part, :], size[:, part, :], d_sign[last][:, part, :], ALU.mult)
+            for q in range(2):
+                cols = slice(u * HALF + q * P, u * HALF + (q + 1) * P)
+                quantize(h_codes[g][:, cols], h_sc[g][:, cols], hb[:, q * P : (q + 1) * P, :])
 
-        roots(
-            x1,
-            plain_root,
-            lambda rs, t: weigh(hp1[:, :, t, :], rs[:, t, :].rearrange("p (u j) -> p u j", u=2), 1, t),
+        def mid_root(rs, sq, t):
+            inv = d_inv[:, 1, t : t + 1]
+            nc.scalar.activation(rs[:, t, :], sq[:], ACT.Abs_reciprocal_sqrt, bias=inv, scale=inv)
+
+        mid = S2 - MID_COLS
+        hp1 = work.tile([P, PACK, mid], BF16, name="hp1", bufs=1)
+
+        def mid_after(rs, t):
+            for lo, hi in ((0, mid),) if t < PACK - 1 else ((0, HALF), (HALF, mid)):
+                r = rs[:, t, lo:hi]
+                nc.vector.scalar_tensor_tensor(hp1[:, t, lo:hi], r, sign[:, 1, t : t + 1], r, ALU.mult, ALU.mult)
+
+        rs1 = roots(x1, mid_root, mid_after)
+        size1 = work.tile([P, MID_COLS, PACK], BF16, name="size1", bufs=1)
+        nc.scalar.activation(
+            size1[:].rearrange("p (c i) t -> p c t i", i=4),
+            rs1[:, :, mid:S2].rearrange("p t (c i) -> p c t i", i=4),
+            ACT.Square,
         )
-        quantize_wf(1, 0, N, w1)
-        w2 = round_wf(nc.vector.tensor_copy, last, 0, N, "wf_v", 2)
-        finish_h(1, hp1)
-        quantize_wf(last, 0, N, w2)
+        for u in range(2):
+            quantize_wf(1, u * N // 2, (u + 1) * N // 2, w1[u])
+        w2 = [round_wf(last, lo, lo + N // 2) for lo in (0, N // 2)]
+        hb1 = work.tile([P, S2, PACK], BF16, name="hb_mid", bufs=1, align_bytes=64)
+        for lo, hi in ((0, HALF), (HALF, mid)):
+            nc.vector.tensor_copy(
+                hb1[:, lo:hi, :].rearrange("p (c i) t -> p c t i", i=4),
+                hp1[:, :, lo:hi].rearrange("p t (c i) -> p c t i", i=4),
+            )
+        nc.vector.tensor_tensor(hb1[:, mid:S2, :], size1[:], d_sign[1][:], ALU.mult)
+        quantize_h(1, 0, hb1[:, 0:HALF, :])
+        quantize_h(1, 1, hb1[:, HALF:S2, :])
+        for u in range(2):
+            quantize_wf(last, u * N // 2, (u + 1) * N // 2, w2[u])
 
         c_banks, f_banks = {}, {}
 
         def c_passes(g, u, k):
             for e in range(2):
                 b = 2 * k + e
-                for s in range(2):
-                    lo = u * HALF + s * P
-                    nc.tensor.matmul_mx(
-                        out=c_banks[u, k][:, e * HALF + s * P : e * HALF + (s + 1) * P],
-                        lhsT=wc_codes[:, g, 2 * P * b : 2 * P * (b + 1)].bitcast(FP4X4),
-                        lhsT_scale=wc_sc[:, g, P * b : P * (b + 1)],
-                        rhs=h_codes[g][:, lo : lo + P].bitcast(FP8X4),
-                        rhs_scale=h_sc[g][:, lo : lo + P],
-                        start=(g == 0 and e == 0 and s == 0),
-                        stop=(g == I_PASSES - 1 and e == 1 and s == 1),
-                    )
+                nc.tensor.matmul_mx(
+                    out=c_banks[u, k][:, e * HALF : (e + 1) * HALF],
+                    lhsT=wc_codes[:, g, 2 * P * b : 2 * P * (b + 1)].bitcast(FP4X4),
+                    lhsT_scale=wc_sc[:, g, P * b : P * (b + 1)],
+                    rhs=h_codes[g][:, half_cols(u)].bitcast(FP8X4),
+                    rhs_scale=h_sc[g][:, half_cols(u)],
+                    start=(g == 0 and e == 0),
+                    stop=(g == I_PASSES - 1 and e == 1),
+                )
 
         def f_passes(g, u, k):
             for e in range(2):
@@ -371,7 +443,7 @@ def tile_list_cauchy_voxel_pooling_kernel(
         def scaled_root(rs, sq, n):
             for s in range(2):
                 t = 2 * (n % 2) + s
-                inv = d_inv[:, t : t + 1]
+                inv = d_inv[:, last, t : t + 1]
                 nc.scalar.activation(
                     rs[:, n, half_cols(s)], sq[:, half_cols(s)], ACT.Abs_reciprocal_sqrt, bias=inv, scale=inv
                 )
@@ -384,7 +456,7 @@ def tile_list_cauchy_voxel_pooling_kernel(
             if u == 1:
                 for t in (2 * e, 2 * e + 1):
                     r = by_slot[:, t, 0:WEIGH_COLS]
-                    nc.vector.scalar_tensor_tensor(hp2[:, t, :], r, sign[:, t : t + 1], r, ALU.mult, ALU.mult)
+                    nc.vector.scalar_tensor_tensor(hp2[:, t, :], r, sign[:, last, t : t + 1], r, ALU.mult, ALU.mult)
             if n == 2:
                 last_passes(0)
                 finish(0, [0])
@@ -405,7 +477,7 @@ def tile_list_cauchy_voxel_pooling_kernel(
                     hp2[:].rearrange("p t (c i) -> p c t i", i=4),
                 )
                 quantize(h_codes[last][:, HALF : HALF + P], h_sc[last][:, HALF : HALF + P], hb[:, 0:P, :])
-                nc.vector.tensor_tensor(hb[:, WEIGH_COLS:HALF, :], size[:], d_sign[:, WEIGH_COLS:HALF, :], ALU.mult)
+                nc.vector.tensor_tensor(hb[:, WEIGH_COLS:HALF, :], size[:], d_sign[last][:, WEIGH_COLS:HALF, :], ALU.mult)
                 quantize(h_codes[last][:, HALF + P : S2], h_sc[last][:, HALF + P : S2], hb[:, P:HALF, :])
 
         roots(x2, scaled_root, last_after)

@@ -26,7 +26,6 @@ ROWS = 4
 SC_BASE = 96
 PLANE = (8, 4)
 EARLY_CARRIES = 4
-WEIGH_COLS = 128
 MID_COLS = 128
 SQ_BUFS = 3
 TINY = 2.0**-100
@@ -196,13 +195,14 @@ def tile_list_cauchy_voxel_pooling_kernel(
 
         def x_last():
             banks = [bank(0, n) for n in range(PACK)]
-            for n in range(PACK):
-                u, e = divmod(n, 2)
+            for e in range(2):
                 for s in range(2):
                     for a in range(K_PASSES):
-                        x_pass(
-                            banks[n][:, s * HALF : (s + 1) * HALF], last, 2 * e + s, a, half_cols(u), a == 0, a == 1
-                        )
+                        x_pass(banks[e][:, half_cols(s)], last, 2 * e + s, a, half_cols(0), a == 0, a == 1)
+            for q in range(2, 4):
+                for t in range(PACK):
+                    for a in range(K_PASSES):
+                        x_pass(banks[q][:, t * P : (t + 1) * P], last, t, a, slice(q * P, (q + 1) * P), a == 0, a == 1)
             return banks
 
         def half_cols(u):
@@ -314,12 +314,7 @@ def tile_list_cauchy_voxel_pooling_kernel(
 
         def square_and_sign(g, u, r_by_slot):
             size = work.tile([P, HALF, PACK], BF16, name="size")
-            for q in range(2):
-                nc.scalar.activation(
-                    size[:, q * P : (q + 1) * P, :].rearrange("p (c i) t -> p c t i", i=4),
-                    r_by_slot[:, q * P // 4 : (q + 1) * P // 4],
-                    ACT.Square,
-                )
+            nc.scalar.activation(size[:].rearrange("p (c i) t -> p c t i", i=4), r_by_slot, ACT.Square)
             hb = work.tile([P, HALF, PACK], BF16, name=f"hb{u}", align_bytes=64)
             for q in range(2):
                 part = slice(q * P, (q + 1) * P)
@@ -396,91 +391,108 @@ def tile_list_cauchy_voxel_pooling_kernel(
                 for g in range(I_PASSES - 1):
                     passes(g, u, k)
 
-        def quarter_passes(s):
-            cols = slice(HALF + s * P, HALF + (s + 1) * P)
-            for k in range(2):
-                for banks, codes, scales, step, fmt in (
-                    (c_banks, wc_codes[:, last, :], wc_sc[:, last, :], 2, FP4X4),
-                    (f_banks, wf_codes[last][:], wf_sc[last][:], 1, FP8X4),
-                ):
-                    for e in range(2):
-                        b = 2 * k + e
-                        nc.tensor.matmul_mx(
-                            out=banks[1, k][:, e * HALF + s * P : e * HALF + (s + 1) * P],
-                            lhsT=codes[:, step * P * b : step * P * (b + 1)].bitcast(fmt),
-                            lhsT_scale=scales[:, P * b : P * (b + 1)],
-                            rhs=h_codes[last][:, cols].bitcast(FP8X4),
-                            rhs_scale=h_sc[last][:, cols],
-                            start=False,
-                            stop=(s == 1 and e == 1),
-                        )
-
-        def last_passes(u):
-            if u == 0:
-                for k in range(2):
-                    c_passes(last, u, k)
-                    f_passes(last, u, k)
-            else:
-                for s in range(2):
-                    quarter_passes(s)
-
-        def finish(u, pairs):
-            for k in pairs:
-                c_sb = keep.tile([P, 2, HALF], F32, name=f"c_sb{u}{k}")
-                res = keep.tile([P, 2, HALF], F32, name=f"res{u}{k}")
-                pieces = [slice(0, 1), slice(1, 2)] if u == 1 else [slice(0, 2)]
-                for e in pieces:
-                    nc.scalar.copy(c_sb[:, e, :], c_banks[u, k][:].rearrange("p (e j) -> p e j", e=2)[:, e, :])
-                    nc.vector.tensor_tensor(
-                        res[:, e, :], f_banks[u, k][:].rearrange("p (e j) -> p e j", e=2)[:, e, :], c_sb[:, e, :], ALU.max
+        def quarter_passes(banks, q, groups):
+            cols = slice(q * P, (q + 1) * P)
+            for g in groups:
+                for b in range(N_TILES):
+                    if banks is c_banks:
+                        lhsT = wc_codes[:, g, 2 * P * b : 2 * P * (b + 1)].bitcast(FP4X4)
+                        lhsT_scale = wc_sc[:, g, P * b : P * (b + 1)]
+                    else:
+                        lhsT = wf_codes[g][:, P * b : P * (b + 1)].bitcast(FP8X4)
+                        lhsT_scale = wf_sc[g][:, P * b : P * (b + 1)]
+                    nc.tensor.matmul_mx(
+                        out=banks[q][:, b * P : (b + 1) * P],
+                        lhsT=lhsT,
+                        lhsT_scale=lhsT_scale,
+                        rhs=h_codes[g][:, cols].bitcast(FP8X4),
+                        rhs_scale=h_sc[g][:, cols],
+                        start=(g == 0 and b == 0),
+                        stop=(g == last and b == N_TILES - 1),
                     )
-                    dst = out[2 * P * k : 2 * P * (k + 1), half_cols(u)].rearrange("(e p) j -> p e j", p=P)
-                    nc.sync.dma_start(dst[:, e, :], res[:, e, :])
+
+        def store(u, k, res):
+            dst = out[2 * P * k : 2 * P * (k + 1), half_cols(u)].rearrange("(e p) j -> p e j", p=P)
+            nc.sync.dma_start(dst, res[:])
+
+        def finish_half(k):
+            c_sb = keep.tile([P, S2], F32, name=f"c_sb{k}")
+            res = keep.tile([P, 2, HALF], F32, name=f"res{k}")
+            nc.scalar.copy(c_sb[:], c_banks[0, k][:])
+            nc.vector.tensor_tensor(res[:].rearrange("p e j -> p (e j)"), f_banks[0, k][:], c_sb[:], ALU.max)
+            store(0, k, res)
+
+        res_late = [keep.tile([P, 2, HALF], F32, name=f"res_late{k}") for k in range(2)]
+
+        def finish_quarter(q, width):
+            c_sb = keep.tile([P, N_TILES, P], F32, name=f"c_quarter{q}")
+            for b in range(0, N_TILES, width):
+                tiles = slice(b, b + width)
+                k, e = divmod(b, 2)
+                nc.scalar.copy(c_sb[:, tiles, :], c_banks[q][:].rearrange("p (b j) -> p b j", j=P)[:, tiles, :])
+                nc.vector.tensor_tensor(
+                    res_late[k][:, e : e + width, (q - 2) * P : (q - 1) * P],
+                    f_banks[q][:].rearrange("p (b j) -> p b j", j=P)[:, tiles, :],
+                    c_sb[:, tiles, :],
+                    ALU.max,
+                )
+                if q == 3:
+                    nc.sync.dma_start(out[P * b : P * (b + 1), half_cols(1)], res_late[k][:, e, :])
 
         early_passes(c_passes, c_banks, 0, 0)
         early_passes(f_passes, f_banks, 0, 2)
 
-        def scaled_root(rs, sq, n):
-            for s in range(2):
-                t = 2 * (n % 2) + s
+        def last_root(rs, sq, n):
+            if n == 2:
+                plain_root(rs, sq, n)
+                return
+            width = HALF if n < 2 else P
+            for s in range(S2 // width):
+                t = 2 * n + s if n < 2 else s
                 inv = d_inv[:, last, t : t + 1]
-                nc.scalar.activation(
-                    rs[:, n, half_cols(s)], sq[:, half_cols(s)], ACT.Abs_reciprocal_sqrt, bias=inv, scale=inv
-                )
-
-        hp2 = keep.tile([P, PACK, WEIGH_COLS], BF16, name="hp2")
+                cols = slice(s * width, (s + 1) * width)
+                nc.scalar.activation(rs[:, n, cols], sq[:, cols], ACT.Abs_reciprocal_sqrt, bias=inv, scale=inv)
 
         def last_after(rs, n):
-            u, e = divmod(n, 2)
-            by_slot = rs[:, 2 * u : 2 * u + 2, :].rearrange("p e (s j) -> p (e s) j", s=2)
-            if u == 1:
-                for t in (2 * e, 2 * e + 1):
-                    r = by_slot[:, t, 0:WEIGH_COLS]
-                    nc.vector.scalar_tensor_tensor(hp2[:, t, :], r, sign[:, last, t : t + 1], r, ALU.mult, ALU.mult)
-            if n == 2:
-                last_passes(0)
-                finish(0, [0])
-            if e == 0:
-                early_passes((c_passes, f_passes)[u], (c_banks, f_banks)[u], 1, n)
-            elif u == 0:
-                square_and_sign(last, u, by_slot.rearrange("p t (c i) -> p c t i", i=4))
-            else:
-                size = work.tile([P, HALF - WEIGH_COLS, PACK], BF16, name="size")
-                nc.scalar.activation(
-                    size[:].rearrange("p (c i) t -> p c t i", i=4),
-                    by_slot[:, :, WEIGH_COLS:HALF].rearrange("p t (c i) -> p c t i", i=4),
-                    ACT.Square,
-                )
-                hb = work.tile([P, HALF, PACK], BF16, name="hb1", align_bytes=64)
+            by_four = rs[:, n, :].rearrange("p (t c i) -> p c t i", t=PACK, i=4)
+            cols = slice(n * P, (n + 1) * P)
+            if n == 0:
+                c_banks[2] = bank(0, 0)
+                quarter_passes(c_banks, 2, range(last))
+            elif n == 1:
+                f_banks[2] = bank(0, 1)
+                quarter_passes(f_banks, 2, range(last))
+                by_slot = rs[:, 0:2, :].rearrange("p e (s j) -> p (e s) j", s=2)
+                square_and_sign(last, 0, by_slot.rearrange("p t (c i) -> p c t i", i=4))
+            elif n == 2:
+                hp2 = keep.tile([P, PACK, P], BF16, name="hp2")
+                for t in range(PACK):
+                    weigh(hp2[:, t, :], rs[:, n, t * P : (t + 1) * P], last, t)
+                for k in range(2):
+                    c_passes(last, 0, k)
+                    f_passes(last, 0, k)
+                hb = keep.tile([P, P, PACK], BF16, name="hb_third", align_bytes=64)
                 nc.vector.tensor_copy(
-                    hb[:, 0:WEIGH_COLS, :].rearrange("p (c i) t -> p c t i", i=4),
-                    hp2[:].rearrange("p t (c i) -> p c t i", i=4),
+                    hb[:].rearrange("p (c i) t -> p c t i", i=4), hp2[:].rearrange("p t (c i) -> p c t i", i=4)
                 )
-                quantize(h_codes[last][:, HALF : HALF + P], h_sc[last][:, HALF : HALF + P], hb[:, 0:P, :])
-                nc.vector.tensor_tensor(hb[:, WEIGH_COLS:HALF, :], size[:], d_sign[last][:, WEIGH_COLS:HALF, :], ALU.mult)
-                quantize(h_codes[last][:, HALF + P : S2], h_sc[last][:, HALF + P : S2], hb[:, P:HALF, :])
+                quantize(h_codes[last][:, cols], h_sc[last][:, cols], hb[:])
+                c_banks[3] = bank(0, 2)
+                f_banks[3] = bank(0, 3)
+                for banks in (c_banks, f_banks):
+                    quarter_passes(banks, 3, range(last))
+                for banks in (c_banks, f_banks):
+                    quarter_passes(banks, 2, [last])
+                finish_half(0)
+            else:
+                size = keep.tile([P, P, PACK], BF16, name="size_last")
+                nc.scalar.activation(size[:].rearrange("p (c i) t -> p c t i", i=4), by_four, ACT.Square)
+                hb = keep.tile([P, P, PACK], BF16, name="hb_last", align_bytes=64)
+                nc.vector.tensor_tensor(hb[:], size[:], d_sign[last][:, 0:P, :], ALU.mult)
+                quantize(h_codes[last][:, cols], h_sc[last][:, cols], hb[:])
+                for banks in (c_banks, f_banks):
+                    quarter_passes(banks, 3, [last])
 
-        roots(x2, scaled_root, last_after)
-        finish(0, [1])
-        last_passes(1)
-        finish(1, [0, 1])
+        roots(x2, last_root, last_after)
+        finish_half(1)
+        finish_quarter(2, 2)
+        finish_quarter(3, 1)

@@ -211,10 +211,12 @@ def tile_list_cauchy_voxel_pooling_kernel(
         def round_wf(g, lo, hi):
             wf_b = work.tile([P, hi - lo, PACK], BF16, name=f"wf_b{g}_{lo}", tag="wf_v", bufs=4, align_bytes=64)
             first = lo if g == 0 else 0
-            nc.vector.tensor_copy(
-                wf_b[:].rearrange("p (c i) t -> p c t i", i=4),
-                wf_raw[g, first][:, :, lo - first : hi - first].rearrange("p t (c i) -> p c t i", i=4),
-            )
+            woven = wf_b[:].rearrange("p (c i) t -> p c t i", i=4)
+            rows_in = wf_raw[g, first][:, :, lo - first : hi - first].rearrange("p t (c i) -> p c t i", i=4)
+            if (g, lo) == (0, 0):
+                nc.gpsimd.tensor_scalar(woven, rows_in, 1.0, 0.0, ALU.mult, ALU.add)
+            else:
+                nc.vector.tensor_copy(woven, rows_in)
             return wf_b
 
         def quantize(codes, scales, src):

@@ -213,7 +213,7 @@ def tile_list_cauchy_voxel_pooling_kernel(
             first = lo if g == 0 else 0
             woven = wf_b[:].rearrange("p (c i) t -> p c t i", i=4)
             rows_in = wf_raw[g, first][:, :, lo - first : hi - first].rearrange("p t (c i) -> p c t i", i=4)
-            if (g, lo) == (0, 0):
+            if g == 0:
                 nc.gpsimd.tensor_scalar(woven, rows_in, 1.0, 0.0, ALU.mult, ALU.add)
             else:
                 nc.vector.tensor_copy(woven, rows_in)
@@ -225,13 +225,17 @@ def tile_list_cauchy_voxel_pooling_kernel(
         def quantize_wf(g, lo, hi, wf_b):
             quantize(wf_codes[g][:, lo:hi], wf_sc[g][:, lo:hi], wf_b[:])
 
-        def roots(banks, root_of, after):
+        def roots(banks, root_of, after, on_vector=()):
             rs = work.tile([P, PACK, S2], F32, name="rs")
             sq = []
             for step in range(PACK + 1):
                 if step < PACK:
                     sq.append(work.tile([P, S2], F32, name="sq", tag="sq", bufs=SQ_BUFS, align_bytes=64))
-                    nc.scalar.activation(sq[step][:], banks[step][:], ACT.Square)
+                    if step in on_vector:
+                        twice = banks[step][:].unsqueeze(2).to_broadcast([P, S2, 2])
+                        nc.vector.tensor_reduce(sq[step][:], twice, mybir.AxisListType.X, ALU.mult)
+                    else:
+                        nc.scalar.activation(sq[step][:], banks[step][:], ACT.Square)
                 if step > 0:
                     root_of(rs, sq[step - 1], step - 1)
                     after(rs, step - 1)
@@ -292,7 +296,7 @@ def tile_list_cauchy_voxel_pooling_kernel(
                     for s in range(2):
                         weigh(hp0[:, 1, 2 + s, q * P : (q + 1) * P], rs[:, n, s * HALF + q * P : s * HALF + (q + 1) * P], 0, 2 + s)
 
-        roots(x0, first_root, first_after)
+        roots(x0, first_root, first_after, (2,))
         for u in range(2):
             quantize_wf(0, u * N // 2, (u + 1) * N // 2, w0[u])
         for u in range(2):

@@ -214,7 +214,8 @@ def tile_list_cauchy_voxel_pooling_kernel(
             woven = wf_b[:].rearrange("p (c i) t -> p c t i", i=4)
             rows_in = wf_raw[g, first][:, :, lo - first : hi - first].rearrange("p t (c i) -> p c t i", i=4)
             if g == 0:
-                nc.gpsimd.tensor_scalar(woven, rows_in, 1.0, 0.0, ALU.mult, ALU.add)
+                by_column = wf_raw[g, first][:].rearrange("p t n -> p n t")
+                nc.gpsimd.tensor_scalar(wf_b[:], by_column, 1.0, 0.0, ALU.mult, ALU.add)
             else:
                 nc.vector.tensor_copy(woven, rows_in)
             return wf_b

@@ -30,6 +30,8 @@ MID_COLS = 128
 SQ_BUFS = 3
 TINY = 2.0**-100
 HALF = S2 // 2
+PAIR = 2
+FIRST_PIECES = ((0, 192), (192, 384), (384, N))
 LIST_COLS = PASS // 16
 
 
@@ -50,11 +52,9 @@ def tile_list_cauchy_voxel_pooling_kernel(
         vs_win = keep.tile([P, T], U8, name="vs_win")
         v2s_win = keep.tile([P, T2], U8, name="v2s_win")
         sc_mm = [keep.tile([P, S + S2], U8, name=f"sc_mm{a}", align_bytes=64) for a in range(K_PASSES)]
-        d_sb = keep.tile([P, I_PASSES, PACK], F32, name="d_sb")
 
         for win in (vs_win, v2s_win):
             nc.vector.memset(win[0:SC_BASE, :].bitcast(I32), 0)
-        nc.gpsimd.dma_start(d_sb[:], dens.rearrange("(g p t) -> p g t", p=P, t=PACK))
         for a in range(K_PASSES):
             nc.gpsimd.memset(sc_mm[a][:].bitcast(I32), 0)
 
@@ -96,7 +96,9 @@ def tile_list_cauchy_voxel_pooling_kernel(
         for a, r in rows[:EARLY_CARRIES]:
             carry(nc.scalar, a, r)
 
-        d_root = keep.tile([P, I_PASSES, PACK], F32, name="d_root", tag="v2_first", align_bytes=64)
+        d_sb = keep.tile([P, I_PASSES, PACK], F32, name="d_sb", tag="v2_first", align_bytes=64)
+        nc.scalar.dma_start(d_sb[:], dens.rearrange("(g p t) -> p g t", p=P, t=PACK))
+        d_root = keep.tile([P, I_PASSES, PACK], F32, name="d_root")
         d_inv = keep.tile([P, I_PASSES, PACK], F32, name="d_inv")
         sign = keep.tile([P, I_PASSES, PACK], F32, name="sign")
         d_sign = {1: keep.tile([P, MID_COLS, PACK], BF16, name="d_sign1"), last: keep.tile([P, HALF, PACK], BF16, name="d_sign2")}
@@ -130,7 +132,7 @@ def tile_list_cauchy_voxel_pooling_kernel(
             carry(nc.sync, a, r)
         gather_v_words(0, 0, I_PASSES, keep.tile([P, I_PASSES, PACK, P], U32, name="v_codes0", align_bytes=64))
         wf_rows = reuse.tile([P, I_PASSES * PACK * N], F32, name="wf_rows", offset=I_PASSES * 3 * N)
-        wf_pieces = [(0, 0, N // 2), (0, N // 2, N), (1, 0, N), (2, 0, N)]
+        wf_pieces = [(0, lo, hi) for lo, hi in FIRST_PIECES] + [(1, 0, N), (2, 0, N)]
         wf_raw = {}
         for g, lo, hi in wf_pieces:
             first = PACK * (g * N + lo)
@@ -210,15 +212,20 @@ def tile_list_cauchy_voxel_pooling_kernel(
 
         def round_wf(g, lo, hi):
             wf_b = work.tile([P, hi - lo, PACK], BF16, name=f"wf_b{g}_{lo}", tag="wf_v", bufs=4, align_bytes=64)
-            first = lo if g == 0 else 0
-            woven = wf_b[:].rearrange("p (c i) t -> p c t i", i=4)
-            rows_in = wf_raw[g, first][:, :, lo - first : hi - first].rearrange("p t (c i) -> p c t i", i=4)
-            if g == 0:
-                by_column = wf_raw[g, first][:].rearrange("p t n -> p n t")
-                nc.gpsimd.tensor_scalar(wf_b[:], by_column, 1.0, 0.0, ALU.mult, ALU.add)
-            else:
-                nc.vector.tensor_copy(woven, rows_in)
+            woven = wf_b[:].rearrange("p (c i) t -> p c t i", i=PAIR)
+            nc.vector.tensor_copy(woven, wf_raw[g, 0][:, :, lo:hi].rearrange("p t (c i) -> p c t i", i=PAIR))
             return wf_b
+
+        def round_first_wf():
+            wf_b = keep.tile([P, N, PACK], BF16, name="wf_b0", align_bytes=64)
+            for lo, hi in FIRST_PIECES:
+                woven = wf_b[:, lo:hi, :].rearrange("p (c i) t -> p c t i", i=PAIR)
+                rows_in = wf_raw[0, lo].rearrange("p t (c i) -> p c t i", i=PAIR)
+                if hi < N:
+                    nc.gpsimd.tensor_scalar(woven, rows_in, 1.0, 0.0, ALU.mult, ALU.add)
+                else:
+                    nc.vector.tensor_copy(woven, rows_in)
+            return [wf_b[:, 0 : N // 2, :], wf_b[:, N // 2 : N, :]]
 
         def quantize(codes, scales, src):
             nc.vector.quantize_mx(out=codes.bitcast(FP8X4), scales=scales, in_=src.rearrange("p c t -> p (c t)"))
@@ -270,7 +277,7 @@ def tile_list_cauchy_voxel_pooling_kernel(
 
         x0 = x_first()
         x1 = x_products(1)
-        w0 = [round_wf(0, lo, lo + N // 2) for lo in (0, N // 2)]
+        w0 = round_first_wf()
         hp0 = work.tile([P, 2, PACK, HALF], BF16, name="hp")
 
         def first_root(rs, sq, n):
@@ -321,7 +328,7 @@ def tile_list_cauchy_voxel_pooling_kernel(
 
         def square_and_sign(g, u, r_by_slot):
             size = work.tile([P, HALF, PACK], BF16, name="size")
-            nc.scalar.activation(size[:].rearrange("p (c i) t -> p c t i", i=4), r_by_slot, ACT.Square)
+            nc.scalar.activation(size[:].rearrange("p (c i) t -> p c t i", i=PAIR), r_by_slot, ACT.Square)
             hb = work.tile([P, HALF, PACK], BF16, name=f"hb{u}", align_bytes=64)
             for q in range(2):
                 part = slice(q * P, (q + 1) * P)
@@ -345,8 +352,8 @@ def tile_list_cauchy_voxel_pooling_kernel(
         rs1 = roots(x1, mid_root, mid_after)
         size1 = work.tile([P, MID_COLS, PACK], BF16, name="size1", bufs=1)
         nc.scalar.activation(
-            size1[:].rearrange("p (c i) t -> p c t i", i=4),
-            rs1[:, :, mid:S2].rearrange("p t (c i) -> p c t i", i=4),
+            size1[:].rearrange("p (c i) t -> p c t i", i=PAIR),
+            rs1[:, :, mid:S2].rearrange("p t (c i) -> p c t i", i=PAIR),
             ACT.Square,
         )
         for u in range(2):
@@ -443,7 +450,9 @@ def tile_list_cauchy_voxel_pooling_kernel(
                     c_sb[:, tiles, :],
                     ALU.max,
                 )
-                if q == 3:
+                if q == 3 and k == 0 and e == 1:
+                    store(1, 0, res_late[0])
+                elif q == 3 and k == 1:
                     nc.sync.dma_start(out[P * b : P * (b + 1), half_cols(1)], res_late[k][:, e, :])
 
         early_passes(c_passes, c_banks, 0, 0)
@@ -461,7 +470,7 @@ def tile_list_cauchy_voxel_pooling_kernel(
                 nc.scalar.activation(rs[:, n, cols], sq[:, cols], ACT.Abs_reciprocal_sqrt, bias=inv, scale=inv)
 
         def last_after(rs, n):
-            by_four = rs[:, n, :].rearrange("p (t c i) -> p c t i", t=PACK, i=4)
+            by_four = rs[:, n, :].rearrange("p (t c i) -> p c t i", t=PACK, i=PAIR)
             cols = slice(n * P, (n + 1) * P)
             if n == 0:
                 c_banks[2] = bank(0, 0)
@@ -470,7 +479,7 @@ def tile_list_cauchy_voxel_pooling_kernel(
                 f_banks[2] = bank(0, 1)
                 quarter_passes(f_banks, 2, range(last))
                 by_slot = rs[:, 0:2, :].rearrange("p e (s j) -> p (e s) j", s=2)
-                square_and_sign(last, 0, by_slot.rearrange("p t (c i) -> p c t i", i=4))
+                square_and_sign(last, 0, by_slot.rearrange("p t (c i) -> p c t i", i=PAIR))
             elif n == 2:
                 hp2 = keep.tile([P, PACK, P], BF16, name="hp2")
                 for t in range(PACK):
@@ -492,10 +501,14 @@ def tile_list_cauchy_voxel_pooling_kernel(
                 finish_half(0)
             else:
                 size = keep.tile([P, P, PACK], BF16, name="size_last")
-                nc.scalar.activation(size[:].rearrange("p (c i) t -> p c t i", i=4), by_four, ACT.Square)
+                nc.scalar.activation(size[:].rearrange("p (c i) t -> p c t i", i=PAIR), by_four, ACT.Square)
                 hb = keep.tile([P, P, PACK], BF16, name="hb_last", align_bytes=64)
-                nc.vector.tensor_tensor(hb[:], size[:], d_sign[last][:, 0:P, :], ALU.mult)
-                quantize(h_codes[last][:, cols], h_sc[last][:, cols], hb[:])
+                parts = [slice(0, P // 2), slice(P // 2, P)]
+                for part in parts:
+                    nc.vector.tensor_tensor(hb[:, part, :], size[:, part, :], d_sign[last][:, part, :], ALU.mult)
+                for part in parts:
+                    done = slice(cols.start + part.start, cols.start + part.stop)
+                    quantize(h_codes[last][:, done], h_sc[last][:, done], hb[:, part, :])
                 for banks in (c_banks, f_banks):
                     quarter_passes(banks, 3, [last])
 

@@ -26,13 +26,14 @@ ROWS = 4
 SC_BASE = 96
 PLANE = (8, 4)
 EARLY_CARRIES = 4
-MID_COLS = 128
+MID_COLS = 96
 SQ_BUFS = 3
 TINY = 2.0**-100
 HALF = S2 // 2
 PAIR = 2
 FIRST_PIECES = ((0, 192), (192, 384), (384, N))
 LIST_COLS = PASS // 16
+LATE_AT = 32768
 
 
 def tile_list_cauchy_voxel_pooling_kernel(
@@ -211,7 +212,7 @@ def tile_list_cauchy_voxel_pooling_kernel(
             return slice(u * HALF, (u + 1) * HALF)
 
         def round_wf(g, lo, hi):
-            wf_b = work.tile([P, hi - lo, PACK], BF16, name=f"wf_b{g}_{lo}", tag="wf_v", bufs=4, align_bytes=64)
+            wf_b = work.tile([P, hi - lo, PACK], BF16, name=f"wf_b{g}_{lo}", tag="wf_v", bufs=3, align_bytes=64)
             woven = wf_b[:].rearrange("p (c i) t -> p c t i", i=PAIR)
             nc.vector.tensor_copy(woven, wf_raw[g, 0][:, :, lo:hi].rearrange("p t (c i) -> p c t i", i=PAIR))
             return wf_b
@@ -225,7 +226,7 @@ def tile_list_cauchy_voxel_pooling_kernel(
                     nc.gpsimd.tensor_scalar(woven, rows_in, 1.0, 0.0, ALU.mult, ALU.add)
                 else:
                     nc.vector.tensor_copy(woven, rows_in)
-            return [wf_b[:, 0 : N // 2, :], wf_b[:, N // 2 : N, :]]
+            return wf_b
 
         def quantize(codes, scales, src):
             nc.vector.quantize_mx(out=codes.bitcast(FP8X4), scales=scales, in_=src.rearrange("p c t -> p (c t)"))
@@ -297,27 +298,16 @@ def tile_list_cauchy_voxel_pooling_kernel(
                 by_slot = rs[:, 0:2, :].rearrange("p e (s j) -> p (e s) j", s=2)
                 for t in range(PACK):
                     weigh(hp0[:, 0, t, n * P : (n + 1) * P], by_slot[:, t, n * P : (n + 1) * P], 0, t)
-            elif n == 2:
-                weigh_pair(hp0, rs, 0, n)
             else:
-                for q in range(2):
-                    for s in range(2):
-                        weigh(hp0[:, 1, 2 + s, q * P : (q + 1) * P], rs[:, n, s * HALF + q * P : s * HALF + (q + 1) * P], 0, 2 + s)
+                weigh_pair(hp0, rs, 0, n)
 
         roots(x0, first_root, first_after, (2,))
-        for u in range(2):
-            quantize_wf(0, u * N // 2, (u + 1) * N // 2, w0[u])
-        for u in range(2):
-            hb0 = work.tile([P, HALF, PACK], BF16, name=f"hb{u}", align_bytes=64)
-            for q in range(2):
-                nc.vector.tensor_copy(
-                    hb0[:, q * P : (q + 1) * P, :].rearrange("p (c i) t -> p c t i", i=4),
-                    hp0[:, u, :, q * P : (q + 1) * P].rearrange("p t (c i) -> p c t i", i=4),
-                )
-            for q in range(2):
-                cols = slice(u * HALF + q * P, u * HALF + (q + 1) * P)
-                quantize(h_codes[0][:, cols], h_sc[0][:, cols], hb0[:, q * P : (q + 1) * P, :])
-        w1 = [round_wf(1, lo, lo + N // 2) for lo in (0, N // 2)]
+        hb0 = [interleave(hp0, 0)]
+        quantize_wf(0, 0, N, w0)
+        hb0.append(interleave(hp0, 1))
+        quantize_h(0, 0, hb0[0][:])
+        w1 = round_wf(1, 0, N)
+        quantize_h(0, 1, hb0[1][:])
         x2 = x_last()
         wc_sc = sc_mm[1][:, 0 : I_PASSES * N].rearrange("p (g n) -> p g n", g=I_PASSES)
         for r in range(ROWS):
@@ -356,9 +346,7 @@ def tile_list_cauchy_voxel_pooling_kernel(
             rs1[:, :, mid:S2].rearrange("p t (c i) -> p c t i", i=PAIR),
             ACT.Square,
         )
-        for u in range(2):
-            quantize_wf(1, u * N // 2, (u + 1) * N // 2, w1[u])
-        w2 = [round_wf(last, lo, lo + N // 2) for lo in (0, N // 2)]
+        quantize_wf(1, 0, N, w1)
         hb1 = work.tile([P, S2, PACK], BF16, name="hb_mid", bufs=1, align_bytes=64)
         for lo, hi in ((0, HALF), (HALF, mid)):
             nc.vector.tensor_copy(
@@ -368,8 +356,7 @@ def tile_list_cauchy_voxel_pooling_kernel(
         nc.vector.tensor_tensor(hb1[:, mid:S2, :], size1[:], d_sign[1][:], ALU.mult)
         quantize_h(1, 0, hb1[:, 0:HALF, :])
         quantize_h(1, 1, hb1[:, HALF:S2, :])
-        for u in range(2):
-            quantize_wf(last, u * N // 2, (u + 1) * N // 2, w2[u])
+        w2 = [round_wf(last, lo, lo + N // 2) for lo in (0, N // 2)]
 
         c_banks, f_banks = {}, {}
 
@@ -402,8 +389,7 @@ def tile_list_cauchy_voxel_pooling_kernel(
         def early_passes(passes, banks, u, first_bank):
             for k in range(2):
                 banks[u, k] = bank(1 - u, first_bank + k)
-                for g in range(I_PASSES - 1):
-                    passes(g, u, k)
+                passes(0, u, k)
 
         def quarter_passes(banks, q, groups):
             cols = slice(q * P, (q + 1) * P)
@@ -431,10 +417,16 @@ def tile_list_cauchy_voxel_pooling_kernel(
 
         def finish_half(k):
             c_sb = keep.tile([P, S2], F32, name=f"c_sb{k}")
-            res = keep.tile([P, 2, HALF], F32, name=f"res{k}")
-            nc.scalar.copy(c_sb[:], c_banks[0, k][:])
-            nc.vector.tensor_tensor(res[:].rearrange("p e j -> p (e j)"), f_banks[0, k][:], c_sb[:], ALU.max)
-            store(0, k, res)
+            res = reuse.tile([P, 2, HALF], F32, name=f"res{k}", offset=LATE_AT + k * 4 * S2)
+            if k == 0:
+                for e in range(2):
+                    nc.scalar.copy(c_sb[:, half_cols(e)], c_banks[0, k][:, half_cols(e)])
+                    nc.vector.tensor_tensor(res[:, e, :], f_banks[0, k][:, half_cols(e)], c_sb[:, half_cols(e)], ALU.max)
+                    nc.sync.dma_start(out[P * e : P * (e + 1), half_cols(0)], res[:, e, :])
+            else:
+                nc.scalar.copy(c_sb[:], c_banks[0, k][:])
+                nc.vector.tensor_tensor(res[:].rearrange("p e j -> p (e j)"), f_banks[0, k][:], c_sb[:], ALU.max)
+                store(0, k, res)
 
         res_late = [keep.tile([P, 2, HALF], F32, name=f"res_late{k}") for k in range(2)]
 
@@ -450,18 +442,13 @@ def tile_list_cauchy_voxel_pooling_kernel(
                     c_sb[:, tiles, :],
                     ALU.max,
                 )
-                if q == 3 and k == 0 and e == 1:
-                    store(1, 0, res_late[0])
-                elif q == 3 and k == 1:
-                    nc.sync.dma_start(out[P * b : P * (b + 1), half_cols(1)], res_late[k][:, e, :])
+                if q == 3:
+                    store(1, k, res_late[k])
 
         early_passes(c_passes, c_banks, 0, 0)
         early_passes(f_passes, f_banks, 0, 2)
 
         def last_root(rs, sq, n):
-            if n == 2:
-                plain_root(rs, sq, n)
-                return
             width = HALF if n < 2 else P
             for s in range(S2 // width):
                 t = 2 * n + s if n < 2 else s
@@ -474,45 +461,52 @@ def tile_list_cauchy_voxel_pooling_kernel(
             cols = slice(n * P, (n + 1) * P)
             if n == 0:
                 c_banks[2] = bank(0, 0)
-                quarter_passes(c_banks, 2, range(last))
+                quarter_passes(c_banks, 2, [0])
             elif n == 1:
                 f_banks[2] = bank(0, 1)
-                quarter_passes(f_banks, 2, range(last))
+                quarter_passes(f_banks, 2, [0])
+                for passes in (f_passes, c_passes):
+                    for k in range(2):
+                        passes(1, 0, k)
+                c_banks[3] = bank(0, 2)
+                quarter_passes(c_banks, 3, range(last))
+                for banks in (c_banks, f_banks):
+                    quarter_passes(banks, 2, [1])
                 by_slot = rs[:, 0:2, :].rearrange("p e (s j) -> p (e s) j", s=2)
                 square_and_sign(last, 0, by_slot.rearrange("p t (c i) -> p c t i", i=PAIR))
+                for u in range(2):
+                    quantize_wf(last, u * N // 2, (u + 1) * N // 2, w2[u])
             elif n == 2:
-                hp2 = keep.tile([P, PACK, P], BF16, name="hp2")
-                for t in range(PACK):
-                    weigh(hp2[:, t, :], rs[:, n, t * P : (t + 1) * P], last, t)
-                for k in range(2):
-                    c_passes(last, 0, k)
-                    f_passes(last, 0, k)
-                hb = keep.tile([P, P, PACK], BF16, name="hb_third", align_bytes=64)
-                nc.vector.tensor_copy(
-                    hb[:].rearrange("p (c i) t -> p c t i", i=4), hp2[:].rearrange("p t (c i) -> p c t i", i=4)
-                )
-                quantize(h_codes[last][:, cols], h_sc[last][:, cols], hb[:])
-                c_banks[3] = bank(0, 2)
                 f_banks[3] = bank(0, 3)
-                for banks in (c_banks, f_banks):
-                    quarter_passes(banks, 3, range(last))
+                quarter_passes(f_banks, 3, range(last))
+                size = keep.tile([P, P, PACK], BF16, name="size_third")
+                nc.scalar.activation(size[:].rearrange("p (c i) t -> p c t i", i=PAIR), by_four, ACT.Square)
+                for passes in (c_passes, f_passes):
+                    for k in range(2):
+                        passes(last, 0, k)
+                hb = keep.tile([P, P, PACK], BF16, name="hb_third", align_bytes=64)
+                nc.vector.tensor_tensor(hb[:], size[:], d_sign[last][:, 0:P, :], ALU.mult)
+                quantize(h_codes[last][:, cols], h_sc[last][:, cols], hb[:])
                 for banks in (c_banks, f_banks):
                     quarter_passes(banks, 2, [last])
-                finish_half(0)
             else:
                 size = keep.tile([P, P, PACK], BF16, name="size_last")
                 nc.scalar.activation(size[:].rearrange("p (c i) t -> p c t i", i=PAIR), by_four, ACT.Square)
-                hb = keep.tile([P, P, PACK], BF16, name="hb_last", align_bytes=64)
+                hb = [
+                    reuse.tile([P, P // 2, PACK], BF16, name="hb_last0", offset=LATE_AT + 2 * S2 - 256, align_bytes=64),
+                    keep.tile([P, P // 2, PACK], BF16, name="hb_last1", align_bytes=64),
+                ]
                 parts = [slice(0, P // 2), slice(P // 2, P)]
-                for part in parts:
-                    nc.vector.tensor_tensor(hb[:, part, :], size[:, part, :], d_sign[last][:, part, :], ALU.mult)
-                for part in parts:
+                for w, part in enumerate(parts):
+                    nc.vector.tensor_tensor(hb[w][:], size[:, part, :], d_sign[last][:, part, :], ALU.mult)
+                for w, part in enumerate(parts):
                     done = slice(cols.start + part.start, cols.start + part.stop)
-                    quantize(h_codes[last][:, done], h_sc[last][:, done], hb[:, part, :])
+                    quantize(h_codes[last][:, done], h_sc[last][:, done], hb[w][:])
                 for banks in (c_banks, f_banks):
                     quarter_passes(banks, 3, [last])
 
         roots(x2, last_root, last_after)
+        finish_half(0)
         finish_half(1)
         finish_quarter(2, 2)
-        finish_quarter(3, 1)
+        finish_quarter(3, 2)

from contextlib import ExitStack

import concourse.mybir as mybir

K, T, S, T2, S2, N = 1024, 4096, 1536, 2048, 512, 512
FLOPS = 2 * K * S * S2 + 2 * 2 * S * N * S2

F32 = mybir.dt.float32
BF16 = mybir.dt.bfloat16
I32 = mybir.dt.int32
U32 = mybir.dt.uint32
U16 = mybir.dt.uint16
U8 = mybir.dt.uint8
FP8X4 = mybir.dt.float8_e4m3fn_x4
FP4X4 = mybir.dt.float4_e2m1fn_x4
ACT = mybir.ActivationFunctionType
ALU = mybir.AluOpType

P = 128
PACK = 4
PASS = P * PACK
K_PASSES = K // PASS
I_PASSES = S // PASS
N_TILES = N // P
ROWS = 4
SC_BASE = 96
PLANE = (8, 4)
EARLY_CARRIES = 4
MID_COLS = 96
SQ_BUFS = 3
TINY = 2.0**-100
HALF = S2 // 2
PAIR = 2
FIRST_PIECES = ((0, 192), (192, 384), (384, N))
LIST_COLS = PASS // 16
LATE_AT = 32768


def tile_list_cauchy_voxel_pooling_kernel(
    tc, tab_words, tab_scales, offs, tab2_words, tab2_scales, offs2, dens, wf, wc_words, wc_scales, out
):
    nc = tc.nc
    with ExitStack() as ctx:
        keep = ctx.enter_context(tc.tile_pool(name="keep", bufs=1))
        work = ctx.enter_context(tc.tile_pool(name="work", bufs=2))
        reuse = ctx.enter_context(tc.tile_pool(name="reuse", bufs=1))
        psum = ctx.enter_context(tc.psum_pool(name="psum", bufs=1))

        idx = keep.tile([P, S // 16], U16, name="idx")
        idx2 = keep.tile([P, S2 // 16], U16, name="idx2")
        v_win = [reuse.tile([P, T], U32, name="v_win0", offset=0), keep.tile([P, T], U32, name="v_win1")]
        v2_win = [keep.tile([P, T2], U32, name=f"v2_win{a}", tag="v2_win", align_bytes=64) for a in range(1)]
        vs_win = keep.tile([P, T], U8, name="vs_win")
        v2s_win = keep.tile([P, T2], U8, name="v2s_win")
        sc_mm = [keep.tile([P, S + S2], U8, name=f"sc_mm{a}", align_bytes=64) for a in range(K_PASSES)]

        for win in (vs_win, v2s_win):
            nc.vector.memset(win[0:SC_BASE, :].bitcast(I32), 0)
        for a in range(K_PASSES):
            nc.gpsimd.memset(sc_mm[a][:].bitcast(I32), 0)


        def load_words(win, words):
            nc.sync.dma_start(win[:].bitcast(I32), words.rearrange("p t i -> p (t i)").bitcast(I32))

        def load_scales(win, scales):
            nc.sync.dma_start(win[SC_BASE:P, :].bitcast(I32), scales.rearrange("a q t -> (a q) t").bitcast(I32))

        nc.sync.dma_start(idx[:], offs)
        load_scales(vs_win, tab_scales)
        nc.sync.dma_start(idx2[:], offs2)
        load_scales(v2s_win, tab2_scales)
        load_words(v2_win[0], tab2_words[0])
        load_words(v_win[0], tab_words[0])
        load_words(v_win[1], tab_words[1])

        last = I_PASSES - 1
        v_sc_list = keep.tile([P, S], U8, name="v_sc_list", tag="v_first", align_bytes=64)
        v2_sc_list = keep.tile([P, S2], U8, name="v2_sc_list", tag="v2_first", align_bytes=64)
        sc_all = keep.tile([P, S + S2], U8, name="sc_all", align_bytes=64)
        nc.vector.tensor_copy(v_sc_list[:], vs_win[:].indirect(idx[:]))
        nc.vector.tensor_copy(v2_sc_list[:], v2s_win[:].indirect(idx2[:]))
        nc.vector.tensor_copy(
            sc_all[:, 0:S].rearrange("p (g t m) -> p t g m", g=I_PASSES, t=PACK),
            v_sc_list[:].rearrange("p (g m t) -> p t g m", g=I_PASSES, t=PACK),
        )
        nc.vector.tensor_copy(sc_all[:, S : S + S2].bitcast(I32), v2_sc_list[:].bitcast(I32))
        planes = [sc_mm[a][PLANE[a] :, :] for a in range(K_PASSES)]

        def carry(queue, a, r):
            queue.dma_start(
                sc_mm[a][PLANE[a] + r : P : 32, :].bitcast(I32),
                sc_all[SC_BASE + 16 * a + r : SC_BASE + 16 * (a + 1) : ROWS, :].bitcast(I32),
            )

        rows = [(a, r) for a in range(K_PASSES) for r in range(ROWS)]
        for a, r in rows[:EARLY_CARRIES]:
            carry(nc.scalar, a, r)

        d_sb = keep.tile([P, I_PASSES, PACK], F32, name="d_sb", tag="v2_first", align_bytes=64)
        nc.scalar.dma_start(d_sb[:], dens.rearrange("(g p t) -> p g t", p=P, t=PACK))
        d_root = keep.tile([P, I_PASSES, PACK], F32, name="d_root")
        d_inv = keep.tile([P, I_PASSES, PACK], F32, name="d_inv")
        sign = keep.tile([P, I_PASSES, PACK], F32, name="sign")
        d_sign = {1: keep.tile([P, MID_COLS, PACK], BF16, name="d_sign1"), last: keep.tile([P, HALF, PACK], BF16, name="d_sign2")}
        nc.scalar.activation(d_root[:], d_sb[:], ACT.Abs_reciprocal_sqrt, bias=TINY)
        nc.scalar.activation(d_inv[:], d_root[:], ACT.Square)
        for g, cols in ((1, MID_COLS), (last, HALF)):
            for t in range(PACK):
                nc.scalar.activation(
                    sign[:, g, t : t + 1], d_sb[:, g, t : t + 1], ACT.Copy, scale=d_inv[:, g, t : t + 1]
                )
            nc.scalar.copy(d_sign[g][:], sign[:, g, :].unsqueeze(1).to_broadcast([P, cols, PACK]))

        v_codes = {}

        def gather_v_words(a, lo, hi, codes):
            for g in range(lo, hi):
                v_codes[a, g] = codes[:, g - lo]
            nc.vector.tensor_copy(
                codes[:].rearrange("p g t m -> p g m t"),
                v_win[a][:].indirect(idx[:, lo * LIST_COLS : hi * LIST_COLS]),
            )

        v2_codes = [
            keep.tile([P, S2], U32, name="v2_codes0", tag="v_first", align_bytes=64),
            keep.tile([P, S2], U32, name="v2_codes1", align_bytes=64),
        ]
        nc.vector.tensor_copy(v2_codes[0][:], v2_win[0][:].indirect(idx2[:]))
        v2_win.append(keep.tile([P, T2], U32, name="v2_win1", tag="v2_win", align_bytes=64))
        load_words(v2_win[1], tab2_words[1])
        for a, r in rows[EARLY_CARRIES:]:
            carry(nc.sync, a, r)
        gather_v_words(0, 0, I_PASSES, keep.tile([P, I_PASSES, PACK, P], U32, name="v_codes0", align_bytes=64))
        wf_rows = reuse.tile([P, I_PASSES * PACK * N], F32, name="wf_rows", offset=I_PASSES * 3 * N)
        wf_pieces = [(0, lo, hi) for lo, hi in FIRST_PIECES] + [(1, 0, N), (2, 0, N)]
        wf_raw = {}
        for g, lo, hi in wf_pieces:
            first = PACK * (g * N + lo)
            wf_raw[g, lo] = wf_rows[:, first : first + PACK * (hi - lo)].rearrange("p (t n) -> p t n", t=PACK)
            nc.sync.dma_start(
                wf_raw[g, lo], wf[g * PASS : (g + 1) * PASS, lo:hi].rearrange("(p t) n -> p t n", t=PACK)
            )
        wc_codes = reuse.tile([P, I_PASSES, 2 * N], U8, name="wc_codes", offset=0, align_bytes=64)
        nc.sync.dma_start(wc_codes[:].bitcast(I32), wc_words.rearrange("g p b -> p g b").bitcast(I32))
        gather_v_words(1, 0, last, keep.tile([P, last, PACK, P], U32, name="v_codes1", align_bytes=64))
        for lo, hi in ((0, P), (P, HALF), (HALF, S2)):
            nc.vector.tensor_copy(v2_codes[1][:, lo:hi], v2_win[1][:].indirect(idx2[:, lo // 16 : hi // 16]))

        gather_v_words(1, last, I_PASSES, keep.tile([P, 1, PACK, P], U32, name="v_last", tag="v2_win", align_bytes=64))

        h_codes = [keep.tile([P, S2], U32, name=f"h_codes{g}", align_bytes=64) for g in range(I_PASSES)]
        h_sc = [keep.tile([P, S2], U8, name=f"h_sc{g}", align_bytes=64) for g in range(I_PASSES)]
        wf_codes = [keep.tile([P, N], U32, name=f"wf_codes{g}", align_bytes=64) for g in range(I_PASSES)]
        wf_sc = [keep.tile([P, N], U8, name=f"wf_sc{g}", align_bytes=64) for g in range(I_PASSES)]

        def bank(half, b):
            return psum.tile([P, 512], F32, name=f"bank{half}{b}", tag=f"bank{half}{b}")

        def x_pass(out_ap, g, t, a, cols, start, stop):
            nc.tensor.matmul_mx(
                out=out_ap,
                lhsT=v_codes[a, g][:, t, :].bitcast(FP8X4),
                lhsT_scale=planes[a][:, (g * PACK + t) * P : (g * PACK + t + 1) * P],
                rhs=v2_codes[a][:, cols].bitcast(FP8X4),
                rhs_scale=planes[a][:, S + cols.start : S + cols.stop],
                start=start,
                stop=stop,
            )

        def x_products(g):
            banks = [bank(g % 2, t) for t in range(PACK)]
            for t in range(PACK):
                for a in reversed(range(K_PASSES)):
                    x_pass(banks[t][:], g, t, a, slice(0, S2), a == 1, a == 0)
            return banks

        def x_first():
            banks = [bank(0, n) for n in range(PACK)]
            for a in range(K_PASSES):
                for q in range(2):
                    for t in range(PACK):
                        x_pass(
                            banks[q][:, t * P : (t + 1) * P],
                            0,
                            t,
                            a,
                            slice(q * P, (q + 1) * P),
                            (a, t) == (0, 0),
                            (a, t) == (1, PACK - 1),
                        )
                for e in range(2):
                    for s in range(2):
                        x_pass(
                            banks[2 + e][:, half_cols(s)], 0, 2 * e + s, a, half_cols(1), (a, s) == (0, 0), (a, s) == (1, 1)
                        )
            return banks

        def x_last():
            banks = [bank(0, n) for n in range(PACK)]
            for e in range(2):
                for s in range(2):
                    for a in range(K_PASSES):
                        x_pass(banks[e][:, half_cols(s)], last, 2 * e + s, a, half_cols(0), a == 0, a == 1)
            for q in range(2, 4):
                for t in range(PACK):
                    for a in range(K_PASSES):
                        x_pass(banks[q][:, t * P : (t + 1) * P], last, t, a, slice(q * P, (q + 1) * P), a == 0, a == 1)
            return banks

        def half_cols(u):
            return slice(u * HALF, (u + 1) * HALF)

        def round_wf(g, lo, hi):
            wf_b = work.tile([P, hi - lo, PACK], BF16, name=f"wf_b{g}_{lo}", tag="wf_v", bufs=3, align_bytes=64)
            woven = wf_b[:].rearrange("p (c i) t -> p c t i", i=PAIR)
            nc.vector.tensor_copy(woven, wf_raw[g, 0][:, :, lo:hi].rearrange("p t (c i) -> p c t i", i=PAIR))
            return wf_b

        def round_first_wf():
            wf_b = keep.tile([P, N, PACK], BF16, name="wf_b0", align_bytes=64)
            for lo, hi in FIRST_PIECES:
                woven = wf_b[:, lo:hi, :].rearrange("p (c i) t -> p c t i", i=PAIR)
                rows_in = wf_raw[0, lo].rearrange("p t (c i) -> p c t i", i=PAIR)
                if hi < N:
                    nc.gpsimd.tensor_scalar(woven, rows_in, 1.0, 0.0, ALU.mult, ALU.add)
                else:
                    nc.vector.tensor_copy(woven, rows_in)
            return wf_b

        def quantize(codes, scales, src):
            nc.vector.quantize_mx(out=codes.bitcast(FP8X4), scales=scales, in_=src.rearrange("p c t -> p (c t)"))

        def quantize_wf(g, lo, hi, wf_b):
            quantize(wf_codes[g][:, lo:hi], wf_sc[g][:, lo:hi], wf_b[:])

        def roots(banks, root_of, after, on_vector=()):
            rs = work.tile([P, PACK, S2], F32, name="rs")
            sq = []
            for step in range(PACK + 1):
                if step < PACK:
                    sq.append(work.tile([P, S2], F32, name="sq", tag="sq", bufs=SQ_BUFS, align_bytes=64))
                    if step in on_vector:
                        twice = banks[step][:].unsqueeze(2).to_broadcast([P, S2, 2])
                        nc.vector.tensor_reduce(sq[step][:], twice, mybir.AxisListType.X, ALU.mult)
                    else:
                        nc.scalar.activation(sq[step][:], banks[step][:], ACT.Square)
                if step > 0:
                    root_of(rs, sq[step - 1], step - 1)
                    after(rs, step - 1)
            return rs

        def plain_root(rs, sq, n):
            nc.scalar.activation(rs[:, n, :], sq[:], ACT.Abs_reciprocal_sqrt, bias=1.0)

        def weigh(out_ap, r, g, t):
            nc.vector.scalar_tensor_tensor(out_ap, r, d_sb[:, g, t : t + 1], r, ALU.mult, ALU.mult)

        def weigh_pair(hp, rs, g, n):
            u, e = divmod(n, 2)
            for s in range(2):
                weigh(hp[:, u, 2 * e + s, :], rs[:, n, half_cols(s)], g, 2 * e + s)

        def interleave(hp, u):
            hb = work.tile([P, HALF, PACK], BF16, name=f"hb{u}", align_bytes=64)
            nc.vector.tensor_copy(
                hb[:].rearrange("p (c i) t -> p c t i", i=4), hp[:, u].rearrange("p t (c i) -> p c t i", i=4)
            )
            return hb

        def quantize_h(g, u, hb):
            quantize(h_codes[g][:, half_cols(u)], h_sc[g][:, half_cols(u)], hb)

        def finish_h(g, hp):
            hb = [interleave(hp, u) for u in range(2)]
            for u in range(2):
                quantize_h(g, u, hb[u][:])

        x0 = x_first()
        x1 = x_products(1)
        w0 = round_first_wf()
        hp0 = work.tile([P, 2, PACK, HALF], BF16, name="hp")

        def first_root(rs, sq, n):
            if n < 2:
                by_slot = rs[:, 0:2, :].rearrange("p e (s j) -> p (e s) j", s=2)
                nc.scalar.activation(
                    by_slot[:, :, n * P : (n + 1) * P],
                    sq[:].rearrange("p (t j) -> p t j", t=PACK),
                    ACT.Abs_reciprocal_sqrt,
                    bias=1.0,
                )
            else:
                plain_root(rs, sq, n)

        def first_after(rs, n):
            if n < 2:
                by_slot = rs[:, 0:2, :].rearrange("p e (s j) -> p (e s) j", s=2)
                for t in range(PACK):
                    weigh(hp0[:, 0, t, n * P : (n + 1) * P], by_slot[:, t, n * P : (n + 1) * P], 0, t)
            else:
                weigh_pair(hp0, rs, 0, n)

        roots(x0, first_root, first_after, (2,))
        hb0 = [interleave(hp0, 0)]
        quantize_wf(0, 0, N, w0)
        hb0.append(interleave(hp0, 1))
        quantize_h(0, 0, hb0[0][:])
        w1 = round_wf(1, 0, N)
        quantize_h(0, 1, hb0[1][:])
        x2 = x_last()
        wc_sc = sc_mm[1][:, 0 : I_PASSES * N].rearrange("p (g n) -> p g n", g=I_PASSES)
        for r in range(ROWS):
            nc.sync.dma_start(
                wc_sc[r:P:32, :, :].bitcast(I32),
                wc_scales.rearrange("g (q r) n -> r q g n", r=ROWS)[r].bitcast(I32),
            )

        def square_and_sign(g, u, r_by_slot):
            size = work.tile([P, HALF, PACK], BF16, name="size")
            nc.scalar.activation(size[:].rearrange("p (c i) t -> p c t i", i=PAIR), r_by_slot, ACT.Square)
            hb = work.tile([P, HALF, PACK], BF16, name=f"hb{u}", align_bytes=64)
            for q in range(2):
                part = slice(q * P, (q + 1) * P)
                nc.vector.tensor_tensor(hb[:, part, :], size[:, part, :], d_sign[last][:, part, :], ALU.mult)
            for q in range(2):
                cols = slice(u * HALF + q * P, u * HALF + (q + 1) * P)
                quantize(h_codes[g][:, cols], h_sc[g][:, cols], hb[:, q * P : (q + 1) * P, :])

        def mid_root(rs, sq, t):
            inv = d_inv[:, 1, t : t + 1]
            nc.scalar.activation(rs[:, t, :], sq[:], ACT.Abs_reciprocal_sqrt, bias=inv, scale=inv)

        mid = S2 - MID_COLS
        hp1 = work.tile([P, PACK, mid], BF16, name="hp1", bufs=1)

        def mid_after(rs, t):
            for lo, hi in ((0, mid),) if t < PACK - 1 else ((0, HALF), (HALF, mid)):
                r = rs[:, t, lo:hi]
                nc.vector.scalar_tensor_tensor(hp1[:, t, lo:hi], r, sign[:, 1, t : t + 1], r, ALU.mult, ALU.mult)

        rs1 = roots(x1, mid_root, mid_after)
        size1 = work.tile([P, MID_COLS, PACK], BF16, name="size1", bufs=1)
        nc.scalar.activation(
            size1[:].rearrange("p (c i) t -> p c t i", i=PAIR),
            rs1[:, :, mid:S2].rearrange("p t (c i) -> p c t i", i=PAIR),
            ACT.Square,
        )
        quantize_wf(1, 0, N, w1)
        hb1 = work.tile([P, S2, PACK], BF16, name="hb_mid", bufs=1, align_bytes=64)
        for lo, hi in ((0, HALF), (HALF, mid)):
            nc.vector.tensor_copy(
                hb1[:, lo:hi, :].rearrange("p (c i) t -> p c t i", i=4),
                hp1[:, :, lo:hi].rearrange("p t (c i) -> p c t i", i=4),
            )
        nc.vector.tensor_tensor(hb1[:, mid:S2, :], size1[:], d_sign[1][:], ALU.mult)
        quantize_h(1, 0, hb1[:, 0:HALF, :])
        quantize_h(1, 1, hb1[:, HALF:S2, :])
        w2 = [round_wf(last, lo, lo + N // 2) for lo in (0, N // 2)]

        c_banks, f_banks = {}, {}

        def c_passes(g, u, k):
            for e in range(2):
                b = 2 * k + e
                nc.tensor.matmul_mx(
                    out=c_banks[u, k][:, e * HALF : (e + 1) * HALF],
                    lhsT=wc_codes[:, g, 2 * P * b : 2 * P * (b + 1)].bitcast(FP4X4),
                    lhsT_scale=wc_sc[:, g, P * b : P * (b + 1)],
                    rhs=h_codes[g][:, half_cols(u)].bitcast(FP8X4),
                    rhs_scale=h_sc[g][:, half_cols(u)],
                    start=(g == 0 and e == 0),
                    stop=(g == I_PASSES - 1 and e == 1),
                )

        def f_passes(g, u, k):
            for e in range(2):
                b = 2 * k + e
                nc.tensor.matmul_mx(
                    out=f_banks[u, k][:, e * HALF : (e + 1) * HALF],
                    lhsT=wf_codes[g][:, P * b : P * (b + 1)].bitcast(FP8X4),
                    lhsT_scale=wf_sc[g][:, P * b : P * (b + 1)],
                    rhs=h_codes[g][:, half_cols(u)].bitcast(FP8X4),
                    rhs_scale=h_sc[g][:, half_cols(u)],
                    start=(g == 0 and e == 0),
                    stop=(g == I_PASSES - 1 and e == 1),
                )

        def early_passes(passes, banks, u, first_bank):
            for k in range(2):
                banks[u, k] = bank(1 - u, first_bank + k)
                passes(0, u, k)

        def quarter_passes(banks, q, groups):
            cols = slice(q * P, (q + 1) * P)
            for g in groups:
                for b in range(N_TILES):
                    if banks is c_banks:
                        lhsT = wc_codes[:, g, 2 * P * b : 2 * P * (b + 1)].bitcast(FP4X4)
                        lhsT_scale = wc_sc[:, g, P * b : P * (b + 1)]
                    else:
                        lhsT = wf_codes[g][:, P * b : P * (b + 1)].bitcast(FP8X4)
                        lhsT_scale = wf_sc[g][:, P * b : P * (b + 1)]
                    nc.tensor.matmul_mx(
                        out=banks[q][:, b * P : (b + 1) * P],
                        lhsT=lhsT,
                        lhsT_scale=lhsT_scale,
                        rhs=h_codes[g][:, cols].bitcast(FP8X4),
                        rhs_scale=h_sc[g][:, cols],
                        start=(g == 0 and b == 0),
                        stop=(g == last and b == N_TILES - 1),
                    )

        def store(u, k, res):
            dst = out[2 * P * k : 2 * P * (k + 1), half_cols(u)].rearrange("(e p) j -> p e j", p=P)
            nc.sync.dma_start(dst, res[:])

        def finish_half(k):
            c_sb = keep.tile([P, S2], F32, name=f"c_sb{k}")
            res = reuse.tile([P, 2, HALF], F32, name=f"res{k}", offset=LATE_AT + k * 4 * S2)
            if k == 0:
                for e in range(2):
                    nc.scalar.copy(c_sb[:, half_cols(e)], c_banks[0, k][:, half_cols(e)])
                    nc.vector.tensor_tensor(res[:, e, :], f_banks[0, k][:, half_cols(e)], c_sb[:, half_cols(e)], ALU.max)
                    nc.sync.dma_start(out[P * e : P * (e + 1), half_cols(0)], res[:, e, :])
            else:
                nc.scalar.copy(c_sb[:], c_banks[0, k][:])
                nc.vector.tensor_tensor(res[:].rearrange("p e j -> p (e j)"), f_banks[0, k][:], c_sb[:], ALU.max)
                store(0, k, res)

        res_late = [keep.tile([P, 2, HALF], F32, name=f"res_late{k}") for k in range(2)]

        def finish_quarter(q, width):
            c_sb = keep.tile([P, N_TILES, P], F32, name=f"c_quarter{q}")
            for b in range(0, N_TILES, width):
                tiles = slice(b, b + width)
                k, e = divmod(b, 2)
                nc.scalar.copy(c_sb[:, tiles, :], c_banks[q][:].rearrange("p (b j) -> p b j", j=P)[:, tiles, :])
                nc.vector.tensor_tensor(
                    res_late[k][:, e : e + width, (q - 2) * P : (q - 1) * P],
                    f_banks[q][:].rearrange("p (b j) -> p b j", j=P)[:, tiles, :],
                    c_sb[:, tiles, :],
                    ALU.max,
                )
                if q == 3:
                    store(1, k, res_late[k])

        early_passes(c_passes, c_banks, 0, 0)
        early_passes(f_passes, f_banks, 0, 2)

        def last_root(rs, sq, n):
            width = HALF if n < 2 else P
            for s in range(S2 // width):
                t = 2 * n + s if n < 2 else s
                inv = d_inv[:, last, t : t + 1]
                cols = slice(s * width, (s + 1) * width)
                nc.scalar.activation(rs[:, n, cols], sq[:, cols], ACT.Abs_reciprocal_sqrt, bias=inv, scale=inv)

        def last_after(rs, n):
            by_four = rs[:, n, :].rearrange("p (t c i) -> p c t i", t=PACK, i=PAIR)
            cols = slice(n * P, (n + 1) * P)
            if n == 0:
                c_banks[2] = bank(0, 0)
                quarter_passes(c_banks, 2, [0])
            elif n == 1:
                f_banks[2] = bank(0, 1)
                quarter_passes(f_banks, 2, [0])
                for passes in (f_passes, c_passes):
                    for k in range(2):
                        passes(1, 0, k)
                c_banks[3] = bank(0, 2)
                quarter_passes(c_banks, 3, range(last))
                for banks in (c_banks, f_banks):
                    quarter_passes(banks, 2, [1])
                by_slot = rs[:, 0:2, :].rearrange("p e (s j) -> p (e s) j", s=2)
                square_and_sign(last, 0, by_slot.rearrange("p t (c i) -> p c t i", i=PAIR))
                for u in range(2):
                    quantize_wf(last, u * N // 2, (u + 1) * N // 2, w2[u])
            elif n == 2:
                f_banks[3] = bank(0, 3)
                quarter_passes(f_banks, 3, range(last))
                size = keep.tile([P, P, PACK], BF16, name="size_third")
                nc.scalar.activation(size[:].rearrange("p (c i) t -> p c t i", i=PAIR), by_four, ACT.Square)
                for passes in (c_passes, f_passes):
                    for k in range(2):
                        passes(last, 0, k)
                hb = keep.tile([P, P, PACK], BF16, name="hb_third", align_bytes=64)
                nc.vector.tensor_tensor(hb[:], size[:], d_sign[last][:, 0:P, :], ALU.mult)
                quantize(h_codes[last][:, cols], h_sc[last][:, cols], hb[:])
                for banks in (c_banks, f_banks):
                    quarter_passes(banks, 2, [last])
            else:
                size = keep.tile([P, P, PACK], BF16, name="size_last")
                nc.scalar.activation(size[:].rearrange("p (c i) t -> p c t i", i=PAIR), by_four, ACT.Square)
                hb = [
                    reuse.tile([P, P // 2, PACK], BF16, name="hb_last0", offset=LATE_AT + 2 * S2 - 256, align_bytes=64),
                    keep.tile([P, P // 2, PACK], BF16, name="hb_last1", align_bytes=64),
                ]
                parts = [slice(0, P // 2), slice(P // 2, P)]
                for w, part in enumerate(parts):
                    nc.vector.tensor_tensor(hb[w][:], size[:, part, :], d_sign[last][:, part, :], ALU.mult)
                for w, part in enumerate(parts):
                    done = slice(cols.start + part.start, cols.start + part.stop)
                    quantize(h_codes[last][:, done], h_sc[last][:, done], hb[w][:])
                for banks in (c_banks, f_banks):
                    quarter_passes(banks, 3, [last])

        roots(x2, last_root, last_after)
        finish_half(0)
        finish_half(1)
        finish_quarter(2, 2)
        finish_quarter(3, 2)
